import numpy as np, ml_dtypes
CORES = [9,25,41,57]
N = 4
BF = ml_dtypes.bfloat16
A, W, HM, RO, MU = 512, 4096, 2, 5, 8
n = A // 4
def view(j, c):
    return np.where(c < 0, W, (((c * (MU * j + 5)) >> 5) + 37 * j) & (W - 1))
def worth(tab, j, b):
    x = tab[:, view(j[None, :], b)]
    return np.add.reduce(np.maximum.accumulate(x[:, ::-1], axis=1)[:, ::-1], axis=0)
def pack(x, b, p):
    return {"sight": x.reshape(N, 128, W).astype(np.float32).astype(BF), "bun": np.ascontiguousarray(b.reshape(N, 128, A)).astype(np.int32), "pots": p.astype(np.int32)}
def looks(rng):
    return (rng.integers(0, 256, (N, 8, 16, W)) * rng.integers(1, 9, (N, 8, 1, W))) >> 3
def some(rng, goods, shares):
    return np.where(rng.random((N, 8, 16, A)) < rng.choice(np.array(shares), (N, 8, 1, A)), goods, -1)
def setup_inputs(rng):
    b = some(rng, rng.integers(0, 4096, (N, 8, 16, A)), [0.05, 0.2, 0.4, 0.7, 1.0])
    p = np.where(rng.random((N, 8, n)) < 0.85, rng.integers(0, 4096, (N, 8, n)), -1)
    return pack(looks(rng), b, p)
def setup_inputs_spread(rng):
    x = np.floor(np.exp2(8 * rng.random((N, 8, 1, W)) * rng.random((N, 8, 16, W)) ** 0.5)).astype(np.int64) - 1
    x = np.where(rng.random((N, 8, 16, W)) < 0.02, 255, np.clip(x, 0, 255))
    e = rng.choice(np.array([0.5, 1.0, 3.0, 6.0]), (N, 8, 1, A))
    b = some(rng, np.minimum((4096 * rng.random((N, 8, 16, A)) ** e).astype(np.int64), 4095), [0.05, 0.15, 0.5, 0.95])
    p = np.minimum((4096 * rng.random((N, 8, n)) ** rng.choice(np.array([0.3, 1.0, 4.0]), (N, 8, 1))).astype(np.int64), 4095)
    return pack(x, b, np.where(rng.random((N, 8, n)) < 0.9, p, -1))
def setup_inputs_ends(rng):
    see = view(np.arange(A), np.int64(4095))
    x = 255 * (rng.random((N, 8, 16, W)) < rng.choice(np.array([0.05, 0.3, 0.6, 0.95]), (N, 8, 1, W))).astype(np.int64)
    x[:, :, 0, see[0::4]] = 255
    far = np.array([0, A - 67, A - 66, A - 65, A - 4, A - 3, A - 2, A - 1]); x[..., see[far]] = 255
    b = some(rng, np.int64(4095), [0.0, 0.1, 0.5, 1.0])
    own = (rng.random((N, 8, 1, A)) < 0.33) & (np.arange(A) % 4 != 0)
    b = np.where(own, rng.integers(0, 4096, (N, 8, 16, A)), b)
    b[:, :, 3, 0::4] = 4095; b[..., 0] = 4095; b[..., A - 67:A - 64] = -1; b[..., A - 4] = -1
    end = np.where(rng.random((N, 8, 1, 3)) < 0.5, 4095, -1); end[N - 1, 7] = np.array([-1, 4095, -1]); end[0, 7] = np.array([-1, -1, 4095]); end[1, 7] = np.array([4095, -1, -1])
    b[..., A - 3:] = end
    p = np.where(rng.random((N, 8, n)) < 0.7, np.where(rng.random((N, 8, n)) < 0.6, 4095, -1), rng.integers(0, 4096, (N, 8, n)))
    p[..., 0] = 4095; p[..., n - 1] = 4095
    return pack(x, b, p)
def setup_inputs_corners(rng):
    x = looks(rng); b = rng.integers(0, 4096, (N, 8, 16, A)); p = rng.integers(0, 4096, (N, 8, n)); d = np.arange(16)[:, None]
    for r in range(N):
        mode = rng.permutation(8)
        for g in range(8):
            m = int(mode[g])
            if m == 0: b[r, g] = -1
            if m == 2: b[r, g, :15] = -1
            if m == 3: b[r, g, 1:] = -1
            if m == 4:
                c = int(b[r, g, 0, 0]); b[r, g] = np.where(rng.random((16, A)) < rng.random((1, A)), c, -1); p[r, g] = c
            if m == 5: b[r, g] = np.where(rng.random((1, A)) < 0.5, b[r, g], -1)
            if m == 6:
                k = rng.choice(np.array([0, 1, 15, 16]), (1, A)); low = rng.random((1, A)) < 0.5
                b[r, g] = np.where(np.where(low, d < k, d >= 16 - k), b[r, g], -1); p[r, g] = -1
            if m == 7: x[r, g] = 0
    return pack(x, b, p)
def calls(rng):
    return np.argsort(rng.random((N, 3, n)), axis=-1) + n * rng.integers(0, W // n, (N, 3, n))
def setup_inputs_ties(rng):
    base = rng.choice(np.array([0, 1, 127, 254]), (N, 8, 1, 1)); base[0, 0] = 0; base[0, 7] = 254; base[N - 1, 7] = 254
    x = base + (rng.random((N, 8, 16, W)) < 0.125)
    few = rng.integers(0, 4096, 32); few[0] = 0; few[1] = 4095
    b = some(rng, few[rng.integers(0, 32, (N, 8, 16, A))], [0.0, 0.1, 0.3, 0.6])
    p = np.where(rng.random((N, 8, n)) < 0.9, few[rng.integers(0, 32, (N, 8, n))], -1)
    full = rng.integers(0, 4096, (N, 16, A)); b3 = np.where(rng.random((N, 1, A)) < 0.5, full, -1)
    b3[:, :, 0::4] = full[:, :, 0::4]
    b3[:, 0:3, 0::4] = calls(rng)
    x[:, 3] = 100; b[:, 3] = b3
    for m in range(3):
        bm = rng.integers(0, 4096, (N, 16, A)); bm[:, 0:3, 0::4] = calls(rng); bm[:, :, m + 1::4] = -1
        x[:, 4 + m] = 100; b[:, 4 + m] = bm
    return pack(x, b, p)
def check_inputs(d):
    bad = []
    for k, lo, hi in (("sight", 0, 255), ("bun", -1, 4095), ("pots", -1, 4095)):
        v = np.asarray(d[k]).astype(np.float64)
        if not np.all((v >= lo) & (v <= hi) & (v == np.floor(v))): bad.append("range of " + k)
    return bad
def reference(sight, bun, pots):
    tab = np.zeros((N, 8, 16, W + 1), np.int32); tab[..., :W] = sight.astype(np.float32).reshape(N, 8, 16, W).astype(np.int32)
    bn = bun.astype(np.int64).reshape(N, 8, 16, A); p = pots.astype(np.int64); val = np.zeros((N, 8, A), np.int64)
    for r in range(N):
        for g in range(8): val[r, g] = worth(tab[r, g], np.arange(A), bn[r, g])[0]
    place = np.arange(16)[:, None]
    for t in range(RO):
        u = 4 * np.arange(n) + (t & 3); nbn = bn.copy(); nval = val.copy(); npots = np.zeros((N, 8, n), np.int64)
        for r in range(N):
            for g in range(8):
                old = bn[r, g][:, u]; s = old.copy(); s[15] = p[r, g]
                best = np.zeros(n, np.int64); who = np.full(n, -1); riv = []
                for m in range(3):
                    q = r if m < HM else (r + 1 + (t + m - HM) % (N - 1)) % N
                    j = 4 * ((old[m] + val[r, g, u] + 13 * t) & (n - 1)) + ((t + 1 + m) & 3)
                    first = np.zeros(n, bool); first[np.unique(j, return_index=True)[1]] = True
                    sv = worth(tab[q, g], j, s)
                    e = np.where(first, np.add.reduce((sv > val[q, g, j]).astype(np.int64), axis=0), 0)
                    who = np.where(e > best, m, who); best = np.maximum(best, e); riv.append((q, j, sv))
                new = s.copy()
                for m in range(3):
                    q, j, sv = riv[m]; c = np.flatnonzero(who == m); jc = j[c]
                    nbn[q, g][:, jc] = np.where(place >= best[c] - 1, s[:, c], -1); nval[q, g, jc] = sv[best[c] - 1, c]
                    new[:, c] = bn[q, g][:, jc]
                nbn[r, g][:, u] = new; nval[r, g, u] = worth(tab[r, g], u, new)[0]
                npots[(r + 1) % N, g] = np.where(best >= 2, s[np.maximum(best - 2, 0), np.arange(n)], old[15])
        bn, val, p = nbn, nval, npots
    return {"yb": bn.reshape(N, 128, A).astype(np.float32), "yv": val.astype(np.float32), "yp": p.astype(np.float32)}

@@ -1,0 +1,699 @@
+import math
+from concourse.bass import DstId, RemoteDMATransfer
+from concourse.mybir import AluOpType as OP, ActivationFunctionType as AF
+
+F, H, I, U = "float32", "bfloat16", "int32", "uint16"
+RO = 5
+CYC, PEC, WAKE, ISSUE, LAT, GAT, SCA, SLACK, VLATE = 0.001, 0.0008, 0.08, 1.2, 2.0, 1.6, 4.0, 0.1, 0.3
+CHS = {"S": 4, "0": 4, "1": 4, "2": 4}
+
+SCRATCH = {}
+
+
+def _sb(name, w, d):
+    SCRATCH[name] = ("sbuf", [128, w], d)
+
+
+_sb("TAB", 4112, H)
+_sb("RAWB", 512, I)
+_sb("POTI", 128, I)
+_sb("BF", 512, F)
+_sb("WIN", 896, F)
+_sb("VR", 896, F)
+_sb("NU", 128, F)
+for _m in ("0", "1", "2", "S"):
+    _sb("OFF" + _m, 128, U)
+    _sb("XI" + _m, 128, I)
+    _sb("XJ" + _m, 128, I)
+_sb("X01", 4096, H)
+_sb("X2", 4096, H)
+_sb("XS", 2048, H)
+_sb("RST", 2048, H)
+_sb("S2", 128, F)
+_sb("SI", 128, F)
+_sb("S1", 128, F)
+_sb("S21", 256, F)
+_sb("KS", 128, F)
+_sb("KT", 128, I)
+_sb("KI", 128, I)
+_sb("KB", 128, H)
+_sb("KB2", 128, H)
+_sb("KRB", 384, H)
+_sb("KM", 384, H)
+_sb("LF", 24, F)
+_sb("VL", 24, U)
+_sb("ZB", 16, F)
+_sb("ZC", 64, F)
+_sb("VJ", 384, F)
+_sb("EB", 3072, H)
+_sb("NF", 384, H)
+_sb("CM", 384, H)
+_sb("CN", 384, H)
+_sb("Z", 32, F)
+_sb("ZN", 8, F)
+_sb("ZQ", 8, F)
+_sb("ZX", 128, H)
+_sb("ZM", 128, F)
+_sb("ZI", 40, I)
+for _m in ("", "b"):
+    _sb("LX" + _m, 8, U)
+    _sb("NV" + _m, 128, F)
+    _sb("NX" + _m, 128, H)
+_sb("LST", 8, U)
+_sb("PP", 128, F)
+_sb("D3", 8, F)
+_sb("LST2", 8, U)
+_sb("OUTB", 512, F)
+_sb("OUTV", 512, F)
+_sb("OUTP", 128, F)
+_sb("SM", RO * 256, F)
+_sb("LM", RO * 256, F)
+_sb("ZS", RO * 8, F)
+_sb("ZL", RO * 8, F)
+_sb("CS", (RO + 1) * 128, F)
+_sb("WS", RO * 144, F)
+_sb("WL", RO * 144, F)
+_sb("PS", RO * 128, F)
+_sb("PL", (RO + 1) * 128, F)
+_sb("PQ", (RO + 1) * 128, F)
+_sb("LS", RO * 8, F)
+_sb("LQ", RO * 8, F)
+_sb("II", 8, I)
+_sb("RO8", 24, F)
+_sb("EC", 24, F)
+_sb("W8", 8, F)
+_sb("COL", 32, F)
+_sb("FF", 128, F)
+_sb("FX", 128, F)
+_sb("FG", 128, F)
+_sb("FY", 128, F)
+_sb("EXL", 8, U)
+_sb("IDN", 128, H)
+_sb("BO", 128, H)
+_sb("MSK", 128, F)
+_sb("BLK", 8, F)
+_sb("GS", 8, H)
+_sb("NSEL", 8, H)
+_sb("SEL", 384, H)
+_sb("S32", 384, H)
+_sb("S148", 384, H)
+_sb("EQ", 512, H)
+_sb("EW", 512, H)
+_sb("QS", 24, H)
+_sb("DIF", 128, F)
+_sb("TMP", 128, F)
+_sb("PSEL", 128, F)
+_sb("POLD", 128, F)
+_sb("REV", 128, F)
+_sb("NEGV", 128, F)
+_sb("BIGN", 128, H)
+_sb("BIAS", 128, H)
+_sb("WT", 1024, H)
+_sb("TH", 128, F)
+_sb("AC", 512, F)
+_sb("WC", 512, I)
+_sb("IL", 8, F)
+_sb("CX", 8, F)
+for _m in range(8):
+    SCRATCH["b%d" % _m] = ("psum", [128, 512], F)
+
+SEMAPHORES = ["cv", "cs", "ct", "cg", "snd", "l0", "l1", "l2", "o0", "o1", "o2"]
+for _m in range(RO + 1):
+    SEMAPHORES += [_k + "%d" % _m for _k in "mkzcwpqf"]
+TWO = (H, U)
+
+
+def rank_program(g, core, T, topo):
+    rank = T.rank_of(core)
+    if rank is None:
+        return
+    N = len(T.cores)
+    Q = {"v": g.vector, "s": g.scalar, "t": g.tensor, "g": g, "y": g.sync}
+    ops = []
+    acc = {}
+    cnt, clk = {}, {}
+    known = {e: {} for e in Q}
+
+    def psum(n):
+        return n[0] == "b" and len(n) == 2
+
+    def op(eng, outs, ins, call, cost, kind="c", sem=None, inc=1, extra=()):
+        k = len(ops)
+        pre = {}
+        for j in extra:
+            pre[j] = False
+        for wr, lst in ((True, outs), (False, ins)):
+            for (_, n, lo, hi) in lst:
+                for (alo, ahi, aw, ae, j) in acc.get(n, []):
+                    if psum(n) and ae == "t" and eng == "t":
+                        pre.setdefault(j, False)
+                    elif (psum(n) and ae != eng) or (alo < hi and lo < ahi and (aw or wr)):
+                        pre[j] = True
+        for wr, lst in ((False, ins), (True, outs)):
+            for (_, n, lo, hi) in lst:
+                a = acc.setdefault(n, [])
+                if psum(n) and eng == "t":
+                    a[:] = [x for x in a if x[3] == eng]
+                if wr:
+                    a[:] = [x for x in a if not (lo <= x[0] and x[1] <= hi)]
+                a.append((lo, hi, wr, eng, k))
+        ops.append({"eng": eng, "call": call, "cost": cost, "pre": pre, "kind": kind, "sem": sem, "inc": inc,
+                    "nm": (outs or ins)[0][1] + ("" if outs else "!")})
+        return k
+
+    def learn(eng, tk):
+        Q[eng].wait_ge(T.sem[tk[0]], tk[1])
+        for s, v in clk[tk].items():
+            if known[eng].get(s, 0) < v:
+                known[eng][s] = v
+
+    def need(eng, toks):
+        toks = sorted(toks)
+        for tk in toks:
+            if known[eng].get(tk[0], 0) >= tk[1]:
+                continue
+            if any(o != tk and clk[o].get(tk[0], 0) >= tk[1] and known[eng].get(o[0], 0) < o[1] for o in toks):
+                continue
+            learn(eng, tk)
+        for tk in toks:
+            if known[eng].get(tk[0], 0) < tk[1]:
+                learn(eng, tk)
+
+    def flush():
+        n = len(ops)
+        succ = [[] for _ in ops]
+        left = [len(o["pre"]) for o in ops]
+        for k, o in enumerate(ops):
+            for j in o["pre"]:
+                succ[j].append(k)
+        prio = [0.0] * n
+        for k in range(n - 1, -1, -1):
+            prio[k] = ops[k]["cost"] + max([prio[j] + (WAKE if ops[j]["pre"][k] else 0.0) for j in succ[k]], default=0.0)
+        free = {e: 0.0 for e in Q}
+        free["r"] = 0.0
+        ready = {k: 0.0 for k in range(n) if left[k] == 0}
+        done = [0.0] * n
+        seq = []
+        while ready:
+            cand = []
+            for k, av in ready.items():
+                for e in ops[k]["eng"]:
+                    b = VLATE if len(ops[k]["eng"]) > 1 and e == "v" else 0.0
+                    cand.append((max(free[e], av) + b if e != "r" else av, -prio[k], k, e))
+            m0 = min(cand)[0] + SLACK
+            st, _, k, e = min((x for x in cand if x[0] <= m0), key=lambda x: (x[1], x[0]))
+            o = ops[k]
+            st = max(free[e], ready[k]) if e != "r" else ready[k]
+            del ready[k]
+            o["on"], o["st"] = e, st
+            if o["kind"] == "arr":
+                done[k] = st
+            elif o["kind"] == "dma":
+                free[e] = st + 0.1
+                done[k] = st + o["cost"]
+            elif o["kind"] == "rem":
+                free[e] = st + ISSUE
+                done[k] = st + ISSUE + LAT
+            else:
+                done[k] = free[e] = st + o["cost"]
+            seq.append(k)
+            for j in succ[k]:
+                left[j] -= 1
+                if left[j] == 0:
+                    ready[j] = max(done[i] + (WAKE if ops[j]["pre"][i] else 0.0) for i in ops[j]["pre"])
+        tok = {}
+        for k in seq:
+            o = ops[k]
+            e = o["on"]
+            if o["kind"] == "arr":
+                tok[k] = (o["sem"], o["inc"])
+                clk[tok[k]] = {o["sem"]: o["inc"]}
+                continue
+            need(e, set(tok[j] for j, w in o["pre"].items() if w))
+            if o["kind"] == "rem":
+                o["call"]()
+                continue
+            sem = o["sem"] or "c" + e
+            cnt[sem] = cnt.get(sem, 0) + o["inc"]
+            tok[k] = (sem, cnt[sem])
+            o["call"](e).then_inc(T.sem[sem], o["inc"])
+            c = dict(known[e])
+            c[sem] = cnt[sem]
+            clk[tok[k]] = c
+        return seq
+
+    sent = [0]
+    sends = {}
+
+    def arrive(n, lo, hi, key, val):
+        op("r", [(None, n, lo, hi)], [], None, 0.0, "arr", key, val, [sends[key]])
+
+    def B(n, lo=0, hi=None):
+        return (T[n][:, lo:SCRATCH[n][1][1] if hi is None else hi], n, lo, SCRATCH[n][1][1] if hi is None else hi)
+
+    V, S_, P_ = g.vector, g.scalar, g.tensor
+
+    def a_(x):
+        return x[0] if isinstance(x, tuple) else x
+
+    def cols(*xs):
+        return [x for x in xs if isinstance(x, tuple)]
+
+    def el(o, *xs):
+        n = 1
+        for d in o[0].shape[1:]:
+            n *= d
+        if all(SCRATCH[x[1]][2] in TWO for x in (o,) + xs):
+            n = n // 2
+        return max(64, n) * CYC
+
+    def copy(o, i):
+        return op("v", [o], [i], lambda e: V.tensor_copy(o[0], i[0]), el(o, i))
+
+    def tt(o, x, y, f):
+        c = el(o) if psum(x[1]) or psum(y[1]) or el(o) < 0.07 else 2 * el(o)
+        return op("v", [o], [x, y], lambda e: V.tensor_tensor(o[0], x[0], y[0], f), c)
+
+    def ts(o, x, s1, f1, s2=None, f2=None):
+        if f2 is None:
+            return op("v", [o], [x] + cols(s1), lambda e: V.tensor_scalar(o[0], x[0], a_(s1), None, f1), el(o, x))
+        return op("v", [o], [x] + cols(s1, s2), lambda e: V.tensor_scalar(o[0], x[0], a_(s1), a_(s2), f1, f2), el(o, x))
+
+    def scaled(o, x, c):
+        return op("vs", [o], [x, c], lambda e: V.tensor_scalar(o[0], x[0], c[0], None, OP.mult) if e == "v"
+                  else S_.activation(o[0], x[0], AF.Copy, scale=c[0]), el(o))
+
+    def fill(o, c):
+        return op("v", [o], [], lambda e: V.memset(o[0], c), el(o))
+
+    def scan(o, d0, d1, f0, f1):
+        return op("v", [o], [d0, d1], lambda e: V.tensor_tensor_scan(o[0], d0[0], d1[0], 0.0, f0, f1), el(o, d0, d1))
+
+    def act(o, i, func=AF.Copy, scale=1.0, bias=0.0):
+        if isinstance(bias, float) and bias == 0.0:
+            return op("s", [o], [i] + cols(scale), lambda e: S_.activation(o[0], i[0], func, scale=a_(scale)), el(o))
+        return op("s", [o], [i] + cols(bias, scale), lambda e: S_.activation(o[0], i[0], func, bias=a_(bias), scale=a_(scale)), el(o))
+
+    def mm(o, l, r, start=True, stop=True):
+        n = max(min(64, l[0].shape[1]), r[0].shape[1])
+        return op("t", [o], [l, r], lambda e: P_.matmul(o[0], l[0], r[0], start, stop), n * PEC * (4 if SCRATCH[l[1]][2] == F else 1))
+
+    def ind(w, off):
+        return w[0].indirect(off[0])
+
+    def gat(eng, o, w, off):
+        return op(eng, [o], [w, off], lambda e: V.tensor_copy(o[0], ind(w, off)) if e == "v"
+                  else S_.activation(o[0], ind(w, off), AF.Copy), 0.06 + 16 * off[0].shape[1] * CYC * GAT)
+
+    def sca(w, off, i):
+        return op("v", [w], [i, off], lambda e: V.tensor_copy(ind(w, off), i[0]), 0.06 + 128 * CYC * SCA)
+
+    def scamul(w, off, x, y):
+        return op("v", [w], [x, y, off], lambda e: V.tensor_tensor(ind(w, off), x[0], y[0], OP.mult), 0.06 + 128 * CYC * SCA)
+
+    def iota(o, pattern, base, cm):
+        c = 0.13 + 2 * el(o)
+        if SCRATCH[o[1]][2] == I:
+            return op("g", [o], [], lambda e: g.iota(o[0], pattern, base, cm), c)
+        return op("g", [o], [], lambda e: g.iota(o[0], pattern, base, cm, allow_small_or_imprecise_dtypes=True), c)
+
+    def dma(q, outs, ins, out, in_, sem):
+        return op(q, outs, ins, lambda e: Q[q].dma_start(out, in_), 7.0 if sem == "l1" else 2.5, "dma", sem, 16)
+
+    def addr(r):
+        return topo.addr(T.cores[r])[:2]
+
+    def send(r, dst, src, sem):
+        m = topo.mask(core, T.cores[r])
+        rid, pid = addr(r)
+        sends[sem] = op("g", [], [src], lambda: g.remote_dma(dst[0], src[0], T.sem[sem], T.sem["snd"], pid, rid, m), ISSUE + LAT, "rem")
+        sent[0] += len(topo.engines(core, T.cores[r]))
+
+    def width(r):
+        return len(topo.engines(T.cores[r], core))
+
+    def col(k):
+        return B("COL", k, k + 1)
+
+    def cls(n, c):
+        return B(n, 128 + 128 * c, 256 + 128 * c)
+
+    def third(n, m):
+        return B(n, 128 * m, 128 * m + 128)
+
+    def eight(n, m):
+        return B(n, 8 * m, 8 * m + 8)
+
+    dma("y", [B("RAWB")], [], T.RAWB[:], T.bun[:], "l0")
+    dma("y", [B("TAB", 0, 4096)], [], T.TAB[:, 0:4096], T.sight[:], "l1")
+    fill(B("POTI"), 0)
+    dma("y", [B("POTI")], [], T.POTI[0:128:16, :], T.pots[:], "l2")
+    fill(B("TAB", 4096, 4112), 0.0)
+
+    iota(B("II", 0, 1), [[1, 1]], 0, 1)
+    iota(B("FX"), [[0, 8], [1, 16]], 0, 0)
+    iota(B("FG"), [[1, 8], [0, 16]], 0, 0)
+    iota(B("AC"), [[8, 4], [32, 128]], 5, 0)
+    iota(B("WC"), [[37, 4], [148, 128]], 0, 0)
+    iota(B("FF"), [[1, 128]], 0, 0)
+    iota(B("RO8", 0, 3), [[-1, 3]], 15, 0)
+    iota(B("RO8", 8, 12), [[8, 4]], 5, 0)
+    iota(B("RO8", 12, 16), [[37, 4]], 0, 0)
+    iota(B("RO8", 16, 24), [[16, 8]], 0, 0)
+    iota(B("FY"), [[0, 8], [1, 16]], 1, 0)
+    for c in range(4):
+        z0, z1 = (2048 * (2 - m) + 128 + 128 * ((c + 1 + m) & 3) for m in range(2))
+        iota(B("ZC", 16 * c, 16 * c + 16), [[z1 - z0, 2], [0, 8]], z0, 0)
+    copy(col(0), B("II", 0, 1))
+    ts(B("II", 1, 2), B("II", 0, 1), 15, OP.bitwise_and)
+    ts(B("II", 2, 3), B("II", 0, 1), 4, OP.logical_shift_right)
+    copy(B("COL", 1, 3), B("II", 1, 3))
+    ts(B("BO"), B("FG"), col(2), OP.is_equal)
+    ts(col(12), col(1), -1.0, OP.mult, 15.0, OP.add)
+    ts(B("TMP"), B("FX"), col(12), OP.is_equal)
+    tt(B("REV"), B("BO"), B("TMP"), OP.mult)
+    for c in range(4):
+        copy(third("BF", c), (T.RAWB[:, c::4], "RAWB", 0, 512))
+        mm(third("b0", c), B("REV"), third("BF", c))
+        act(cls("WIN", c), third("b0", c), AF.Identity, 1.0, 1.0)
+    ts(B("WC"), B("WC"), 4095, OP.bitwise_and)
+    fill(B("RST"), 1.0)
+    op("v", [B("RST")], [], lambda e: V.memset(T.RST[:, 0:2048:16], 0.0), 128 * CYC)
+    ts(B("IDN"), B("FF"), col(0), OP.is_equal)
+    ts(B("MSK"), B("FX"), col(1), OP.is_equal)
+    ts(B("BLK"), B("FF", 0, 8), col(2), OP.is_equal)
+    copy(B("GS"), B("BLK"))
+    copy(B("EXL"), B("FF", 0, 8))
+    ts(col(3), col(1), 0.0, OP.is_equal)
+    ts(col(4), col(1), 0.0, OP.is_gt)
+    ts(col(8), col(1), 13.0, OP.is_ge)
+    ts(col(9), col(1), -2.0, OP.mult, 18.0, OP.add)
+    ts(col(10), col(0), 768.0, OP.add, 1.0 / 4096, OP.mult)
+    ts(col(11), col(0), 3.0 * 2048 + 640 - 65536, OP.add, 1.0 / 4096, OP.mult)
+    ts(B("ZC"), B("ZC"), 1.0 / 4096, OP.mult)
+    ts(B("EC", 0, 3), B("RO8", 0, 3), col(1), OP.is_equal)
+    ts(B("EC", 3, 6), B("EC", 0, 3), 32.0, OP.mult)
+    ts(B("EC", 6, 9), B("EC", 0, 3), 148.0, OP.mult)
+    ts(B("EC", 9, 17), B("RO8", 8, 16), col(3), OP.mult)
+    ts(B("BIAS"), B("MSK"), 512.0, OP.mult, -512.0, OP.add)
+    for m in range(3):
+        scaled(third("SEL", m), B("BO"), B("EC", m, m + 1))
+        scaled(third("S32", m), B("BO"), B("EC", 3 + m, 4 + m))
+        scaled(third("S148", m), B("BO"), B("EC", 6 + m, 7 + m))
+        ts(eight("QS", m), B("GS"), B("EC", m, m + 1), OP.mult, 1.0 / 4096, OP.mult)
+    for c in range(4):
+        scaled(third("EQ", c), B("BO"), B("EC", 9 + c, 10 + c))
+        scaled(third("EW", c), B("BO"), B("EC", 13 + c, 14 + c))
+    ts(B("IL"), B("RO8", 16, 24), col(1), OP.add)
+    ts(B("CX"), B("IL"), 16.0, OP.mult, 4096.0 + 16.0, OP.add)
+    fill(col(14), 63 * math.log(2.0))
+    fill(col(15), 63 * math.log(2.0) + math.log(2.5))
+    act(B("W8"), B("IL"), AF.Exp, -math.log(2.0), col(14))
+    act(B("TH"), B("FF"), AF.Exp, -math.log(2.0), col(15))
+    for c in range(8):
+        scaled(third("WT", c), B("BO"), B("W8", c, c + 1))
+    ts(B("NEGV"), B("BO"), col(3), OP.mult, -1.0, OP.mult)
+    ts(B("BIGN"), B("BO"), col(3), OP.mult, -16384.0, OP.mult)
+    ts(B("NSEL"), B("GS"), col(3), OP.mult, -64.0, OP.mult)
+    fill(B("VR", 0, 128), 0.0)
+    fill(B("VR", 640, 896), 0.0)
+    fill(B("WIN", 0, 128), 0.0)
+    ts(third("PL", 0), B("POTI"), 1.0, OP.add, col(3), OP.mult)
+    ts(B("TMP"), B("FX"), 0.0, OP.is_equal)
+    tt(B("PSEL"), B("BO"), B("TMP"), OP.mult)
+    ts(col(16), col(1), 1.0, OP.is_equal)
+    ts(B("POLD"), B("PSEL"), col(16), OP.mult)
+    ts(col(13), col(3), 16.0, OP.mult, col(1), OP.add)
+    ts(B("FY"), B("FY"), col(13), OP.is_equal)
+    tt(B("TMP"), B("FY"), B("MSK"), OP.subtract)
+    tt(B("DIF"), B("TMP"), B("BO"), OP.mult)
+    ts(B("TMP"), B("FX"), 0.0, OP.is_gt)
+    tt(B("DIF"), B("DIF"), B("TMP"), OP.mult)
+
+    FLAG = (1 << 19) | 4095
+
+    def index(tag, s, a, w):
+        xi, xj, off = B("XI" + tag), B("XJ" + tag), B("OFF" + tag)
+        tt(xi, s, a, OP.mult)
+        ts(xj, xi, 5, OP.arith_shift_right, FLAG, OP.bitwise_and)
+        tt(xi, xj, w, OP.add)
+        ts(xj, xi, FLAG, OP.bitwise_and)
+        ts(off, xj, 4096.0, OP.min)
+
+    TABW = B("TAB", 0, 4097)
+
+    def look(tag, xn, base):
+        w = 128 // CHS[tag]
+        for a in range(0, 128, w):
+            x = B(xn, base + 16 * a, base + 16 * (a + w))
+            gat("sv", x, TABW, B("OFF" + tag, a, a + w))
+            scan(x, B("RST", 0, 16 * w), x, OP.mult, OP.max)
+
+    def selfsum(xn, base, c, bank):
+        o = B(bank, 128, 256)
+        mm(o, B("BO"), (T[xn][:, base + 15:base + 2048:16], xn, base, base + 2048))
+        act(cls("VR", c), o)
+
+    for c, (tag, xn, base) in enumerate((("S", "XS", 0), ("0", "X01", 0), ("1", "X01", 2048), ("2", "X2", 0))):
+        index(tag, third("b0", c), third("AC", c), third("WC", c))
+        look(tag, xn, base)
+        selfsum(xn, base, c, "b%d" % (4 + c))
+
+    def partner(r, t):
+        return (r + 1 + t % 3) % N
+
+    def asker(t):
+        return (rank - 1 - t % 3) % N
+
+    def kpart(t):
+        c = t & 3
+        tt(B("KS"), cls("WIN", c), cls("VR", c), OP.add)
+        ts(B("KT"), B("KS"), 13.0 * t - 1.0, OP.add)
+        ts(B("KI"), B("KT"), 127, OP.bitwise_and)
+        ts(third("SM", 2 * t + 1), B("KI"), col(8), OP.mult, col(3), OP.add)
+        act(B("KB"), third("SM", 2 * t + 1))
+
+    def marks(t, ms, kb):
+        for m in ms:
+            cm = (t + 1 + m) & 3
+            mm(third("b0", m), third("S32", m), kb, True, False)
+            mm(third("b0", m), third("EQ", cm), kb, False, True)
+            mm(third("b1", m), third("S148", m), kb, True, False)
+            mm(third("b1", m), third("EW", cm), kb, False, True)
+
+    def spread(t, kb):
+        for m in range(3):
+            mm(third("b2", m), third("SEL", m), kb)
+        mm(B("b3", 0, 384), kb, B("SEL"), True, False)
+        for m in range(3):
+            mm(third("b3", m), B("IDN"), B("BIAS"), False, m == 2)
+        act(B("KM"), B("b3", 0, 384), AF.Relu)
+        act(B("KRB", 0, 256), B("b2", 0, 256))
+        act(B("KRB", 256, 384), B("b2", 256, 384))
+        for m in range(3):
+            mm(B("b3", 384 + m * 8, 392 + m * 8), third("KM", m), B("GS"))
+        mm(B("b3", 416, 432), kb, B("QS", 0, 16))
+        copy(B("LF"), B("b3", 384, 408))
+        ts(eight("LS", t), eight("LF", 2), 128.0 + 128 * ((t + 3) & 3), OP.add)
+        for m in range(2):
+            ts(eight("VL", m), eight("LF", m), 128.0 + 128 * ((t + 1 + m) & 3), OP.add)
+        tt(B("ZB"), B("b3", 416, 432), B("ZC", 16 * (t & 3), 16 * (t & 3) + 16), OP.add)
+
+    def firsts():
+        for c in range(8):
+            for m in range(3):
+                o = c * 384 + m * 128
+                ts(B("EB", o, o + 128), third("KRB", m), B("LF", m * 8 + c, m * 8 + c + 1), OP.is_equal)
+            mm(B("b7", 0, 384), third("WT", c), B("EB", c * 384, c * 384 + 384), c == 0, c == 7)
+        for m in range(3):
+            tt(third("NF", m), third("b7", m), B("TH"), OP.is_gt)
+
+    def vj(m):
+        gat("sv", third("VJ", m), B("VR", 0, 640), eight("VL", m))
+
+    def verdict(m, xn, base):
+        bank = "b%d" % (4 + m)
+        o = B(bank, 0, 128)
+        mm(o, third("VJ", m), B("NEGV"), True, False)
+        if m < 2:
+            mm(o, third("NF", m), B("BIGN"), False, False)
+        for x in range(16):
+            mm((T[bank][:, x:128:16], bank, 0, 128), (T[xn][:, base + x:base + 2048:16], xn, base, base + 2048), B("GS"), False, x == 15)
+        act(third("CM", m), o, AF.Sign, 1.0, -0.5)
+        scan(third("CN", m), B("RST", 0, 128), third("CM", m), OP.mult, OP.add)
+        return (T.CN[:, m * 128 + 15:m * 128 + 128:16], "CN", m * 128, m * 128 + 128)
+
+    def late(t):
+        o = t * 144
+        x2 = (t & 1) * 2048
+        arrive("WL", o, o + 144, "w%d" % t, width(asker(t)))
+        ts(B("LXb"), B("WL", o + 136, o + 144), -4096.0, OP.add, 2047.0, OP.min)
+        tt(B("D3"), B("WL", o + 128, o + 136), eight("LQ", t), OP.min)
+        copy(B("LST2"), B("D3"))
+        gat("sv", B("NXb"), B("X2", x2, x2 + 2048), B("LXb"))
+        mm(B("b6", 384, 512), B("BO"), B("NXb"))
+        act(B("NVb"), B("b6", 384, 512))
+        scamul(B("WIN", 0, 640), B("LST2"), third("S21", t & 1), B("WL", o, o + 128))
+        sca(B("VR", 0, 640), B("LST2"), B("NVb"))
+
+    def selflook(t):
+        c = t & 3
+        index("S", B("NU"), third("AC", c), third("WC", c))
+        look("S", "XS", 0)
+        selfsum("XS", 0, c, "b4")
+
+    for t in range(RO):
+        q = partner(rank, t)
+        ask = asker(t)
+        old = cls("WIN", t & 3)
+        S = B("WIN", 640, 768)
+        sm, smk = third("SM", 2 * t), third("SM", 2 * t + 1)
+        lm, lk = third("LM", 2 * t), third("LM", 2 * t + 1)
+        act(sm, old, AF.Identity, col(4), -1.0)
+        si = B("SI")
+        if t == 0:
+            si = third("CS", RO)
+            tt(si, sm, third("PL", 0), OP.add)
+            send(q, lm, si, "m0")
+        kpart(t)
+        if t == 0:
+            send(q, lk, smk, "k0")
+        else:
+            send(q, B("LM", t * 256, t * 256 + 256), B("SM", t * 256, t * 256 + 256), "m%d" % t)
+        spread(t, B("KB"))
+        send(q, eight("LQ", t), eight("LS", t), "f%d" % t)
+        marks(t, [0, 1], B("KB"))
+        mm(B("b5", 256, 384), B("DIF"), old)
+        vj(0)
+        firsts()
+        mm(B("b3", 432, 440), third("NF", 2), B("NSEL"))
+        if t:
+            selflook(t - 1)
+        wk = width(ask)
+        if t == 0:
+            arrive("LM", 0, 128, "m0", wk)
+            arrive("LM", 128, 256, "k0", wk)
+        else:
+            arrive("LM", t * 256, t * 256 + 256, "m%d" % t, wk)
+        act(B("KB2"), lk)
+        marks(t, [2], B("KB2"))
+        if t == 0:
+            S2 = lm
+        else:
+            pr = (ask - 1) % N
+            if pr == rank:
+                pq = third("PS", t - 1)
+            else:
+                arrive("PQ", t * 128, t * 128 + 128, "q%d" % t, width(pr) // 2)
+                pq = third("PQ", t)
+            S2 = B("S2")
+            tt(S2, lm, pq, OP.add)
+        x2 = (t & 1) * 2048
+        index("2", S2, third("b0", 2), third("b1", 2))
+        look("2", "X2", x2)
+        act(third("S21", t & 1), S2, AF.Identity, 1.0, 1.0)
+        if t:
+            solo = partner(rank, t) == (rank - 1) % N
+            arrive("PL", t * 128, t * 128 + 128, "p%d" % t, width((rank - 1) % N) // (1 if solo else 2))
+            tt(si, sm, third("PL", t), OP.add)
+        act(S, si, AF.Identity, 1.0, 1.0)
+        act(B("S1"), si, AF.Identity, 1.0, 1.0)
+        index("0", si, third("b0", 0), third("b1", 0))
+        look("0", "X01", 0)
+        arrive("LQ", t * 8, t * 8 + 8, "f%d" % t, wk)
+        copy(eight("VL", 2), eight("LQ", t))
+        vj(2)
+        cs = third("CS", t)
+        gat("sv", cs, B("WIN", 0, 640), eight("VL", 2))
+        send(ask, B("WIN", 768, 896), cs, "c%d" % t)
+        e2 = verdict(2, "X2", x2)
+        zs = eight("ZS", t)
+        ts(zs, e2, col(10), OP.add)
+        send(ask, eight("ZL", t), zs, "z%d" % t)
+        index("1", si, third("b0", 1), third("b1", 1))
+        look("1", "X01", 2048)
+        if t:
+            late(t - 1)
+        vj(1)
+        e0 = verdict(0, "X01", 0)
+        tt(eight("Z", 0), e0, eight("ZB", 0), OP.add)
+        e1 = verdict(1, "X01", 2048)
+        tt(eight("Z", 1), e1, eight("ZB", 1), OP.add)
+        tt(eight("Z", 2), eight("Z", 0), eight("Z", 1), OP.max)
+        ts(eight("Z", 3), eight("Z", 2), col(11), OP.max)
+        mm(B("b1", 384, 512), B("POLD"), old, True, False)
+        arrive("ZL", t * 8, t * 8 + 8, "z%d" % t, width(q))
+        zq, zx, zm = B("ZQ"), B("ZX"), B("ZM")
+        wo = t * 144
+        keep = B("WS", wo, wo + 128)
+        tt(B("ZN"), eight("ZL", t), B("b3", 432, 440), OP.add)
+        tt(zq, eight("Z", 3), B("ZN"), OP.max)
+        gat("s", zx, zq, B("EXL"))
+        op("v", [zm], [zq, B("EXL"), B("MSK")], lambda e: V.tensor_tensor(T.ZM[:], T.ZQ[:].indirect(T.EXL[:]), T.MSK[:], OP.mult),
+           0.06 + 128 * CYC * GAT)
+        mm(B("b2", 0, 128), zx, B("IDN"))
+        mm(B("b3", 440, 448), zm, B("BLK"))
+        ts(keep, B("b2", 0, 128), col(9), OP.is_lt)
+        ts(B("ZI", 0, 8), B("b3", 440, 448), 4096.0, OP.mult, 65536.0, OP.add)
+        tt(B("PP"), B("b5", 256, 384), keep, OP.mult)
+        mm(B("b1", 384, 512), B("PSEL"), B("PP"), False, True)
+        ps = third("PS", t)
+        act(ps, B("b1", 384, 512))
+        nx = (rank + 1) % N
+        z = partner(nx, t + 1)
+        pl = third("PL", t + 1)
+        if t == RO - 1 or z == rank:
+            send(nx, pl, ps, "p%d" % (t + 1))
+        else:
+            tr = []
+            for k, (dst, land, sm_) in enumerate(((nx, pl, "p"), (z, third("PQ", t + 1), "q"))):
+                en = topo.engines(core, T.cores[dst])
+                en = en[k * len(en) // 2:(k + 1) * len(en) // 2]
+                rid, pid = addr(dst)
+                tr.append(RemoteDMATransfer(dst_ids=[DstId(rid=rid, pnc=pid)], dma_engine_mask=sum(1 << e for e in en),
+                                            remote_sem=T.sem["%s%d" % (sm_, t + 1)], srcs=[ps[0]], dsts=[land[0]]))
+                sent[0] += len(en)
+            sends["p%d" % (t + 1)] = sends["q%d" % (t + 1)] = op(
+                "g", [], [ps], lambda tr=tr: g.remote_dma_fused(tr, local_sem=T.sem["snd"]), ISSUE + LAT, "rem")
+        ts(B("ZI", 32, 40), B("ZI", 0, 8), 1023, OP.bitwise_and)
+        copy(B("LST"), B("ZI", 32, 40))
+        ts(B("ZI", 8, 16), B("ZI", 0, 8), 13, OP.logical_shift_right)
+        ts(B("ZI", 16, 24), B("ZI", 0, 8), 6144, OP.bitwise_and)
+        tt(B("ZI", 8, 16), B("ZI", 8, 16), B("ZI", 16, 24), OP.add)
+        lx = B("WS", wo + 136, wo + 144)
+        tt(lx, B("CX"), B("ZI", 8, 16), OP.subtract)
+        ts(B("LX"), lx, 4095.0, OP.min)
+        gat("sv", B("NX"), B("X01"), B("LX"))
+        mm(B("b7", 384, 512), B("BO"), B("NX"))
+        act(B("NV"), B("b7", 384, 512))
+        ws = B("WS", wo + 128, wo + 136)
+        ts(ws, B("ZI", 32, 40), 768.0, OP.is_ge, 2000.0, OP.mult)
+        tt(ws, ws, B("IL"), OP.max)
+        send(q, B("WL", wo, wo + 144), B("WS", wo, wo + 144), "w%d" % t)
+        arrive("WIN", 768, 896, "c%d" % t, width(q))
+        nu, w, ls = B("NU"), B("WIN"), B("LST")
+        op("sv", [nu], [w, ls], lambda e: V.tensor_scalar(T.NU[:], T.WIN[:].indirect(T.LST[:]), -1.0, None, OP.add) if e == "v"
+           else S_.activation(T.NU[:], T.WIN[:].indirect(T.LST[:]), AF.Identity, bias=-1.0), 0.06 + 128 * CYC * GAT)
+        scamul(w, ls, B("S1"), keep)
+        sca(B("VR"), ls, B("NV"))
+        act(old, nu, AF.Identity, 1.0, 1.0)
+
+    late(RO - 1)
+    for k in range(4):
+        mm(third("b0", k), B("REV"), cls("WIN", k))
+        ts((T.OUTB[:, k::4], "OUTB", 0, 512), third("b0", k), -1.0, OP.add)
+    dma("y", [], [B("OUTB")], T.yb[:], T.OUTB[:], "o0")
+    selflook(RO - 1)
+    for k in range(4):
+        copy((T.OUTV[:, k::4], "OUTV", 0, 512), cls("VR", k))
+    dma("y", [], [B("OUTV")], T.yv[:], T.OUTV[0:128:16, :], "o1")
+    arrive("PL", RO * 128, RO * 128 + 128, "p%d" % RO, width((rank - 1) % N))
+    ts(B("OUTP"), third("PL", RO), -1.0, OP.add)
+    dma("y", [], [B("OUTP")], T.yp[:], T.OUTP[0:128:16, :], "o2")
+    flush()
+    for k in ("o0", "o1", "o2"):
+        g.sync.wait_ge(T.sem[k], 16)
+    for k in ("cv", "cs", "ct", "cg"):
+        if cnt.get(k):
+            g.wait_ge(T.sem[k], cnt[k])
+    g.wait_ge(T.sem["snd"], sent[0])

@@ -1,11 +1,23 @@
 import math
 from concourse.bass import DstId, RemoteDMATransfer
-from concourse.mybir import AluOpType as OP, ActivationFunctionType as AF
+from concourse.mybir import AluOpType as OP, ActivationFunctionType as AF, AxisListType as AX
 
-F, H, I, U = "float32", "bfloat16", "int32", "uint16"
+F, H, G, I, U = "float32", "bfloat16", "float16", "int32", "uint16"
 RO = 5
-CYC, PEC, WAKE, ISSUE, LAT, GAT, SCA, SLACK, VLATE = 0.001, 0.0008, 0.08, 1.2, 2.0, 1.6, 4.0, 0.1, 0.3
-CHS = {"S": 4, "0": 4, "1": 4, "2": 4}
+CYC, PEC, WAKE, ISSUE, GAT, SCA, SLACK = 0.00083, 0.00083, 0.2, 1.2, 1.6, 3.8, 0.3
+CH = 64
+PIECES = ((("s", 32), ("s", 32), ("s", 32), ("v", 32)), (("s", 32), ("s", 32), ("s", 32), ("v", 32)),
+          (("s", 32), ("s", 32), ("s", 32), ("s", 16), ("v", 16)),
+          (("s", 16), ("s", 32), ("s", 32), ("s", 48)))
+FIRST = ((("s", 48), ("v", 32), ("s", 48)), (("s", 64), ("s", 64)), (("s", 64), ("s", 64)), (("s", 64), ("v", 32), ("s", 32)))
+TILES = (((0, 128),), ((0, 128),), ((0, 128),))
+LAST = (("s", 32), ("s", 32), ("s", 32), ("v", 32))
+TURNS = ("names index0 lists lists2 index1 rows0 value0 rows1 rows2 gatherS helpS first0 late first1 pool gather0 index2 value1 first2 "
+         "scanS value2 bundle2 scan0 verdict0 gather1 help0 scan1 help1 verdict1 gather2 help2 scan2 verdict2 decide indexS change end").split()
+SEG = 19
+NV_ = 8 * SEG
+UNIT = 2.0 ** -22
+VOFF = 64.0
 
 SCRATCH = {}
 
@@ -15,112 +27,103 @@ def _sb(name, w, d):
 
 
 _sb("TAB", 4112, H)
-_sb("RAWB", 512, I)
+for _m, _w, _d in (("T", 1024, H), ("P", 2, I)):
+    SCRATCH["D" + _m] = ("dram", [4, 128, _w], _d)
+    SCRATCH["L" + _m] = ("dram", [4, 128, _w], _d)
+_sb("TAB0", 4112, H)
+_sb("RAW0", 512, I)
+for _m, _w in (("VA", 16), ("LVA", 16), ("VB", 32), ("LVB", 32)):
+    _sb(_m, _w, F)
+_sb("EXV", 32, U)
+_sb("SU", 512, U)
+_sb("LB", 512, U)
+_sb("BN", 512, F)
 _sb("POTI", 128, I)
+_sb("PL0", 128, F)
 _sb("BF", 512, F)
-_sb("WIN", 896, F)
-_sb("VR", 896, F)
+_sb("KC", 512, H)
+_sb("WIN", 1024, F)
+_sb("VR", 1024, F)
+BASE = (0, 256, 384, 640)
 _sb("NU", 128, F)
 for _m in ("0", "1", "2", "S"):
-    _sb("OFF" + _m, 128, U)
     _sb("XI" + _m, 128, I)
     _sb("XJ" + _m, 128, I)
-_sb("X01", 4096, H)
-_sb("X2", 4096, H)
+    _sb("OFF" + _m, 128, U)
+_sb("X", 6144, H)
 _sb("XS", 2048, H)
-_sb("RST", 2048, H)
-_sb("S2", 128, F)
-_sb("SI", 128, F)
-_sb("S1", 128, F)
-_sb("S21", 256, F)
+_sb("RST", 16 * CH, H)
+_sb("S2", 256, F)
+for _m in ("SM", "S1", "CS", "KEEP", "KEEP1", "KEEP2", "NV", "NVb", "PP", "ZM", "TMP", "MSK", "REV", "DIF", "PSEL", "POLD",
+           "PSELA", "POLDA"):
+    _sb(_m, 128, F)
 _sb("KS", 128, F)
 _sb("KT", 128, I)
 _sb("KI", 128, I)
 _sb("KB", 128, H)
-_sb("KB2", 128, H)
 _sb("KRB", 384, H)
 _sb("KM", 384, H)
-_sb("LF", 24, F)
+_sb("LF", 24, H)
+_sb("LQ", 8, F)
 _sb("VL", 24, U)
-_sb("ZB", 16, F)
-_sb("ZC", 64, F)
 _sb("VJ", 384, F)
 _sb("EB", 3072, H)
-_sb("NF", 384, H)
-_sb("CM", 384, H)
-_sb("CN", 384, H)
-_sb("Z", 32, F)
-_sb("ZN", 8, F)
-_sb("ZQ", 8, F)
+_sb("CODE", 3 * NV_, F)
+_sb("ZS", 3 * NV_, F)
 _sb("ZX", 128, H)
-_sb("ZM", 128, F)
-_sb("ZI", 40, I)
-for _m in ("", "b"):
-    _sb("LX" + _m, 8, U)
-    _sb("NV" + _m, 128, F)
-    _sb("NX" + _m, 128, H)
-_sb("LST", 8, U)
-_sb("PP", 128, F)
-_sb("D3", 8, F)
-_sb("LST2", 8, U)
-_sb("OUTB", 512, F)
-_sb("OUTV", 512, F)
-_sb("OUTP", 128, F)
-_sb("SM", RO * 256, F)
-_sb("LM", RO * 256, F)
-_sb("ZS", RO * 8, F)
-_sb("ZL", RO * 8, F)
-_sb("CS", (RO + 1) * 128, F)
-_sb("WS", RO * 144, F)
-_sb("WL", RO * 144, F)
-_sb("PS", RO * 128, F)
-_sb("PL", (RO + 1) * 128, F)
-_sb("PQ", (RO + 1) * 128, F)
-_sb("LS", RO * 8, F)
-_sb("LQ", RO * 8, F)
+_sb("ZL", 8, F)
+_sb("ZI", 64, I)
+_sb("ZT", 32, F)
+for _m in ("LX", "LXb", "LST", "LST2", "EXL"):
+    _sb(_m, 8, U)
+_sb("NX", 128, H)
+_sb("NXb", 128, H)
+_sb("WH", 640, G)
+_sb("HOME", 4 * 132, G)
+_sb("OU", 640, U)
+_sb("LO", 640, U)
+_sb("OUT", 640, F)
+_sb("VT", 32, F)
+_sb("LV", 24, F)
 _sb("II", 8, I)
-_sb("RO8", 24, F)
-_sb("EC", 24, F)
-_sb("W8", 8, F)
-_sb("COL", 32, F)
-_sb("FF", 128, F)
+_sb("FF", 132, F)
 _sb("FX", 128, F)
 _sb("FG", 128, F)
-_sb("FY", 128, F)
-_sb("EXL", 8, U)
+_sb("SLOT", NV_, F)
+_sb("T19", NV_, F)
+_sb("C64", 8, H)
+_sb("VI", 32, I)
+_sb("U19", NV_, F)
+_sb("NEGV", 2 * NV_, F)
+_sb("CD", NV_, H)
+_sb("QX", 2 * NV_, H)
+_sb("COL", 32, F)
+_sb("RW", 48, F)
+_sb("CA", 8, F)
+_sb("CAI", 8, I)
+_sb("W8", 8, F)
+_sb("WG", 128, H)
+_sb("BO", 256, H)
+_sb("PI", 256, F)
 _sb("IDN", 128, H)
-_sb("BO", 128, H)
-_sb("MSK", 128, F)
-_sb("BLK", 8, F)
-_sb("GS", 8, H)
-_sb("NSEL", 8, H)
-_sb("SEL", 384, H)
-_sb("S32", 384, H)
-_sb("S148", 384, H)
-_sb("EQ", 512, H)
-_sb("EW", 512, H)
-_sb("QS", 24, H)
-_sb("DIF", 128, F)
-_sb("TMP", 128, F)
-_sb("PSEL", 128, F)
-_sb("POLD", 128, F)
-_sb("REV", 128, F)
-_sb("NEGV", 128, F)
-_sb("BIGN", 128, H)
 _sb("BIAS", 128, H)
-_sb("WT", 1024, H)
-_sb("TH", 128, F)
-_sb("AC", 512, F)
-_sb("WC", 512, I)
-_sb("IL", 8, F)
-_sb("CX", 8, F)
+_sb("GF", 16, F)
+_sb("GS", 16, H)
+_sb("GB", 16, H)
+_sb("G0", 8, F)
+_sb("SEL", 512, H)
+_sb("MA", 512, H)
+_sb("MW", 512, H)
+_sb("IL", 24, F)
+_sb("CX", 16, F)
+_sb("NONE", 8, F)
 for _m in range(8):
     SCRATCH["b%d" % _m] = ("psum", [128, 512], F)
 
-SEMAPHORES = ["cv", "cs", "ct", "cg", "snd", "l0", "l1", "l2", "o0", "o1", "o2"]
-for _m in range(RO + 1):
-    SEMAPHORES += [_k + "%d" % _m for _k in "mkzcwpqf"]
-TWO = (H, U)
+SEMAPHORES = ["cv", "cs", "ct", "cg", "snd", "t1", "t2", "t3", "u1", "u2", "u3", "w1", "w2", "w3", "v1", "v2", "v3", "p1", "p2", "p3",
+              "VA1", "VA2", "VA3", "VB1", "VB2", "VB3"]
+SEMAPHORES += ["d%d" % _m for _m in range(90)]
+TWO = (H, G, U)
 
 
 def rank_program(g, core, T, topo):
@@ -132,6 +135,7 @@ def rank_program(g, core, T, topo):
     ops = []
     acc = {}
     cnt, clk = {}, {}
+    lead = [-1000.0]
     known = {e: {} for e in Q}
 
     def psum(n):
@@ -147,7 +151,7 @@ def rank_program(g, core, T, topo):
                 for (alo, ahi, aw, ae, j) in acc.get(n, []):
                     if psum(n) and ae == "t" and eng == "t":
                         pre.setdefault(j, False)
-                    elif (psum(n) and ae != eng) or (alo < hi and lo < ahi and (aw or wr)):
+                    elif (psum(n) and (ae != eng or len(eng) > 1)) or (alo < hi and lo < ahi and (aw or wr)):
                         pre[j] = True
         for wr, lst in ((False, ins), (True, outs)):
             for (_, n, lo, hi) in lst:
@@ -157,8 +161,7 @@ def rank_program(g, core, T, topo):
                 if wr:
                     a[:] = [x for x in a if not (lo <= x[0] and x[1] <= hi)]
                 a.append((lo, hi, wr, eng, k))
-        ops.append({"eng": eng, "call": call, "cost": cost, "pre": pre, "kind": kind, "sem": sem, "inc": inc,
-                    "nm": (outs or ins)[0][1] + ("" if outs else "!")})
+        ops.append({"eng": eng, "call": call, "cost": cost, "pre": pre, "kind": kind, "sem": sem, "inc": inc, "lead": lead[0]})
         return k
 
     def learn(eng, tk):
@@ -181,50 +184,37 @@ def rank_program(g, core, T, topo):
 
     def flush():
         n = len(ops)
+        pre = [[(j, WAKE if w else 0.0) for j, w in o["pre"].items()] for o in ops]
         succ = [[] for _ in ops]
-        left = [len(o["pre"]) for o in ops]
-        for k, o in enumerate(ops):
-            for j in o["pre"]:
-                succ[j].append(k)
-        prio = [0.0] * n
+        for k in range(n):
+            for j, w in pre[k]:
+                succ[j].append((k, w))
+        cost = [o["cost"] for o in ops]
+        hold = [{"arr": 0.0, "dma": 0.1, "rem": ISSUE}.get(o["kind"], o["cost"]) for o in ops]
+
+        key = [o["lead"] for o in ops]
         for k in range(n - 1, -1, -1):
-            prio[k] = ops[k]["cost"] + max([prio[j] + (WAKE if ops[j]["pre"][k] else 0.0) for j in succ[k]], default=0.0)
-        free = {e: 0.0 for e in Q}
-        free["r"] = 0.0
+            key[k] = min([key[k]] + [key[j] for j, w in succ[k]])
+        left = [len(x) for x in pre]
         ready = {k: 0.0 for k in range(n) if left[k] == 0}
-        done = [0.0] * n
-        seq = []
+        free = {e: 0.0 for e in "vstgyr"}
+        at, on, seq = [0.0] * n, [""] * n, []
         while ready:
-            cand = []
-            for k, av in ready.items():
-                for e in ops[k]["eng"]:
-                    b = VLATE if len(ops[k]["eng"]) > 1 and e == "v" else 0.0
-                    cand.append((max(free[e], av) + b if e != "r" else av, -prio[k], k, e))
-            m0 = min(cand)[0] + SLACK
-            st, _, k, e = min((x for x in cand if x[0] <= m0), key=lambda x: (x[1], x[0]))
-            o = ops[k]
-            st = max(free[e], ready[k]) if e != "r" else ready[k]
-            del ready[k]
-            o["on"], o["st"] = e, st
-            if o["kind"] == "arr":
-                done[k] = st
-            elif o["kind"] == "dma":
-                free[e] = st + 0.1
-                done[k] = st + o["cost"]
-            elif o["kind"] == "rem":
-                free[e] = st + ISSUE
-                done[k] = st + ISSUE + LAT
-            else:
-                done[k] = free[e] = st + o["cost"]
+            t0, e = min((max(free[e], av), e) for k, av in ready.items() for e in ops[k]["eng"])
+            mine = sorted((key[k], k) for k in ready if e in ops[k]["eng"])
+            now = next(k for _, k in mine if ready[k] <= t0)
+            k = next(k for _, k in mine if ready[k] <= t0 + SLACK * hold[now])
+            at[k], on[k] = max(t0, ready.pop(k)), e
+            free[e] = at[k] + hold[k]
             seq.append(k)
-            for j in succ[k]:
+            for j, _ in succ[k]:
                 left[j] -= 1
                 if left[j] == 0:
-                    ready[j] = max(done[i] + (WAKE if ops[j]["pre"][i] else 0.0) for i in ops[j]["pre"])
+                    ready[j] = max(at[i] + (cost[i] + w if w or ops[i]["kind"] != "dma" else hold[i]) for i, w in pre[j])
         tok = {}
         for k in seq:
             o = ops[k]
-            e = o["on"]
+            e = on[k]
             if o["kind"] == "arr":
                 tok[k] = (o["sem"], o["inc"])
                 clk[tok[k]] = {o["sem"]: o["inc"]}
@@ -240,16 +230,17 @@ def rank_program(g, core, T, topo):
             c = dict(known[e])
             c[sem] = cnt[sem]
             clk[tok[k]] = c
-        return seq
 
     sent = [0]
     sends = {}
+    dmas = []
 
-    def arrive(n, lo, hi, key, val):
-        op("r", [(None, n, lo, hi)], [], None, 0.0, "arr", key, val, [sends[key]])
+    def arrive(x, key, val):
+        op("r", [x], [], None, 0.0, "arr", key, val, [sends[key]])
 
-    def B(n, lo=0, hi=None):
-        return (T[n][:, lo:SCRATCH[n][1][1] if hi is None else hi], n, lo, SCRATCH[n][1][1] if hi is None else hi)
+    def B(n, lo=0, hi=None, step=1):
+        hi = SCRATCH[n][1][1] if hi is None else hi
+        return (T[n][:, lo:hi] if step == 1 else T[n][:, lo:hi:step], n, lo, hi)
 
     V, S_, P_ = g.vector, g.scalar, g.tensor
 
@@ -260,10 +251,8 @@ def rank_program(g, core, T, topo):
         return [x for x in xs if isinstance(x, tuple)]
 
     def el(o, *xs):
-        n = 1
-        for d in o[0].shape[1:]:
-            n *= d
-        if all(SCRATCH[x[1]][2] in TWO for x in (o,) + xs):
+        n = o[0].shape[1]
+        if xs and all(SCRATCH[x[1]][2] in TWO for x in (o,) + xs):
             n = n // 2
         return max(64, n) * CYC
 
@@ -271,7 +260,7 @@ def rank_program(g, core, T, topo):
         return op("v", [o], [i], lambda e: V.tensor_copy(o[0], i[0]), el(o, i))
 
     def tt(o, x, y, f):
-        c = el(o) if psum(x[1]) or psum(y[1]) or el(o) < 0.07 else 2 * el(o)
+        c = el(o) if psum(x[1]) or psum(y[1]) or o[0].shape[1] <= 32 else 2 * el(o)
         return op("v", [o], [x, y], lambda e: V.tensor_tensor(o[0], x[0], y[0], f), c)
 
     def ts(o, x, s1, f1, s2=None, f2=None):
@@ -283,11 +272,15 @@ def rank_program(g, core, T, topo):
         return op("vs", [o], [x, c], lambda e: V.tensor_scalar(o[0], x[0], c[0], None, OP.mult) if e == "v"
                   else S_.activation(o[0], x[0], AF.Copy, scale=c[0]), el(o))
 
+    def plus(o, x, c):
+        return op("sv", [o], [x], lambda e: V.tensor_scalar(o[0], x[0], c, None, OP.add) if e == "v"
+                  else S_.activation(o[0], x[0], AF.Identity, bias=c), el(o))
+
     def fill(o, c):
-        return op("v", [o], [], lambda e: V.memset(o[0], c), el(o))
+        return op("v", [o], [], lambda e: V.memset(o[0], c), el(o, o))
 
     def scan(o, d0, d1, f0, f1):
-        return op("v", [o], [d0, d1], lambda e: V.tensor_tensor_scan(o[0], d0[0], d1[0], 0.0, f0, f1), el(o, d0, d1))
+        return op("v", [o], [d0, d1], lambda e: V.tensor_tensor_scan(o[0], d0[0], d1[0], 0.0, f0, f1), 2 * el(o, d0, d1))
 
     def act(o, i, func=AF.Copy, scale=1.0, bias=0.0):
         if isinstance(bias, float) and bias == 0.0:
@@ -306,10 +299,10 @@ def rank_program(g, core, T, topo):
                   else S_.activation(o[0], ind(w, off), AF.Copy), 0.06 + 16 * off[0].shape[1] * CYC * GAT)
 
     def sca(w, off, i):
-        return op("v", [w], [i, off], lambda e: V.tensor_copy(ind(w, off), i[0]), 0.06 + 128 * CYC * SCA)
+        return op("s", [w], [i, off], lambda e: S_.activation(ind(w, off), i[0], AF.Silu), 0.06 + 128 * CYC * SCA)
 
-    def scamul(w, off, x, y):
-        return op("v", [w], [x, y, off], lambda e: V.tensor_tensor(ind(w, off), x[0], y[0], OP.mult), 0.06 + 128 * CYC * SCA)
+    def scamax(w, off, x, y):
+        return op("v", [w], [x, y, off], lambda e: V.tensor_tensor(ind(w, off), x[0], y[0], OP.max), 0.06 + 128 * CYC * SCA)
 
     def iota(o, pattern, base, cm):
         c = 0.13 + 2 * el(o)
@@ -317,26 +310,47 @@ def rank_program(g, core, T, topo):
             return op("g", [o], [], lambda e: g.iota(o[0], pattern, base, cm), c)
         return op("g", [o], [], lambda e: g.iota(o[0], pattern, base, cm, allow_small_or_imprecise_dtypes=True), c)
 
-    def dma(q, outs, ins, out, in_, sem):
-        return op(q, outs, ins, lambda e: Q[q].dma_start(out, in_), 7.0 if sem == "l1" else 2.5, "dma", sem, 16)
+    def dma(q, outs, ins, out, in_, cost=2.5, after=()):
+        dmas.append("d%d" % len(dmas))
+        return op(q, outs, ins, lambda e: Q[e].dma_start(out, in_), cost, "dma", dmas[-1], 16, after)
 
-    def addr(r):
-        return topo.addr(T.cores[r])[:2]
+    def peer(s):
+        return (rank + s) % N
 
-    def send(r, dst, src, sem):
-        m = topo.mask(core, T.cores[r])
-        rid, pid = addr(r)
-        sends[sem] = op("g", [], [src], lambda: g.remote_dma(dst[0], src[0], T.sem[sem], T.sem["snd"], pid, rid, m), ISSUE + LAT, "rem")
-        sent[0] += len(topo.engines(core, T.cores[r]))
+    def send(s, dst, src, sem, cost):
+        m = topo.mask(core, T.cores[peer(s)])
+        rid, pid = topo.addr(T.cores[peer(s)])[:2]
+        sends[sem] = op("g", [], [src], lambda: g.remote_dma(dst[0], src[0], T.sem[sem], T.sem["snd"], pid, rid, m), cost, "rem")
+        sent[0] += len(topo.engines(core, T.cores[peer(s)]))
 
-    def width(r):
-        return len(topo.engines(T.cores[r], core))
+    def share(a, b, s):
+        en = topo.engines(a, b)
+        k = len(en) // 4
+        return en[(s - 1) * k:s * k] if s < N - 1 else en[2 * k:]
+
+    def send3(dst, src, sem, cost):
+        tr = []
+        for s in range(1, N):
+            en = share(core, T.cores[peer(s)], s)
+            rid, pid = topo.addr(T.cores[peer(s)])[:2]
+            tr.append(RemoteDMATransfer(dst_ids=[DstId(rid=rid, pnc=pid)], dma_engine_mask=sum(1 << e for e in en),
+                                        remote_sem=T.sem[sem + str(s)], srcs=[src(s)[0]], dsts=[dst(s)[0]]))
+            sent[0] += len(en)
+        k = op("g", [], [src(s) for s in range(1, N)], lambda: g.remote_dma_fused(tr, local_sem=T.sem["snd"]), cost, "rem")
+        for s in range(1, N):
+            sends[sem + str(s)] = k
+
+    def arrive3(x, sem, s):
+        arrive(x, sem + str(s), len(share(T.cores[peer(-s)], core, s)))
 
     def col(k):
         return B("COL", k, k + 1)
 
+    def isx(k):
+        return B("MSK", k, k + 1)
+
     def cls(n, c):
-        return B(n, 128 + 128 * c, 256 + 128 * c)
+        return B(n, BASE[c], BASE[c] + 128)
 
     def third(n, m):
         return B(n, 128 * m, 128 * m + 128)
@@ -344,355 +358,483 @@ def rank_program(g, core, T, topo):
     def eight(n, m):
         return B(n, 8 * m, 8 * m + 8)
 
-    dma("y", [B("RAWB")], [], T.RAWB[:], T.bun[:], "l0")
-    dma("y", [B("TAB", 0, 4096)], [], T.TAB[:, 0:4096], T.sight[:], "l1")
+    def seg(n, m):
+        return B(n, NV_ * m, NV_ * (m + 1))
+
+    def ahead(n, s, lo=0):
+        return B(n, lo + 128 - 32 * s, lo + 256 - 32 * s)
+
+    def rows(r):
+        return slice(32 * r, 32 * r + 32)
+
+    def slot(n, r):
+        return (T[n][r], n, r, r + 1)
+
+    dma("s", [(None, "DP", 0, N)], [], T.DP[:], T.pots[:])
+    dma("s", [slot("LP", rank)], [], T.LP[rank], T.pots[2 * rank:2 * rank + 2, :])
+    dma("s", [B("RAW0")], [], T.RAW0[:], T.bun[:], 6.5)
+    send3(lambda s: slot("LP", rank), lambda s: slot("DP", peer(s)), "p", 7.0)
+    order = []
+
+    def load(outs, ins, out, in_, cost):
+        order.append(dma("y", outs, ins, out, in_, cost, order[-1:]))
+
+    def table(s, cost):
+        x = slot("DT", peer(s))
+        load([x], [], x[0], T.sight[rows(peer(s)), :], cost)
+        send(s, slot("LT", rank), x, "t%d" % s, 5.5)
+
+    def land(s):
+        r = peer(-s)
+        arrive(slot("LT", r), "t%d" % s, len(topo.engines(T.cores[r], core)))
+        load([(None, "TAB", 1024 * r, 1024 * r + 1024)], [slot("LT", r)], T.TAB[rows(r), 0:4096], T.LT[r], 4.0)
+
+    table(1, 3.8)
+    table(2, 6.8)
+    load([B("TAB0", 0, 4096)], [], T.TAB0[:, 0:4096], T.sight[:], 12.5)
+    table(3, 14.0)
+    lead[0] = -500.0
+    for s in range(1, N):
+        for q in range(4):
+            op("v", [(None, "SU", 128 * s + 32 * q, 128 * s + 32 * q + 32)], [B("RAW0")],
+               lambda e, s=s, q=q: V.tensor_scalar(T.SU[rows(q), 128 * s:128 * s + 128], T.RAW0[rows(peer(s)), 128 * q:128 * q + 128],
+                                                   1.0, None, OP.add), 128 * CYC)
+    send3(lambda s: third("LB", s), lambda s: third("SU", s), "u", 7.0)
+    lead[0] = -1000.0
     fill(B("POTI"), 0)
-    dma("y", [B("POTI")], [], T.POTI[0:128:16, :], T.pots[:], "l2")
     fill(B("TAB", 4096, 4112), 0.0)
+    fill(B("TAB0", 4096, 4112), 0.0)
+    for s in range(1, N):
+        arrive3(slot("LP", peer(-s)), "p", s)
+    load([B("POTI")], [(None, "LP", 0, N)], T.POTI[0:128:16, :], T.LP[:], 6.0)
+    for s in range(1, N):
+        land(s)
 
     iota(B("II", 0, 1), [[1, 1]], 0, 1)
+    iota(B("FF"), [[1, 132]], 0, 0)
     iota(B("FX"), [[0, 8], [1, 16]], 0, 0)
     iota(B("FG"), [[1, 8], [0, 16]], 0, 0)
-    iota(B("AC"), [[8, 4], [32, 128]], 5, 0)
-    iota(B("WC"), [[37, 4], [148, 128]], 0, 0)
-    iota(B("FF"), [[1, 128]], 0, 0)
-    iota(B("RO8", 0, 3), [[-1, 3]], 15, 0)
-    iota(B("RO8", 8, 12), [[8, 4]], 5, 0)
-    iota(B("RO8", 12, 16), [[37, 4]], 0, 0)
-    iota(B("RO8", 16, 24), [[16, 8]], 0, 0)
-    iota(B("FY"), [[0, 8], [1, 16]], 1, 0)
-    for c in range(4):
-        z0, z1 = (2048 * (2 - m) + 128 + 128 * ((c + 1 + m) & 3) for m in range(2))
-        iota(B("ZC", 16 * c, 16 * c + 16), [[z1 - z0, 2], [0, 8]], z0, 0)
-    copy(col(0), B("II", 0, 1))
+    iota(B("SLOT"), [[0, 8], [1, SEG]], 0, 0)
+    iota(B("T19", 0, NV_), [[1, 8], [0, SEG]], 0, 0)
     ts(B("II", 1, 2), B("II", 0, 1), 15, OP.bitwise_and)
     ts(B("II", 2, 3), B("II", 0, 1), 4, OP.logical_shift_right)
-    copy(B("COL", 1, 3), B("II", 1, 3))
-    ts(B("BO"), B("FG"), col(2), OP.is_equal)
-    ts(col(12), col(1), -1.0, OP.mult, 15.0, OP.add)
-    ts(B("TMP"), B("FX"), col(12), OP.is_equal)
-    tt(B("REV"), B("BO"), B("TMP"), OP.mult)
-    for c in range(4):
-        copy(third("BF", c), (T.RAWB[:, c::4], "RAWB", 0, 512))
-        mm(third("b0", c), B("REV"), third("BF", c))
-        act(cls("WIN", c), third("b0", c), AF.Identity, 1.0, 1.0)
-    ts(B("WC"), B("WC"), 4095, OP.bitwise_and)
+    copy(B("COL", 0, 3), B("II", 0, 3))
     fill(B("RST"), 1.0)
-    op("v", [B("RST")], [], lambda e: V.memset(T.RST[:, 0:2048:16], 0.0), 128 * CYC)
-    ts(B("IDN"), B("FF"), col(0), OP.is_equal)
-    ts(B("MSK"), B("FX"), col(1), OP.is_equal)
-    ts(B("BLK"), B("FF", 0, 8), col(2), OP.is_equal)
-    copy(B("GS"), B("BLK"))
-    copy(B("EXL"), B("FF", 0, 8))
-    ts(col(3), col(1), 0.0, OP.is_equal)
+    fill(B("RST", 0, 16 * CH, 16), 0.0)
+    BO = B("BO", 0, 128)
+    ts(BO, B("FG"), col(2), OP.is_equal)
+    act(B("BO", 128, 256), BO)
+    ts(B("MSK"), B("FX", 0, 128), col(1), OP.is_equal)
+    ts(col(12), col(1), -1.0, OP.mult, 15.0, OP.add)
+    ts(B("TMP"), B("FX", 0, 128), col(12), OP.is_equal)
+    tt(B("REV"), BO, B("TMP"), OP.mult)
+    IDF, BLK = third("PI", 0), eight("GF", 0)
+    ts(IDF, B("FF", 0, 128), col(0), OP.is_equal)
+    act(third("PI", 1), IDF)
+    act(B("IDN"), IDF)
+    for h in range(2):
+        ts(eight("GF", h), B("FF", 0, 8), col(2), OP.is_equal)
+    act(B("GS"), B("GF"))
+    act(B("GB"), B("GF"), AF.Copy, 2.0)
+    act(B("G0"), BLK, AF.Copy, isx(0))
+    ts(B("EXL"), B("FF", 0, 8), float(SEG), OP.mult, SEG - 1.0, OP.add)
     ts(col(4), col(1), 0.0, OP.is_gt)
     ts(col(8), col(1), 13.0, OP.is_ge)
-    ts(col(9), col(1), -2.0, OP.mult, 18.0, OP.add)
-    ts(col(10), col(0), 768.0, OP.add, 1.0 / 4096, OP.mult)
-    ts(col(11), col(0), 3.0 * 2048 + 640 - 65536, OP.add, 1.0 / 4096, OP.mult)
-    ts(B("ZC"), B("ZC"), 1.0 / 4096, OP.mult)
-    ts(B("EC", 0, 3), B("RO8", 0, 3), col(1), OP.is_equal)
-    ts(B("EC", 3, 6), B("EC", 0, 3), 32.0, OP.mult)
-    ts(B("EC", 6, 9), B("EC", 0, 3), 148.0, OP.mult)
-    ts(B("EC", 9, 17), B("RO8", 8, 16), col(3), OP.mult)
-    ts(B("BIAS"), B("MSK"), 512.0, OP.mult, -512.0, OP.add)
-    for m in range(3):
-        scaled(third("SEL", m), B("BO"), B("EC", m, m + 1))
-        scaled(third("S32", m), B("BO"), B("EC", 3 + m, 4 + m))
-        scaled(third("S148", m), B("BO"), B("EC", 6 + m, 7 + m))
-        ts(eight("QS", m), B("GS"), B("EC", m, m + 1), OP.mult, 1.0 / 4096, OP.mult)
+    act(B("BIAS"), B("MSK"), AF.Identity, 512.0, -512.0)
+    for k in range(3):
+        fill(B("RW", k, 16, 3), float(k))
+    for k, pieces in ((1, ((0, 3, 8), (3, 6, 37), (6, 8, 128), (8, 16, 0))), (2, ((0, 3, 5), (3, 8, 0), (8, 10, 1), (10, 16, 0)))):
+        for lo, hi, v in pieces:
+            fill(B("RW", 16 * k + lo, 16 * k + hi), float(v))
+    for k in range(3):
+        x, y = B("RW", 16 * k, 16 * k + 16), col(17 + k)
+        tt(x, x, B("MSK", 0, 16), OP.mult)
+        op("v", [y], [x], lambda e, x=x, y=y: V.tensor_reduce(y[0], x[0], AX.X, OP.add), 64 * CYC)
+    ts(B("CAI"), B("FF", 0, 8), col(17), OP.add, 1.0, OP.add)
+    ts(B("CAI"), B("CAI"), 3, OP.bitwise_and)
+    ts(B("CA"), B("CAI"), col(18), OP.mult, col(19), OP.add)
+    ts(B("CAI"), B("CAI"), 1.0, OP.add)
+    ts(B("CAI"), B("CAI"), 1, OP.logical_shift_right)
+    ts(col(27), isx(6), isx(7), OP.add, 128.0, OP.mult)
+    ts(B("ZT", 0, 8), B("CAI"), col(27), OP.mult)
+    tt(B("CA"), B("CA"), B("ZT", 0, 8), OP.add)
     for c in range(4):
-        scaled(third("EQ", c), B("BO"), B("EC", 9 + c, 10 + c))
-        scaled(third("EW", c), B("BO"), B("EC", 13 + c, 14 + c))
-    ts(B("IL"), B("RO8", 16, 24), col(1), OP.add)
-    ts(B("CX"), B("IL"), 16.0, OP.mult, 4096.0 + 16.0, OP.add)
+        act(third("KC", c), B("FF", 0, 128), AF.Identity, col(8), B("CA", (c + 3) & 3, ((c + 3) & 3) + 1))
+    for m in range(3):
+        w = 256 if m == 2 else 128
+        ts(col(20 + m), isx(15 - m), -32.0, OP.mult, isx(m), OP.subtract)
+        ts(col(23 + m), isx(15 - m), 148.0, OP.mult, isx(3 + m), OP.add)
+        act(B("MA", 128 * m, 128 * m + w), B("BO", 0, w), AF.Copy, col(20 + m))
+        act(B("MW", 128 * m, 128 * m + w), B("BO", 0, w), AF.Copy, col(23 + m))
+        act(B("SEL", 128 * m, 128 * m + w), B("BO", 0, w), AF.Copy, isx(15 - m))
+    IL = eight("IL", 0)
+    ts(IL, B("FF", 0, 8), 16.0, OP.mult, col(1), OP.add)
+    act(eight("IL", 1), IL, AF.Identity, 1.0, 128.0)
+    act(eight("IL", 2), IL, AF.Identity, 1.0, 872.0)
+    act(eight("CX", 0), IL, AF.Identity, 16.0, 4096.0 + 15.0)
+    ts(col(7), col(0), 768.0, OP.add, UNIT, OP.mult)
+    act(B("NONE"), B("FF", 0, 8), AF.Identity, 0.0, col(7))
     fill(col(14), 63 * math.log(2.0))
     fill(col(15), 63 * math.log(2.0) + math.log(2.5))
-    act(B("W8"), B("IL"), AF.Exp, -math.log(2.0), col(14))
-    act(B("TH"), B("FF"), AF.Exp, -math.log(2.0), col(15))
+    fill(col(10), 67.5 * 16384)
+    act(B("W8"), IL, AF.Exp, -math.log(2.0), col(14))
+    k = act(col(16), col(0), AF.Exp, -math.log(2.0), col(15))
+    op("s", [col(9)], [col(1), col(10), B("W8"), col(16)], lambda e: S_.activation(col(9)[0], col(1)[0], AF.Silu, bias=col(10)[0], scale=-4.0 * 16384), 1.5)
     for c in range(8):
-        scaled(third("WT", c), B("BO"), B("W8", c, c + 1))
-    ts(B("NEGV"), B("BO"), col(3), OP.mult, -1.0, OP.mult)
-    ts(B("BIGN"), B("BO"), col(3), OP.mult, -16384.0, OP.mult)
-    ts(B("NSEL"), B("GS"), col(3), OP.mult, -64.0, OP.mult)
-    fill(B("VR", 0, 128), 0.0)
-    fill(B("VR", 640, 896), 0.0)
-    fill(B("WIN", 0, 128), 0.0)
-    ts(third("PL", 0), B("POTI"), 1.0, OP.add, col(3), OP.mult)
-    ts(B("TMP"), B("FX"), 0.0, OP.is_equal)
-    tt(B("PSEL"), B("BO"), B("TMP"), OP.mult)
-    ts(col(16), col(1), 1.0, OP.is_equal)
-    ts(B("POLD"), B("PSEL"), col(16), OP.mult)
-    ts(col(13), col(3), 16.0, OP.mult, col(1), OP.add)
-    ts(B("FY"), B("FY"), col(13), OP.is_equal)
-    tt(B("TMP"), B("FY"), B("MSK"), OP.subtract)
-    tt(B("DIF"), B("TMP"), B("BO"), OP.mult)
-    ts(B("TMP"), B("FX"), 0.0, OP.is_gt)
-    tt(B("DIF"), B("DIF"), B("TMP"), OP.mult)
+        act(B("WG", 16 * c, 16 * c + 16), B("GF"), AF.Copy, B("W8", c, c + 1))
+    t19 = seg("T19", 0)
+    ts(t19, t19, col(2), OP.is_equal)
+    for k in (0, SEG - 2, SEG - 1):
+        fill(B("T19", k, NV_, SEG), 0.0)
+    ts(col(11), isx(0), -2.0, OP.mult)
+    for h in range(2):
+        act(seg("NEGV", h), t19, AF.Copy, col(11))
+    fill(B("CD"), 2.0 * VOFF - 1.0)
+    for k, v in ((0, 1.0), (SEG - 2, -1.0), (SEG - 1, 0.0)):
+        fill(B("CD", k, NV_, SEG), v)
+    ts(col(26), isx(8), 64.0, OP.mult, isx(9), OP.add)
+    ts(col(26), col(26), 1024.0 * UNIT, OP.mult)
+    for m in range(2):
+        ts(col(27), isx(8), (2 - m) * 16.0, OP.mult, isx(9), OP.subtract)
+        ts(col(27), col(27), 1024.0, OP.mult, isx(15 - m), OP.add)
+        ts(col(27), col(27), isx(6 + m), OP.add, UNIT, OP.mult)
+        act(B("U19"), B("SLOT"), AF.Identity, col(26), col(27))
+        tt(seg("QX", m), B("U19"), t19, OP.mult)
+        act(B("QX", NV_ * m + SEG - 1, NV_ * (m + 1), SEG), BLK, AF.Copy, isx(8))
+    ts(col(27), col(0), 896.0 - 1024.0, OP.add, UNIT, OP.mult)
+    act(seg("CODE", 2), B("SLOT"), AF.Identity, (65536.0 + 1024.0) * UNIT, col(27))
+    fill(B("CODE", 2 * NV_, 3 * NV_, SEG), 0.0)
+    fill(B("CODE", 2 * NV_ + SEG - 1, 3 * NV_, SEG), 1.0)
+    for x in (B("WIN", 128, 256), B("WIN", 512, 640), B("VR", 128, 256), B("VR", 512, 640), B("VR", 768, 896), B("VR", 896, 1024)):
+        act(x, B("FX"))
+    ts(col(5), isx(0), -1.0, OP.mult)
+    act(B("PSELA"), ahead("BO", 1), AF.Copy, 0.5)
+    ts(col(6), col(1), 2.0, OP.is_lt)
+    act(B("POLDA"), B("PSELA"), AF.Copy, col(6))
+    fill(B("PSEL"), 0.0)
+    act(B("PSEL", 0, 128, 16), B("PSELA", 0, 128, 16))
+    act(B("POLD"), B("PSEL"), AF.Copy, col(6))
+    ts(col(13), isx(0), 16.0, OP.mult, col(1), OP.add)
+    ts(B("TMP"), B("FX", 0, 128), 1.0, OP.add, col(13), OP.is_equal)
+    tt(B("TMP"), B("TMP"), B("MSK"), OP.subtract)
+    tt(B("DIF"), B("TMP"), BO, OP.mult)
+    fill(B("DIF", 0, 128, 16), 0.0)
+    ts(B("II", 3, 4), B("II", 2, 3), 1, OP.bitwise_and)
+    ts(B("II", 4, 5), B("II", 2, 3), 1, OP.logical_shift_right)
+    copy(B("COL", 28, 30), B("II", 3, 5))
+    ts(col(28), col(28), 16.0, OP.mult, col(12), OP.add)
+    ts(col(28), col(28), 4.0, OP.mult, 3.0, OP.add)
+    ts(B("U19", 0, 132), B("FF", 0, 132), col(28), OP.is_equal)
+    ts(B("ZT", 8, 12), B("FF", 0, 4), col(29), OP.is_equal, -1.0, OP.mult)
+    for r in range(N):
+        ts(B("HOME", 132 * r, 132 * r + 132), B("U19", 0, 132), B("ZT", 8 + r, 9 + r), OP.mult)
+    fill(B("C64"), VOFF)
+    copy(eight("ZI", 0), B("FF", 0, 8))
+    ts(eight("ZI", 1), eight("ZI", 0), 1, OP.logical_shift_right)
+    tt(eight("ZT", 2), eight("ZI", 0), eight("ZI", 1), OP.add)
+    tt(eight("ZT", 3), eight("ZT", 2), eight("ZI", 1), OP.add)
+    copy(eight("EXV", 0), eight("ZT", 3))
+    tt(eight("ZT", 3), eight("ZT", 3), eight("ZI", 0), OP.add)
+    tt(eight("ZT", 3), eight("ZT", 3), eight("ZI", 0), OP.add)
+    for c in range(1, 4):
+        ts(eight("EXV", c), eight("ZT", 3), c - 1.0, OP.add)
 
     FLAG = (1 << 19) | 4095
 
-    def index(tag, s, a, w):
-        xi, xj, off = B("XI" + tag), B("XJ" + tag), B("OFF" + tag)
-        tt(xi, s, a, OP.mult)
-        ts(xj, xi, 5, OP.arith_shift_right, FLAG, OP.bitwise_and)
-        tt(xi, xj, w, OP.add)
-        ts(xj, xi, FLAG, OP.bitwise_and)
-        ts(off, xj, 4096.0, OP.min)
+    def part(x, lo, hi):
+        return B(x[1], x[2] + lo, x[2] + hi)
+
+    def index(tag, s, a, w, halves=1):
+        n = 128 // halves
+        for lo in range(0, 128, n):
+            xi, xj = B("XI" + tag, lo, lo + n), B("XJ" + tag, lo, lo + n)
+            tt(xi, part(s, lo, lo + n), part(a, lo, lo + n), OP.mult)
+            ts(xj, xi, 5, OP.arith_shift_right, FLAG, OP.bitwise_and)
+            tt(xi, xj, part(w, lo, lo + n), OP.add)
+            ts(xj, xi, FLAG, OP.bitwise_and)
+            ts(B("OFF" + tag, lo, lo + n), xj, 4096.0, OP.min)
 
     TABW = B("TAB", 0, 4097)
 
-    def look(tag, xn, base):
-        w = 128 // CHS[tag]
-        for a in range(0, 128, w):
-            x = B(xn, base + 16 * a, base + 16 * (a + w))
-            gat("sv", x, TABW, B("OFF" + tag, a, a + w))
-            scan(x, B("RST", 0, 16 * w), x, OP.mult, OP.max)
+    def looks(tag):
+        return B("XS") if tag == "S" else B("X", 2048 * int(tag), 2048 * int(tag) + 2048)
 
-    def selfsum(xn, base, c, bank):
-        o = B(bank, 128, 256)
-        mm(o, B("BO"), (T[xn][:, base + 15:base + 2048:16], xn, base, base + 2048))
-        act(cls("VR", c), o)
+    def place(tag, k):
+        x = looks(tag)
+        return B(x[1], x[2] + k, x[3], 16)
 
-    for c, (tag, xn, base) in enumerate((("S", "XS", 0), ("0", "X01", 0), ("1", "X01", 2048), ("2", "X2", 0))):
-        index(tag, third("b0", c), third("AC", c), third("WC", c))
-        look(tag, xn, base)
-        selfsum(xn, base, c, "b%d" % (4 + c))
+    def turn(t, name):
+        lead[0] = 100.0 * t + TURNS.index(name)
 
-    def partner(r, t):
-        return (r + 1 + t % 3) % N
+    def look(t, tag, pieces, name=None, tab=TABW):
+        a = 0
+        for eng, n in pieces:
+            x = part(looks(tag), 16 * a, 16 * (a + n))
+            turn(t, ("gather" if eng == "s" else "help") + (name or tag))
+            gat(eng, x, tab, B("OFF" + tag, a, a + n))
+            turn(t, "scan" + (name or tag))
+            scan(x, B("RST", 0, 16 * n), x, OP.mult, OP.max)
+            a += n
 
-    def asker(t):
-        return (rank - 1 - t % 3) % N
+    def own_marks(c, bank):
+        mm(third(bank, 2), third("MA", 0), third("KC", c))
+        mm(third(bank, 3), third("MW", 0), third("KC", c))
+
+    fill(B("VA"), 0.0)
+    fill(B("VB"), 0.0)
+    for c, tag in enumerate("S012"):
+        bank = "b%d" % (3 + c)
+        turn(-3 + (c > 0), "index" + tag if c else "names")
+        ts(third("BF", c), B("RAW0", c, 512, 4), -1.0, OP.mult)
+        own_marks(c, bank)
+        index(tag, third("BF", c), third(bank, 2), third(bank, 3))
+        look(-3 + (c > 0), tag, FIRST[c], tag, B("TAB0", 0, 4097))
+        mm(B(bank, 0, 8), place(tag, 15), eight("GS", 0))
+        ts(B("VB", c - 1, 24, 3) if c else B("VA", 0, 8), B(bank, 0, 8), VOFF, OP.add)
+        if c in (0, 3):
+            n, w, k = ("VA", 2, 4) if c == 0 else ("VB", 6, 8)
+            send3(lambda s: B("L" + n, k * rank, k * rank + k), lambda s: B(n, w * peer(s), w * peer(s) + k), n, 8.0 if c == 0 else 4.5)
+            copy(B("L" + n, k * rank, k * rank + k), B(n, w * rank, w * rank + k))
+            for s in range(1, N):
+                arrive3(B("L" + n, k * peer(-s), k * peer(-s) + k), n, s)
+    turn(-2, "end")
+    for q in range(4):
+        op("v", [(None, "TAB", 1024 * rank + 256 * q, 1024 * rank + 256 * q + 256)], [B("TAB0")],
+           lambda e, q=q: V.tensor_copy(T.TAB[rows(rank), 1024 * q:1024 * q + 1024], T.TAB0[rows(rank), 1024 * q:1024 * q + 1024]), 512 * CYC)
+    op("v", [(None, "BN", 128 * rank, 128 * rank + 128)], [B("RAW0")],
+       lambda e: V.tensor_scalar(T.BN[rows(rank), :], T.RAW0[rows(rank), :], -1.0, None, OP.mult), 512 * CYC)
+    for s in range(1, N):
+        r = peer(-s)
+        arrive3(third("LB", s), "u", s)
+        for q in range(4):
+            op("v", [(None, "BN", 128 * r + 32 * q, 128 * r + 32 * q + 32)], [third("LB", s)],
+               lambda e, s=s, r=r, q=q: V.tensor_scalar(T.BN[rows(r), 128 * q:128 * q + 128], T.LB[rows(q), 128 * s:128 * s + 128],
+                                                        -1.0, 1.0, OP.mult, OP.add), 128 * CYC)
+    for c in range(4):
+        bank = "b%d" % (3 + c)
+        turn(0 if c else -1, "pool")
+        mm(third(bank, 0), B("REV"), (T.BN[:, c:512:4], "BN", 0, 512))
+        act(cls("WIN", c), third(bank, 0))
+        turn(0 if c else -1, ("names", "value0", "value1", "value2")[c])
+        gat("s", third("VJ", c % 3), B("LVB" if c else "LVA"), eight("EXV", c))
+        mm(third("b7", 1 + c % 3), third("VJ", c % 3), IDF)
+        act(cls("VR", c), third("b7", 1 + c % 3))
+    turn(-1, "end")
+    ts(B("PL0"), B("POTI"), col(5), OP.mult)
+
+    def shift(o, x, s, via):
+        mm(via, ahead("PI", s), x)
+        act(o, via)
 
     def kpart(t):
         c = t & 3
-        tt(B("KS"), cls("WIN", c), cls("VR", c), OP.add)
-        ts(B("KT"), B("KS"), 13.0 * t - 1.0, OP.add)
+        tt(B("KS"), cls("VR", c), cls("WIN", c), OP.subtract)
+        ts(B("KT"), B("KS"), 13.0 * t - VOFF, OP.add)
         ts(B("KI"), B("KT"), 127, OP.bitwise_and)
-        ts(third("SM", 2 * t + 1), B("KI"), col(8), OP.mult, col(3), OP.add)
-        act(B("KB"), third("SM", 2 * t + 1))
+        ts(B("KB"), B("KI"), col(8), OP.mult, B("CA", t, t + 1), OP.add)
 
-    def marks(t, ms, kb):
-        for m in ms:
-            cm = (t + 1 + m) & 3
-            mm(third("b0", m), third("S32", m), kb, True, False)
-            mm(third("b0", m), third("EQ", cm), kb, False, True)
-            mm(third("b1", m), third("S148", m), kb, True, False)
-            mm(third("b1", m), third("EW", cm), kb, False, True)
+    def of(n, m, s):
+        return third(n, m) if m < 2 else ahead(n, s, 256)
 
-    def spread(t, kb):
+    def spread(t, s):
+        kb = B("KB")
         for m in range(3):
-            mm(third("b2", m), third("SEL", m), kb)
-        mm(B("b3", 0, 384), kb, B("SEL"), True, False)
+            turn(t, "index%d" % m)
+            mm(third("b%d" % m, 0), of("MA", m, s), kb)
+            mm(third("b%d" % m, 1), of("MW", m, s), kb)
+        turn(t, "lists")
         for m in range(3):
-            mm(third("b3", m), B("IDN"), B("BIAS"), False, m == 2)
+            mm(third("b3", m), B("IDN"), B("BIAS"), True, False)
+            mm(third("b3", m), kb, of("SEL", m, s), False, True)
         act(B("KM"), B("b3", 0, 384), AF.Relu)
-        act(B("KRB", 0, 256), B("b2", 0, 256))
-        act(B("KRB", 256, 384), B("b2", 256, 384))
         for m in range(3):
-            mm(B("b3", 384 + m * 8, 392 + m * 8), third("KM", m), B("GS"))
-        mm(B("b3", 416, 432), kb, B("QS", 0, 16))
-        copy(B("LF"), B("b3", 384, 408))
-        ts(eight("LS", t), eight("LF", 2), 128.0 + 128 * ((t + 3) & 3), OP.add)
-        for m in range(2):
-            ts(eight("VL", m), eight("LF", m), 128.0 + 128 * ((t + 1 + m) & 3), OP.add)
-        tt(B("ZB"), B("b3", 416, 432), B("ZC", 16 * (t & 3), 16 * (t & 3) + 16), OP.add)
-
-    def firsts():
-        for c in range(8):
-            for m in range(3):
-                o = c * 384 + m * 128
-                ts(B("EB", o, o + 128), third("KRB", m), B("LF", m * 8 + c, m * 8 + c + 1), OP.is_equal)
-            mm(B("b7", 0, 384), third("WT", c), B("EB", c * 384, c * 384 + 384), c == 0, c == 7)
+            mm(B("b3", 384 + m * 8, 392 + m * 8), third("KM", m), eight("GS", 0))
+        act(B("LF"), B("b3", 384, 408))
+        copy(B("VL"), B("LF"))
         for m in range(3):
-            tt(third("NF", m), third("b7", m), B("TH"), OP.is_gt)
+            bank = "b%d" % (4 + m)
+            turn(t, "rows%d" % m)
+            mm(third(bank, 3), of("SEL", m, s), kb)
+            if m < 2:
+                mm(B(bank, 160, 160 + NV_), kb, seg("QX", m))
+                act(seg("CODE", m), B(bank, 160, 160 + NV_))
+            act(third("KRB", m), third(bank, 3))
 
-    def vj(m):
-        gat("sv", third("VJ", m), B("VR", 0, 640), eight("VL", m))
+    def firsts(t, s):
+        for m in range(3):
+            turn(t, "first%d" % m)
+            sh = 2 * s if m == 2 else 0
+            for c in range(8):
+                x = third("EB", 8 * m + c)
+                ts(x, third("KRB", m), B("LF", m * 8 + c, m * 8 + c + 1), OP.is_equal)
+                mm(eight("b7", m), x, B("WG", 16 * c + sh, 16 * c + sh + 8), c == 0, c == 7)
+            act(B("CODE", NV_ * m + SEG - 2, NV_ * (m + 1), SEG), eight("b7", m), AF.Sign, -1.0, col(16))
 
-    def verdict(m, xn, base):
+    def verdict(t, m, best):
         bank = "b%d" % (4 + m)
-        o = B(bank, 0, 128)
-        mm(o, third("VJ", m), B("NEGV"), True, False)
-        if m < 2:
-            mm(o, third("NF", m), B("BIGN"), False, False)
-        for x in range(16):
-            mm((T[bank][:, x:128:16], bank, 0, 128), (T[xn][:, base + x:base + 2048:16], xn, base, base + 2048), B("GS"), False, x == 15)
-        act(third("CM", m), o, AF.Sign, 1.0, -0.5)
-        scan(third("CN", m), B("RST", 0, 128), third("CM", m), OP.mult, OP.add)
-        return (T.CN[:, m * 128 + 15:m * 128 + 128:16], "CN", m * 128, m * 128 + 128)
+        sh = 2 * (1 + t % 3) if m == 2 else 0
+        turn(t, "value%d" % m)
+        gat("s", third("VJ", m), cls("VR", (t + 1 + m) & 3), eight("VL", m))
+        o = B(bank, 0, NV_)
+        mm(o, B("IDN"), B("CD"), True, False)
+        mm(o, third("VJ", m), B("NEGV", SEG * sh, SEG * sh + NV_), False, False)
+        turn(t, "verdict%d" % m)
+        x = looks(str(m))
+        for lo, hi in TILES[m]:
+            if hi == 128:
+                mm(B(bank, SEG - 1, NV_, SEG), IDF, best, False, False)
+            for k in range(16):
+                out = (T[bank][lo:hi, 16 - k:NV_:SEG], bank, 0, NV_)
+                mm(out, B(x[1], x[2] + 16 * lo + k, x[2] + 16 * hi, 16), B("GB", sh, sh + 8), False, k == 15 and hi == 128)
+        scan(seg("ZS", m), o, seg("CODE", m), OP.max, OP.min)
+        return B("ZS", NV_ * m + SEG - 1, NV_ * (m + 1), SEG)
 
     def late(t):
-        o = t * 144
-        x2 = (t & 1) * 2048
-        arrive("WL", o, o + 144, "w%d" % t, width(asker(t)))
-        ts(B("LXb"), B("WL", o + 136, o + 144), -4096.0, OP.add, 2047.0, OP.min)
-        tt(B("D3"), B("WL", o + 128, o + 136), eight("LQ", t), OP.min)
-        copy(B("LST2"), B("D3"))
-        gat("sv", B("NXb"), B("X2", x2, x2 + 2048), B("LXb"))
-        mm(B("b6", 384, 512), B("BO"), B("NXb"))
-        act(B("NVb"), B("b6", 384, 512))
-        scamul(B("WIN", 0, 640), B("LST2"), third("S21", t & 1), B("WL", o, o + 128))
-        sca(B("VR", 0, 640), B("LST2"), B("NVb"))
-
-    def selflook(t):
-        c = t & 3
-        index("S", B("NU"), third("AC", c), third("WC", c))
-        look("S", "XS", 0)
-        selfsum("XS", 0, c, "b4")
+        s = 1 + t % 3
+        c = (t + 3) & 3
+        lo = BASE[c] - 128 * (c & 1)
+        odd = c & 1
+        ts(eight("ZT", 2), eight("ZI", 2), 896.0, OP.is_ge if odd else OP.is_lt, 1000.0, OP.mult)
+        mm(B("b5", 320, 328), ahead("PI", s), eight("ZT", 0))
+        mm(B("b5", 328, 336), B("IDN"), eight("LF", 2), True, False)
+        mm(B("b5", 328, 336), ahead("PI", s), eight("ZT", 2), False, True)
+        copy(B("LXb"), B("b5", 320, 328))
+        tt(eight("ZT", 3), B("b5", 328, 336), eight("IL", 1 + odd), OP.max if odd else OP.min)
+        ts(B("LST2"), eight("ZT", 3), -872.0 * odd, OP.add)
+        shift(B("KEEP2"), B("KEEP1"), s, third("b6", 3))
+        if t == RO - 1:
+            scamax(B("WIN", lo, lo + 256), B("LST2"), third("S2", t & 1), B("KEEP2"))
+            turn(t + 1, "lists2")
+        gat("s", B("NXb"), B("X"), B("LXb"))
+        mm(third("b5", 3), BO, B("NXb"))
+        act(B("NVb"), third("b5", 3), AF.Identity, 1.0, VOFF)
+        turn(t + 1, "late")
+        if t < RO - 1:
+            scamax(B("WIN", lo, lo + 256), B("LST2"), third("S2", t & 1), B("KEEP2"))
+        sca(B("VR", lo, lo + 256), B("LST2"), B("NVb"))
 
     for t in range(RO):
-        q = partner(rank, t)
-        ask = asker(t)
+        s = 1 + t % 3
         old = cls("WIN", t & 3)
-        S = B("WIN", 640, 768)
-        sm, smk = third("SM", 2 * t), third("SM", 2 * t + 1)
-        lm, lk = third("LM", 2 * t), third("LM", 2 * t + 1)
-        act(sm, old, AF.Identity, col(4), -1.0)
-        si = B("SI")
-        if t == 0:
-            si = third("CS", RO)
-            tt(si, sm, third("PL", 0), OP.add)
-            send(q, lm, si, "m0")
+        sm, si, s2 = B("SM"), B("WIN", 768, 896), third("S2", t & 1)
+        turn(t, "names")
         kpart(t)
-        if t == 0:
-            send(q, lk, smk, "k0")
-        else:
-            send(q, B("LM", t * 256, t * 256 + 256), B("SM", t * 256, t * 256 + 256), "m%d" % t)
-        spread(t, B("KB"))
-        send(q, eight("LQ", t), eight("LS", t), "f%d" % t)
-        marks(t, [0, 1], B("KB"))
-        mm(B("b5", 256, 384), B("DIF"), old)
-        vj(0)
-        firsts()
-        mm(B("b3", 432, 440), third("NF", 2), B("NSEL"))
+        act(sm, old, AF.Copy, col(4))
+        tt(si, sm, third("b1", 3) if t else B("PL0"), OP.add)
+        turn(t, "rows2")
+        shift(s2, si, s, third("b2", 2))
+        turn(t, "bundle2")
+        act(B("S1"), si)
+        spread(t, s)
+        for m in range(3):
+            turn(t, "index%d" % m)
+            index(str(m), si if m < 2 else s2, third("b%d" % m, 0), third("b%d" % m, 1), 2 if m == 0 else 1)
+            look(t, str(m), PIECES[m])
+        turn(t, "scanS")
+        own_marks(t & 3, "b0")
         if t:
-            selflook(t - 1)
-        wk = width(ask)
-        if t == 0:
-            arrive("LM", 0, 128, "m0", wk)
-            arrive("LM", 128, 256, "k0", wk)
-        else:
-            arrive("LM", t * 256, t * 256 + 256, "m%d" % t, wk)
-        act(B("KB2"), lk)
-        marks(t, [2], B("KB2"))
-        if t == 0:
-            S2 = lm
-        else:
-            pr = (ask - 1) % N
-            if pr == rank:
-                pq = third("PS", t - 1)
-            else:
-                arrive("PQ", t * 128, t * 128 + 128, "q%d" % t, width(pr) // 2)
-                pq = third("PQ", t)
-            S2 = B("S2")
-            tt(S2, lm, pq, OP.add)
-        x2 = (t & 1) * 2048
-        index("2", S2, third("b0", 2), third("b1", 2))
-        look("2", "X2", x2)
-        act(third("S21", t & 1), S2, AF.Identity, 1.0, 1.0)
-        if t:
-            solo = partner(rank, t) == (rank - 1) % N
-            arrive("PL", t * 128, t * 128 + 128, "p%d" % t, width((rank - 1) % N) // (1 if solo else 2))
-            tt(si, sm, third("PL", t), OP.add)
-        act(S, si, AF.Identity, 1.0, 1.0)
-        act(B("S1"), si, AF.Identity, 1.0, 1.0)
-        index("0", si, third("b0", 0), third("b1", 0))
-        look("0", "X01", 0)
-        arrive("LQ", t * 8, t * 8 + 8, "f%d" % t, wk)
-        copy(eight("VL", 2), eight("LQ", t))
-        vj(2)
-        cs = third("CS", t)
-        gat("sv", cs, B("WIN", 0, 640), eight("VL", 2))
-        send(ask, B("WIN", 768, 896), cs, "c%d" % t)
-        e2 = verdict(2, "X2", x2)
-        zs = eight("ZS", t)
-        ts(zs, e2, col(10), OP.add)
-        send(ask, eight("ZL", t), zs, "z%d" % t)
-        index("1", si, third("b0", 1), third("b1", 1))
-        look("1", "X01", 2048)
-        if t:
-            late(t - 1)
-        vj(1)
-        e0 = verdict(0, "X01", 0)
-        tt(eight("Z", 0), e0, eight("ZB", 0), OP.add)
-        e1 = verdict(1, "X01", 2048)
-        tt(eight("Z", 1), e1, eight("ZB", 1), OP.add)
-        tt(eight("Z", 2), eight("Z", 0), eight("Z", 1), OP.max)
-        ts(eight("Z", 3), eight("Z", 2), col(11), OP.max)
-        mm(B("b1", 384, 512), B("POLD"), old, True, False)
-        arrive("ZL", t * 8, t * 8 + 8, "z%d" % t, width(q))
-        zq, zx, zm = B("ZQ"), B("ZX"), B("ZM")
-        wo = t * 144
-        keep = B("WS", wo, wo + 128)
-        tt(B("ZN"), eight("ZL", t), B("b3", 432, 440), OP.add)
-        tt(zq, eight("Z", 3), B("ZN"), OP.max)
-        gat("s", zx, zq, B("EXL"))
-        op("v", [zm], [zq, B("EXL"), B("MSK")], lambda e: V.tensor_tensor(T.ZM[:], T.ZQ[:].indirect(T.EXL[:]), T.MSK[:], OP.mult),
+            mm(third("b1", 2), BO, place("S", 15))
+            act(cls("VR", (t - 1) & 3), third("b1", 2), AF.Identity, 1.0, VOFF)
+        firsts(t, s)
+        turn(t, "pool")
+        dif = B("b6", 160, 288)
+        mm(dif, B("DIF"), old)
+        last = t == RO - 1
+        mm(third("b1", 3), B("POLDA" if last else "POLD"), old, True, False)
+        turn(t, "bundle2")
+        gat("s", B("CS"), cls("WIN", (t + 3) & 3), eight("VL", 2))
+        shift(B("WIN", 896, 1024), B("CS"), N - s, third("b2", 2))
+        best = B("NONE")
+        for m in range(3):
+            best = verdict(t, m, best)
+        turn(t, "decide")
+        zq, zx, zm = seg("ZS", 2), B("ZX"), B("ZM")
+        op("s", [zx], [zq, B("EXL")], lambda e, zq=zq: S_.activation(T.ZX[:], zq[0].indirect(T.EXL[:]), AF.Copy, scale=1.0 / UNIT),
            0.06 + 128 * CYC * GAT)
-        mm(B("b2", 0, 128), zx, B("IDN"))
-        mm(B("b3", 440, 448), zm, B("BLK"))
-        ts(keep, B("b2", 0, 128), col(9), OP.is_lt)
-        ts(B("ZI", 0, 8), B("b3", 440, 448), 4096.0, OP.mult, 65536.0, OP.add)
-        tt(B("PP"), B("b5", 256, 384), keep, OP.mult)
-        mm(B("b1", 384, 512), B("PSEL"), B("PP"), False, True)
-        ps = third("PS", t)
-        act(ps, B("b1", 384, 512))
-        nx = (rank + 1) % N
-        z = partner(nx, t + 1)
-        pl = third("PL", t + 1)
-        if t == RO - 1 or z == rank:
-            send(nx, pl, ps, "p%d" % (t + 1))
-        else:
-            tr = []
-            for k, (dst, land, sm_) in enumerate(((nx, pl, "p"), (z, third("PQ", t + 1), "q"))):
-                en = topo.engines(core, T.cores[dst])
-                en = en[k * len(en) // 2:(k + 1) * len(en) // 2]
-                rid, pid = addr(dst)
-                tr.append(RemoteDMATransfer(dst_ids=[DstId(rid=rid, pnc=pid)], dma_engine_mask=sum(1 << e for e in en),
-                                            remote_sem=T.sem["%s%d" % (sm_, t + 1)], srcs=[ps[0]], dsts=[land[0]]))
-                sent[0] += len(en)
-            sends["p%d" % (t + 1)] = sends["q%d" % (t + 1)] = op(
-                "g", [], [ps], lambda tr=tr: g.remote_dma_fused(tr, local_sem=T.sem["snd"]), ISSUE + LAT, "rem")
-        ts(B("ZI", 32, 40), B("ZI", 0, 8), 1023, OP.bitwise_and)
-        copy(B("LST"), B("ZI", 32, 40))
-        ts(B("ZI", 8, 16), B("ZI", 0, 8), 13, OP.logical_shift_right)
-        ts(B("ZI", 16, 24), B("ZI", 0, 8), 6144, OP.bitwise_and)
-        tt(B("ZI", 8, 16), B("ZI", 8, 16), B("ZI", 16, 24), OP.add)
-        lx = B("WS", wo + 136, wo + 144)
-        tt(lx, B("CX"), B("ZI", 8, 16), OP.subtract)
-        ts(B("LX"), lx, 4095.0, OP.min)
-        gat("sv", B("NX"), B("X01"), B("LX"))
-        mm(B("b7", 384, 512), B("BO"), B("NX"))
-        act(B("NV"), B("b7", 384, 512))
-        ws = B("WS", wo + 128, wo + 136)
-        ts(ws, B("ZI", 32, 40), 768.0, OP.is_ge, 2000.0, OP.mult)
-        tt(ws, ws, B("IL"), OP.max)
-        send(q, B("WL", wo, wo + 144), B("WS", wo, wo + 144), "w%d" % t)
-        arrive("WIN", 768, 896, "c%d" % t, width(q))
+        op("v", [zm], [zq, B("EXL"), B("MSK")], lambda e, zq=zq: V.tensor_tensor(T.ZM[:], zq[0].indirect(T.EXL[:]), T.MSK[:], OP.mult),
+           0.06 + 128 * CYC * GAT)
+        mm(B("b3", 440, 448), zm, BLK)
+        mm(third("b2", 3), zx, B("IDN"))
+        ts(eight("ZI", 0), B("b3", 440, 448), 1.0 / UNIT, OP.mult)
+        ts(eight("ZI", 2), eight("ZI", 0), 1023, OP.bitwise_and)
+        ts(eight("ZI", 1), eight("ZI", 0), 10, OP.logical_shift_right, 15, OP.bitwise_and)
+        copy(B("LST"), eight("ZI", 2))
+        ts(eight("ZI", 3), eight("ZI", 0), 3, OP.logical_shift_right, 6144, OP.bitwise_and)
+        tt(eight("ZT", 0), eight("CX", 0), eight("ZI", 1), OP.subtract)
+        tt(eight("ZT", 1), eight("ZT", 0), eight("ZI", 3), OP.subtract)
+        copy(B("LX"), eight("ZT", 1))
         nu, w, ls = B("NU"), B("WIN"), B("LST")
-        op("sv", [nu], [w, ls], lambda e: V.tensor_scalar(T.NU[:], T.WIN[:].indirect(T.LST[:]), -1.0, None, OP.add) if e == "v"
-           else S_.activation(T.NU[:], T.WIN[:].indirect(T.LST[:]), AF.Identity, bias=-1.0), 0.06 + 128 * CYC * GAT)
-        scamul(w, ls, B("S1"), keep)
+        gat("s", nu, w, ls)
+        gat("s", B("NX"), B("X"), B("LX"))
+        mm(third("b4", 3), BO, B("NX"))
+        act(B("NV"), third("b4", 3), AF.Identity, 1.0, VOFF)
+        ts(B("KEEP1"), third("b2", 3), col(9), OP.subtract, 1.0, OP.min)
+        act(B("KEEP"), third("b2", 3), AF.Sign, -1.0, col(9))
+        turn(t, "indexS")
+        index("S", nu, third("b0", 2), third("b0", 3))
+        turn(t, "change")
+        scamax(w, ls, B("S1"), B("KEEP1"))
+        if last:
+            turn(RO, "late")
         sca(B("VR"), ls, B("NV"))
-        act(old, nu, AF.Identity, 1.0, 1.0)
+        turn(RO if last else t, "index0" if last else "change")
+        tt(B("PP"), dif, B("KEEP"), OP.mult)
+        mm(third("b1", 3), B("PSELA" if last else "PSEL"), B("PP"), False, True)
+        if not last:
+            turn(t + 1, "rows2")
+            act(old, nu)
+        look(t + 1, "S", LAST if last else PIECES[3])
+        turn(t + 1 - last, "indexS" if last else "lists2")
+        late(t)
+    turn(RO, "names")
 
-    late(RO - 1)
-    for k in range(4):
-        mm(third("b0", k), B("REV"), cls("WIN", k))
-        ts((T.OUTB[:, k::4], "OUTB", 0, 512), third("b0", k), -1.0, OP.add)
-    dma("y", [], [B("OUTB")], T.yb[:], T.OUTB[:], "o0")
-    selflook(RO - 1)
-    for k in range(4):
-        copy((T.OUTV[:, k::4], "OUTV", 0, 512), cls("VR", k))
-    dma("y", [], [B("OUTV")], T.yv[:], T.OUTV[0:128:16, :], "o1")
-    arrive("PL", RO * 128, RO * 128 + 128, "p%d" % RO, width((rank - 1) % N))
-    ts(B("OUTP"), third("PL", RO), -1.0, OP.add)
-    dma("y", [], [B("OUTP")], T.yp[:], T.OUTP[0:128:16, :], "o2")
+    def piece(n, s, lo=0, hi=160):
+        return B(n, 160 * s + lo, 160 * s + hi)
+
+    def tile(s, lo, hi, step=1):
+        return B(("b3", "b4", "b6", "b0")[s], lo, hi, step)
+
+    def home(s, k):
+        for q in range(4):
+            lo = 132 * peer(s) + 3 - q
+            mm(tile(s, 128, 160) if k == 4 else tile(s, k, 128, 4), B("HOME", lo, lo + 128),
+               B("WH", 128 * k + 32 * q, 128 * k + 32 * q + 32), q == 0, q == 3)
+
+    for k in (0, 1, 2, 3, 4):
+        ts(third("WH", k), third("b1", 3) if k == 4 else cls("WIN", k) if k else B("NU"), 2047.0, OP.add)
+        for s in range(1, N):
+            home(s, k)
+    for s in range(1, N):
+        ts(piece("OU", s), tile(s, 0, 160), 2048.0, OP.add)
+    send3(lambda s: piece("LO", s), lambda s: piece("OU", s), "w", 5.0)
+    turn(RO, "verdict2")
+    for c in range(1, 4):
+        mm(B("b2", c, 32, 4), cls("VR", c), B("G0"))
+    mm(B("b2", 0, 32, 4), B("IDN"), B("C64"), True, False)
+    mm(B("b2", 0, 32, 4), place("S", 15), eight("GS", 0), False, True)
+    ts(B("VI"), B("b2", 0, 32), -VOFF, OP.add)
+    copy(B("VT"), B("VI"))
+    turn(RO, "end")
+    for k in range(5):
+        home(0, k)
+    plus(piece("OUT", 0), tile(0, 0, 160), 2047.0)
+    turn(RO, "verdict2")
+    send3(lambda s: eight("LV", s - 1), lambda s: eight("VT", peer(s)), "v", 3.5)
+    for s in range(N):
+        r = peer(-s)
+        x = eight("LV", s - 1) if s else eight("VT", rank)
+        if s:
+            arrive3(piece("LO", s), "w", s)
+            ts(piece("OUT", s), piece("LO", s), -1.0, OP.add)
+            arrive3(x, "v", s)
+        dma("y", [], [piece("OUT", s)], T.yb[rows(r), :], piece("OUT", s, 0, 128)[0])
+        dma("s", [], [piece("OUT", s)], T.yp[2 * r:2 * r + 2, :], T.OUT[0:128:17, 160 * s + 128:160 * s + 160])
+        for h in range(2):
+            dma("ys"[h], [], [x], T.yv[2 * r + h, :], part(x, 4 * h, 4 * h + 4)[0])
     flush()
-    for k in ("o0", "o1", "o2"):
-        g.sync.wait_ge(T.sem[k], 16)
+    for k in dmas:
+        if known["y"].get(k, 0) < 16:
+            g.sync.wait_ge(T.sem[k], 16)
     for k in ("cv", "cs", "ct", "cg"):
         if cnt.get(k):
             g.wait_ge(T.sem[k], cnt[k])

@@ -4,16 +4,18 @@ from concourse.mybir import AluOpType as OP, ActivationFunctionType as AF, AxisL
 
 F, H, G, I, U = "float32", "bfloat16", "float16", "int32", "uint16"
 RO = 5
-CYC, PEC, WAKE, ISSUE, GAT, SCA, SLACK = 0.00083, 0.00083, 0.2, 1.2, 1.6, 3.8, 0.3
+CYC, PEC, WAKE, SELF, ISSUE, GAT, SCA, SLACK, SCAN = 0.00083, 0.0008, 0.15, 0.2, 1.2, 1.45, 3.8, (0.2, 0.8, 1.2), 1.0
+VFIX, CAP, PASSES = 0.02, 0.15, 0
 CH = 64
-PIECES = ((("s", 32), ("s", 32), ("s", 32), ("v", 32)), (("s", 32), ("s", 32), ("s", 32), ("v", 32)),
-          (("s", 32), ("s", 32), ("s", 32), ("s", 16), ("v", 16)),
-          (("s", 16), ("s", 32), ("s", 32), ("s", 48)))
-FIRST = ((("s", 48), ("v", 32), ("s", 48)), (("s", 64), ("s", 64)), (("s", 64), ("s", 64)), (("s", 64), ("v", 32), ("s", 32)))
-TILES = (((0, 128),), ((0, 128),), ((0, 128),))
-LAST = (("s", 32), ("s", 32), ("s", 32), ("v", 32))
-TURNS = ("names index0 lists lists2 index1 rows0 value0 rows1 rows2 gatherS helpS first0 late first1 pool gather0 index2 value1 first2 "
-         "scanS value2 bundle2 scan0 verdict0 gather1 help0 scan1 help1 verdict1 gather2 help2 scan2 verdict2 decide indexS change end").split()
+PIECES = ((("s", 64), ("v", 64)), (("s", 64), ("s", 64)), (("s", 56), ("s", 40), ("v", 16), ("s", 16)), (("s", 32), ("s", 48), ("s", 48)))
+FIRST = ((("v", 32), ("s", 48), ("s", 48)), (("s", 64), ("s", 64)), (("v", 40), ("s", 64), ("v", 24)),
+         (("v", 40), ("s", 24), ("s", 48), ("s", 16)))
+HALVES = (2, 1, 1, 2)
+TILES = ((0, 128),)
+ON = ("KM", "NXb", "WIN")
+LAST = (("s", 48), ("s", 40), ("s", 24), ("s", 16))
+TURNS = ("names index0 index1 lists rows2 lists2 rows0 index2 rows1 first1 gatherS helpS value0 late first0 first2 scanS gather0 value1 "
+         "pool value2 help0 scan0 gather1 help1 scan1 verdict0 verdict1 help2 scan2 gather2 bundle2 verdict2 decide indexS change end").split()
 SEG = 19
 NV_ = 8 * SEG
 UNIT = 2.0 ** -22
@@ -35,9 +37,12 @@ _sb("RAW0", 512, I)
 for _m, _w in (("VA", 16), ("LVA", 16), ("VB", 32), ("LVB", 32)):
     _sb(_m, _w, F)
 _sb("EXV", 32, U)
-_sb("SU", 512, U)
-_sb("LB", 512, U)
-_sb("BN", 512, F)
+_sb("SU", 512, G)
+_sb("LB", 512, G)
+_sb("BG", 512, G)
+_sb("REV", 256, F)
+_sb("RG", 256, G)
+_sb("CL", 8, H)
 _sb("POTI", 128, I)
 _sb("PL0", 128, F)
 _sb("BF", 512, F)
@@ -46,32 +51,26 @@ _sb("WIN", 1024, F)
 _sb("VR", 1024, F)
 BASE = (0, 256, 384, 640)
 _sb("NU", 128, F)
-for _m in ("0", "1", "2", "S"):
-    _sb("XI" + _m, 128, I)
-    _sb("XJ" + _m, 128, I)
-    _sb("OFF" + _m, 128, U)
-_sb("X", 6144, H)
-_sb("XS", 2048, H)
+_sb("XI", 512, I)
+_sb("XJ", 512, I)
+_sb("OFF", 512, U)
+_sb("X", 8192, H)
 _sb("RST", 16 * CH, H)
 _sb("S2", 256, F)
-for _m in ("SM", "S1", "CS", "KEEP", "KEEP1", "KEEP2", "NV", "NVb", "PP", "ZM", "TMP", "MSK", "REV", "DIF", "PSEL", "POLD",
-           "PSELA", "POLDA"):
+for _m in ("S1", "KEEP1", "KEEP2", "NV", "NVb", "PP", "ZM", "TMP", "MSK", "DIF", "PSEL", "POLD", "PSELA", "POLDA", "IXP", "KS"):
     _sb(_m, 128, F)
-_sb("KS", 128, F)
 _sb("KT", 128, I)
 _sb("KI", 128, I)
 _sb("KB", 128, H)
 _sb("KRB", 384, H)
 _sb("KM", 384, H)
 _sb("LF", 24, H)
-_sb("LQ", 8, F)
 _sb("VL", 24, U)
 _sb("VJ", 384, F)
 _sb("EB", 3072, H)
 _sb("CODE", 3 * NV_, F)
 _sb("ZS", 3 * NV_, F)
 _sb("ZX", 128, H)
-_sb("ZL", 8, F)
 _sb("ZI", 64, I)
 _sb("ZT", 32, F)
 for _m in ("LX", "LXb", "LST", "LST2", "EXL"):
@@ -83,8 +82,8 @@ _sb("HOME", 4 * 132, G)
 _sb("OU", 640, U)
 _sb("LO", 640, U)
 _sb("OUT", 640, F)
-_sb("VT", 32, F)
-_sb("LV", 24, F)
+_sb("VT", 32, G)
+_sb("LV", 32, G)
 _sb("II", 8, I)
 _sb("FF", 132, F)
 _sb("FX", 128, F)
@@ -106,7 +105,11 @@ _sb("WG", 128, H)
 _sb("BO", 256, H)
 _sb("PI", 256, F)
 _sb("IDN", 128, H)
-_sb("BIAS", 128, H)
+_sb("BIAS", 384, H)
+_sb("PH", 256, H)
+_sb("PG", 256, G)
+_sb("KEEP", 128, H)
+_sb("CS", 128, G)
 _sb("GF", 16, F)
 _sb("GS", 16, H)
 _sb("GB", 16, H)
@@ -161,7 +164,7 @@ def rank_program(g, core, T, topo):
                 if wr:
                     a[:] = [x for x in a if not (lo <= x[0] and x[1] <= hi)]
                 a.append((lo, hi, wr, eng, k))
-        ops.append({"eng": eng, "call": call, "cost": cost, "pre": pre, "kind": kind, "sem": sem, "inc": inc, "lead": lead[0]})
+        ops.append({"eng": eng, "call": call, "cost": cost + (VFIX if eng == "v" else 0.0), "pre": pre, "kind": kind, "sem": sem, "inc": inc, "lead": lead[0]})
         return k
 
     def learn(eng, tk):
@@ -184,7 +187,7 @@ def rank_program(g, core, T, topo):
 
     def flush():
         n = len(ops)
-        pre = [[(j, WAKE if w else 0.0) for j, w in o["pre"].items()] for o in ops]
+        pre = [[(j, (SELF if ops[j]["eng"] == o["eng"] else WAKE) if w else 0.0) for j, w in o["pre"].items()] for o in ops]
         succ = [[] for _ in ops]
         for k in range(n):
             for j, w in pre[k]:
@@ -195,22 +198,41 @@ def rank_program(g, core, T, topo):
         key = [o["lead"] for o in ops]
         for k in range(n - 1, -1, -1):
             key[k] = min([key[k]] + [key[j] for j, w in succ[k]])
-        left = [len(x) for x in pre]
-        ready = {k: 0.0 for k in range(n) if left[k] == 0}
-        free = {e: 0.0 for e in "vstgyr"}
-        at, on, seq = [0.0] * n, [""] * n, []
-        while ready:
-            t0, e = min((max(free[e], av), e) for k, av in ready.items() for e in ops[k]["eng"])
-            mine = sorted((key[k], k) for k in ready if e in ops[k]["eng"])
-            now = next(k for _, k in mine if ready[k] <= t0)
-            k = next(k for _, k in mine if ready[k] <= t0 + SLACK * hold[now])
-            at[k], on[k] = max(t0, ready.pop(k)), e
-            free[e] = at[k] + hold[k]
-            seq.append(k)
-            for j, _ in succ[k]:
-                left[j] -= 1
-                if left[j] == 0:
-                    ready[j] = max(at[i] + (cost[i] + w if w or ops[i]["kind"] != "dma" else hold[i]) for i, w in pre[j])
+        on = [o["eng"] for o in ops]
+
+        def gap(i, w):
+            return cost[i] + w if w or ops[i]["kind"] != "dma" else hold[i]
+
+        def plan(key, back):
+            before, after = (succ, pre) if back else (pre, succ)
+            left = [len(x) for x in before]
+            ready = {e: {} for e in "vstgyr"}
+            for k in range(n):
+                if left[k] == 0:
+                    ready[on[k]][k] = cost[k] - hold[k] if back else 0.0
+            free = {e: 0.0 for e in ready}
+            at, seq = [0.0] * n, []
+            while len(seq) < n:
+                t0, e = min((max(free[e], min(r.values())), e) for e, r in ready.items() if r)
+                mine = sorted(ready[e], key=lambda k: (key[k], -k if back else k))
+                now = next(k for k in mine if ready[e][k] <= t0)
+                k = next(k for k in mine if ready[e][k] <= t0 + min(CAP, SLACK["vst".find(e)] * hold[now]))
+                at[k] = max(t0, ready[e].pop(k))
+                free[e] = at[k] + hold[k]
+                seq.append(k)
+                for j, _ in after[k]:
+                    left[j] -= 1
+                    if left[j] == 0:
+                        ready[on[j]][j] = (max(at[i] + hold[i] + gap(j, w) - hold[j] for i, w in succ[j]) if back
+                                           else max(at[i] + gap(i, w) for i, w in pre[j]))
+            return max(at[k] + cost[k] for k in range(n)), seq, at
+
+        best = now = plan(key, False)
+        for _ in range(PASSES):
+            at = plan([-now[2][k] - hold[k] for k in range(n)], True)[2]
+            now = plan([-at[k] - hold[k] for k in range(n)], False)
+            best = min(best, now)
+        seq = best[1]
         tok = {}
         for k in seq:
             o = ops[k]
@@ -273,19 +295,30 @@ def rank_program(g, core, T, topo):
                   else S_.activation(o[0], x[0], AF.Copy, scale=c[0]), el(o))
 
     def plus(o, x, c):
-        return op("sv", [o], [x], lambda e: V.tensor_scalar(o[0], x[0], c, None, OP.add) if e == "v"
+        return op("s", [o], [x], lambda e: V.tensor_scalar(o[0], x[0], c, None, OP.add) if e == "v"
                   else S_.activation(o[0], x[0], AF.Identity, bias=c), el(o))
 
     def fill(o, c):
         return op("v", [o], [], lambda e: V.memset(o[0], c), el(o, o))
 
     def scan(o, d0, d1, f0, f1):
-        return op("v", [o], [d0, d1], lambda e: V.tensor_tensor_scan(o[0], d0[0], d1[0], 0.0, f0, f1), 2 * el(o, d0, d1))
+        return op("v", [o], [d0, d1], lambda e: V.tensor_tensor_scan(o[0], d0[0], d1[0], 0.0, f0, f1), SCAN * el(o, d0, d1))
 
     def act(o, i, func=AF.Copy, scale=1.0, bias=0.0):
         if isinstance(bias, float) and bias == 0.0:
             return op("s", [o], [i] + cols(scale), lambda e: S_.activation(o[0], i[0], func, scale=a_(scale)), el(o))
         return op("s", [o], [i] + cols(bias, scale), lambda e: S_.activation(o[0], i[0], func, bias=a_(bias), scale=a_(scale)), el(o))
+
+    def mov(name, o, i, scale=1.0, bias=0.0):
+        if name in ON:
+            return ts(o, i, scale, OP.mult, bias, OP.add)
+        return act(o, i, AF.Identity if bias else AF.Copy, scale, bias)
+
+    def twin(o, i):
+        return op("g", [o], [i], lambda e: g.affine_select(o[0], i[0], [[0, 128]], OP.is_ge, 0.0, 0, 0), 0.17 + 2 * el(o))
+
+    def eng(name):
+        return "v" if name in ON else "s"
 
     def mm(o, l, r, start=True, stop=True):
         n = max(min(64, l[0].shape[1]), r[0].shape[1])
@@ -298,8 +331,9 @@ def rank_program(g, core, T, topo):
         return op(eng, [o], [w, off], lambda e: V.tensor_copy(o[0], ind(w, off)) if e == "v"
                   else S_.activation(o[0], ind(w, off), AF.Copy), 0.06 + 16 * off[0].shape[1] * CYC * GAT)
 
-    def sca(w, off, i):
-        return op("s", [w], [i, off], lambda e: S_.activation(ind(w, off), i[0], AF.Silu), 0.06 + 128 * CYC * SCA)
+    def sca(en, w, off, i):
+        return op(en, [w], [i, off], lambda e: V.tensor_copy(ind(w, off), i[0]) if e == "v" else S_.activation(ind(w, off), i[0], AF.Silu),
+                  0.06 + 128 * CYC * SCA)
 
     def scamax(w, off, x, y):
         return op("v", [w], [x, y, off], lambda e: V.tensor_tensor(ind(w, off), x[0], y[0], OP.max), 0.06 + 128 * CYC * SCA)
@@ -393,14 +427,7 @@ def rank_program(g, core, T, topo):
     table(2, 6.8)
     load([B("TAB0", 0, 4096)], [], T.TAB0[:, 0:4096], T.sight[:], 12.5)
     table(3, 14.0)
-    lead[0] = -500.0
-    for s in range(1, N):
-        for q in range(4):
-            op("v", [(None, "SU", 128 * s + 32 * q, 128 * s + 32 * q + 32)], [B("RAW0")],
-               lambda e, s=s, q=q: V.tensor_scalar(T.SU[rows(q), 128 * s:128 * s + 128], T.RAW0[rows(peer(s)), 128 * q:128 * q + 128],
-                                                   1.0, None, OP.add), 128 * CYC)
-    send3(lambda s: third("LB", s), lambda s: third("SU", s), "u", 7.0)
-    lead[0] = -1000.0
+    load([(None, "TAB", 1024 * rank, 1024 * rank + 1024)], [], T.TAB[rows(rank), 0:4096], T.sight[rows(rank), :], 15.5)
     fill(B("POTI"), 0)
     fill(B("TAB", 4096, 4112), 0.0)
     fill(B("TAB0", 4096, 4112), 0.0)
@@ -427,7 +454,8 @@ def rank_program(g, core, T, topo):
     ts(B("MSK"), B("FX", 0, 128), col(1), OP.is_equal)
     ts(col(12), col(1), -1.0, OP.mult, 15.0, OP.add)
     ts(B("TMP"), B("FX", 0, 128), col(12), OP.is_equal)
-    tt(B("REV"), BO, B("TMP"), OP.mult)
+    tt(third("REV", 0), BO, B("TMP"), OP.mult)
+    act(third("REV", 1), third("REV", 0))
     IDF, BLK = third("PI", 0), eight("GF", 0)
     ts(IDF, B("FF", 0, 128), col(0), OP.is_equal)
     act(third("PI", 1), IDF)
@@ -440,7 +468,10 @@ def rank_program(g, core, T, topo):
     ts(B("EXL"), B("FF", 0, 8), float(SEG), OP.mult, SEG - 1.0, OP.add)
     ts(col(4), col(1), 0.0, OP.is_gt)
     ts(col(8), col(1), 13.0, OP.is_ge)
-    act(B("BIAS"), B("MSK"), AF.Identity, 512.0, -512.0)
+    for m in range(3):
+        act(third("BIAS", m), B("MSK"), AF.Identity, 512.0, -512.0)
+    act(B("PH"), B("PI"))
+    copy(B("PG"), B("PI"))
     for k in range(3):
         fill(B("RW", k, 16, 3), float(k))
     for k, pieces in ((1, ((0, 3, 8), (3, 6, 37), (6, 8, 128), (8, 16, 0))), (2, ((0, 3, 5), (3, 8, 0), (8, 10, 1), (10, 16, 0)))):
@@ -471,7 +502,12 @@ def rank_program(g, core, T, topo):
     ts(IL, B("FF", 0, 8), 16.0, OP.mult, col(1), OP.add)
     act(eight("IL", 1), IL, AF.Identity, 1.0, 128.0)
     act(eight("IL", 2), IL, AF.Identity, 1.0, 872.0)
-    act(eight("CX", 0), IL, AF.Identity, 16.0, 4096.0 + 15.0)
+    act(eight("CX", 0), IL, AF.Identity, 32.0, 47.0)
+    act(B("TMP", 0, 8), B("FF", 0, 8), AF.Identity, -256.0, 4096.0 - 32.0)
+    ts(col(3), col(1), -16.0, OP.mult)
+    act(B("CL"), B("TMP", 0, 8), AF.Identity, 1.0, col(3))
+    act(B("IXP"), IDF, AF.Copy, col(4))
+    copy(B("RG"), B("REV"))
     ts(col(7), col(0), 768.0, OP.add, UNIT, OP.mult)
     act(B("NONE"), B("FF", 0, 8), AF.Identity, 0.0, col(7))
     fill(col(14), 63 * math.log(2.0))
@@ -546,33 +582,33 @@ def rank_program(g, core, T, topo):
 
     def index(tag, s, a, w, halves=1):
         n = 128 // halves
+        k = len(a)
         for lo in range(0, 128, n):
-            xi, xj = B("XI" + tag, lo, lo + n), B("XJ" + tag, lo, lo + n)
-            tt(xi, part(s, lo, lo + n), part(a, lo, lo + n), OP.mult)
+            o = 128 * "012S".index(tag) + k * lo
+            xi, xj = B("XI", o, o + k * n), B("XJ", o, o + k * n)
+            for m in range(k):
+                tt(B("XI", o + m, o + k * n, k), s if halves == 1 else part(s, lo, lo + n), part(a[m], lo, lo + n), OP.mult)
             ts(xj, xi, 5, OP.arith_shift_right, FLAG, OP.bitwise_and)
-            tt(xi, xj, part(w, lo, lo + n), OP.add)
+            tt(xi, xj, part(w, k * lo, k * (lo + n)), OP.add)
             ts(xj, xi, FLAG, OP.bitwise_and)
-            ts(B("OFF" + tag, lo, lo + n), xj, 4096.0, OP.min)
+            ts(B("OFF", o, o + k * n), xj, 4096.0, OP.min)
 
     TABW = B("TAB", 0, 4097)
 
-    def looks(tag):
-        return B("XS") if tag == "S" else B("X", 2048 * int(tag), 2048 * int(tag) + 2048)
-
-    def place(tag, k):
-        x = looks(tag)
-        return B(x[1], x[2] + k, x[3], 16)
+    def place(tag, k, pair=False):
+        m = "012S".index(tag)
+        return B("X", 16 * m + k, 4096, 32) if pair else B("X", 2048 * m + k, 2048 * m + 2048, 16)
 
     def turn(t, name):
         lead[0] = 100.0 * t + TURNS.index(name)
 
-    def look(t, tag, pieces, name=None, tab=TABW):
-        a = 0
+    def look(t, tag, pieces, tab=TABW):
+        a = 128 * "012S".index(tag)
         for eng, n in pieces:
-            x = part(looks(tag), 16 * a, 16 * (a + n))
-            turn(t, ("gather" if eng == "s" else "help") + (name or tag))
-            gat(eng, x, tab, B("OFF" + tag, a, a + n))
-            turn(t, "scan" + (name or tag))
+            x = B("X", 16 * a, 16 * (a + n))
+            turn(t, ("gather" if eng == "s" else "help") + tag)
+            gat(eng, x, tab, B("OFF", a, a + n))
+            turn(t, "scan" + tag)
             scan(x, B("RST", 0, 16 * n), x, OP.mult, OP.max)
             a += n
 
@@ -582,13 +618,26 @@ def rank_program(g, core, T, topo):
 
     fill(B("VA"), 0.0)
     fill(B("VB"), 0.0)
+    turn(-4, "names")
+    ts(B("BF"), B("RAW0"), -1.0, OP.mult)
+
+    def some(x, r):
+        return (T[x[1]][rows(r), x[2]:x[3]],) + x[1:]
+
+    turn(-3, "end")
+    ts(B("BG"), B("RAW0"), -1.0, OP.mult, 2047.0, OP.add)
+    for s in (1, 2, 3, 0):
+        o = third(("b7", "b0", "b1", "b2")[s], 0)
+        for q in range(4):
+            mm(o, some(ahead("PG", (q - peer(s)) % N), peer(s)), some(third("BG", q), peer(s)), q == 0, q == 3)
+        copy(third("SU" if s else "LB", s), o)
+    send3(lambda s: third("LB", s), lambda s: third("SU", s), "u", 7.0)
     for c, tag in enumerate("S012"):
         bank = "b%d" % (3 + c)
         turn(-3 + (c > 0), "index" + tag if c else "names")
-        ts(third("BF", c), B("RAW0", c, 512, 4), -1.0, OP.mult)
         own_marks(c, bank)
-        index(tag, third("BF", c), third(bank, 2), third(bank, 3))
-        look(-3 + (c > 0), tag, FIRST[c], tag, B("TAB0", 0, 4097))
+        index(tag, B("BF", c, 512, 4), [third(bank, 2)], third(bank, 3))
+        look(-3 + (c > 0), tag, FIRST[c], B("TAB0", 0, 4097))
         mm(B(bank, 0, 8), place(tag, 15), eight("GS", 0))
         ts(B("VB", c - 1, 24, 3) if c else B("VA", 0, 8), B(bank, 0, 8), VOFF, OP.add)
         if c in (0, 3):
@@ -598,23 +647,16 @@ def rank_program(g, core, T, topo):
             for s in range(1, N):
                 arrive3(B("L" + n, k * peer(-s), k * peer(-s) + k), n, s)
     turn(-2, "end")
-    for q in range(4):
-        op("v", [(None, "TAB", 1024 * rank + 256 * q, 1024 * rank + 256 * q + 256)], [B("TAB0")],
-           lambda e, q=q: V.tensor_copy(T.TAB[rows(rank), 1024 * q:1024 * q + 1024], T.TAB0[rows(rank), 1024 * q:1024 * q + 1024]), 512 * CYC)
-    op("v", [(None, "BN", 128 * rank, 128 * rank + 128)], [B("RAW0")],
-       lambda e: V.tensor_scalar(T.BN[rows(rank), :], T.RAW0[rows(rank), :], -1.0, None, OP.mult), 512 * CYC)
     for s in range(1, N):
-        r = peer(-s)
         arrive3(third("LB", s), "u", s)
-        for q in range(4):
-            op("v", [(None, "BN", 128 * r + 32 * q, 128 * r + 32 * q + 32)], [third("LB", s)],
-               lambda e, s=s, r=r, q=q: V.tensor_scalar(T.BN[rows(r), 128 * q:128 * q + 128], T.LB[rows(q), 128 * s:128 * s + 128],
-                                                        -1.0, 1.0, OP.mult, OP.add), 128 * CYC)
+    for q in range(4):
+        for s in range(N):
+            k = mm(third("b2", q), some(ahead("RG", (peer(-s) - q) % N), q), some(third("LB", s), q), s == 0, s == N - 1)
+            if s == 0 and q:
+                ops[k]["pre"][k - 1] = True
     for c in range(4):
-        bank = "b%d" % (3 + c)
-        turn(0 if c else -1, "pool")
-        mm(third(bank, 0), B("REV"), (T.BN[:, c:512:4], "BN", 0, 512))
-        act(cls("WIN", c), third(bank, 0))
+        turn(-1, "pool")
+        mov("WIN", cls("WIN", c), B("b2", c, 512, 4), 1.0, -2047.0)
         turn(0 if c else -1, ("names", "value0", "value1", "value2")[c])
         gat("s", third("VJ", c % 3), B("LVB" if c else "LVA"), eight("EXV", c))
         mm(third("b7", 1 + c % 3), third("VJ", c % 3), IDF)
@@ -622,14 +664,14 @@ def rank_program(g, core, T, topo):
     turn(-1, "end")
     ts(B("PL0"), B("POTI"), col(5), OP.mult)
 
-    def shift(o, x, s, via):
-        mm(via, ahead("PI", s), x)
-        act(o, via)
+    def shift(name, o, x, s, via, scale=1.0, bias=0.0):
+        mm(via, ahead({F: "PI", H: "PH", G: "PG"}[SCRATCH[x[1]][2]], s), x)
+        mov(name, o, via, scale, bias)
 
     def kpart(t):
         c = t & 3
-        tt(B("KS"), cls("VR", c), cls("WIN", c), OP.subtract)
-        ts(B("KT"), B("KS"), 13.0 * t - VOFF, OP.add)
+        mov("KS", B("KS"), cls("WIN", c), -1.0, 13.0 * t - VOFF)
+        tt(B("KT"), B("KS"), cls("VR", c), OP.add)
         ts(B("KI"), B("KT"), 127, OP.bitwise_and)
         ts(B("KB"), B("KI"), col(8), OP.mult, B("CA", t, t + 1), OP.add)
 
@@ -638,27 +680,34 @@ def rank_program(g, core, T, topo):
 
     def spread(t, s):
         kb = B("KB")
-        for m in range(3):
-            turn(t, "index%d" % m)
-            mm(third("b%d" % m, 0), of("MA", m, s), kb)
-            mm(third("b%d" % m, 1), of("MW", m, s), kb)
+        turn(t, "index0")
+        for m in range(2):
+            mm(third("b0", m), of("MA", m, s), kb)
+        for m in range(2):
+            mm(B("b1", m, 256, 2), of("MW", m, s), kb)
+        turn(t, "index2")
+        mm(third("b2", 0), of("MA", 2, s), kb)
+        mm(third("b2", 1), of("MW", 2, s), kb)
         turn(t, "lists")
+        mm(B("b3", 0, 384), B("IDN"), B("BIAS"), True, False)
         for m in range(3):
-            mm(third("b3", m), B("IDN"), B("BIAS"), True, False)
-            mm(third("b3", m), kb, of("SEL", m, s), False, True)
-        act(B("KM"), B("b3", 0, 384), AF.Relu)
+            mm(third("b3", m), kb, of("SEL", m, s), False, m == 2)
+        if "KM" in ON:
+            ts(B("KM"), B("b3", 0, 384), 0.0, OP.max)
+        else:
+            act(B("KM"), B("b3", 0, 384), AF.Relu)
         for m in range(3):
             mm(B("b3", 384 + m * 8, 392 + m * 8), third("KM", m), eight("GS", 0))
-        act(B("LF"), B("b3", 384, 408))
-        copy(B("VL"), B("LF"))
+        mov("LF", B("LF"), B("b3", 384, 408))
+        copy(B("VL"), B("b3", 384, 408))
         for m in range(3):
             bank = "b%d" % (4 + m)
             turn(t, "rows%d" % m)
             mm(third(bank, 3), of("SEL", m, s), kb)
             if m < 2:
                 mm(B(bank, 160, 160 + NV_), kb, seg("QX", m))
-                act(seg("CODE", m), B(bank, 160, 160 + NV_))
-            act(third("KRB", m), third(bank, 3))
+                mov("CODE", seg("CODE", m), B(bank, 160, 160 + NV_))
+            mov("KRB", third("KRB", m), third(bank, 3))
 
     def firsts(t, s):
         for m in range(3):
@@ -668,24 +717,28 @@ def rank_program(g, core, T, topo):
                 x = third("EB", 8 * m + c)
                 ts(x, third("KRB", m), B("LF", m * 8 + c, m * 8 + c + 1), OP.is_equal)
                 mm(eight("b7", m), x, B("WG", 16 * c + sh, 16 * c + sh + 8), c == 0, c == 7)
-            act(B("CODE", NV_ * m + SEG - 2, NV_ * (m + 1), SEG), eight("b7", m), AF.Sign, -1.0, col(16))
+        act(B("CODE", SEG - 2, 3 * NV_, SEG), B("b7", 0, 24), AF.Sign, -1.0, col(16))
 
     def verdict(t, m, best):
         bank = "b%d" % (4 + m)
         sh = 2 * (1 + t % 3) if m == 2 else 0
         turn(t, "value%d" % m)
-        gat("s", third("VJ", m), cls("VR", (t + 1 + m) & 3), eight("VL", m))
+        gat(eng("VJ%d" % m), third("VJ", m), cls("VR", (t + 1 + m) & 3), eight("VL", m))
         o = B(bank, 0, NV_)
         mm(o, B("IDN"), B("CD"), True, False)
         mm(o, third("VJ", m), B("NEGV", SEG * sh, SEG * sh + NV_), False, False)
         turn(t, "verdict%d" % m)
-        x = looks(str(m))
-        for lo, hi in TILES[m]:
-            if hi == 128:
+        tiles = TILES if m == 2 else ((0, 128),)
+        for lo, hi in tiles:
+            if hi == 128 and m != 1:
                 mm(B(bank, SEG - 1, NV_, SEG), IDF, best, False, False)
             for k in range(16):
-                out = (T[bank][lo:hi, 16 - k:NV_:SEG], bank, 0, NV_)
-                mm(out, B(x[1], x[2] + 16 * lo + k, x[2] + 16 * hi, 16), B("GB", sh, sh + 8), False, k == 15 and hi == 128)
+                x = place(str(m), k, m < 2)
+                if m == 2:
+                    x = B("X", 4096 + 16 * lo + k, 4096 + 16 * hi, 16)
+                mm((T[bank][lo:hi, 16 - k:NV_:SEG], bank, 0, NV_), x, B("GB", sh, sh + 8), False, k == 15 and m != 1 and hi == 128)
+        if m == 1:
+            mm(B(bank, SEG - 1, NV_, SEG), IDF, best, False, True)
         scan(seg("ZS", m), o, seg("CODE", m), OP.max, OP.min)
         return B("ZS", NV_ * m + SEG - 1, NV_ * (m + 1), SEG)
 
@@ -695,46 +748,52 @@ def rank_program(g, core, T, topo):
         lo = BASE[c] - 128 * (c & 1)
         odd = c & 1
         ts(eight("ZT", 2), eight("ZI", 2), 896.0, OP.is_ge if odd else OP.is_lt, 1000.0, OP.mult)
-        mm(B("b5", 320, 328), ahead("PI", s), eight("ZT", 0))
+        mm(B("b5", 320, 328), B("IDN"), B("CL"), True, False)
+        mm(B("b5", 320, 328), ahead("PI", s), eight("ZT", 0), False, True)
         mm(B("b5", 328, 336), B("IDN"), eight("LF", 2), True, False)
         mm(B("b5", 328, 336), ahead("PI", s), eight("ZT", 2), False, True)
         copy(B("LXb"), B("b5", 320, 328))
         tt(eight("ZT", 3), B("b5", 328, 336), eight("IL", 1 + odd), OP.max if odd else OP.min)
         ts(B("LST2"), eight("ZT", 3), -872.0 * odd, OP.add)
-        shift(B("KEEP2"), B("KEEP1"), s, third("b6", 3))
+        shift("KEEP2", B("KEEP2"), B("KEEP"), s, third("b6", 3), -4096.5, -4095.5)
         if t == RO - 1:
             scamax(B("WIN", lo, lo + 256), B("LST2"), third("S2", t & 1), B("KEEP2"))
-            turn(t + 1, "lists2")
-        gat("s", B("NXb"), B("X"), B("LXb"))
+            turn(t, "change")
+        gat(eng("NXb") if t < RO - 1 else "s", B("NXb"), B("X", 0, 6144), B("LXb"))
         mm(third("b5", 3), BO, B("NXb"))
-        act(B("NVb"), third("b5", 3), AF.Identity, 1.0, VOFF)
-        turn(t + 1, "late")
+        mov("NVb" if t < RO - 1 else "", B("NVb"), third("b5", 3), 1.0, VOFF)
+        turn(t + (t < RO - 1), "late" if t < RO - 1 else "end")
         if t < RO - 1:
             scamax(B("WIN", lo, lo + 256), B("LST2"), third("S2", t & 1), B("KEEP2"))
-        sca(B("VR", lo, lo + 256), B("LST2"), B("NVb"))
+        sca(eng("SCA2"), B("VR", lo, lo + 256), B("LST2"), B("NVb"))
 
     for t in range(RO):
         s = 1 + t % 3
         old = cls("WIN", t & 3)
-        sm, si, s2 = B("SM"), B("WIN", 768, 896), third("S2", t & 1)
+        si, s2 = B("WIN", 768, 896), third("S2", t & 1)
         turn(t, "names")
+        if t == 0:
+            mm(third("b1", 3), IDF, B("PL0"), True, False)
+        mm(third("b1", 3), B("IXP"), old, False, True)
+        mov("SI", si, third("b1", 3))
         kpart(t)
-        act(sm, old, AF.Copy, col(4))
-        tt(si, sm, third("b1", 3) if t else B("PL0"), OP.add)
         turn(t, "rows2")
-        shift(s2, si, s, third("b2", 2))
+        shift("S2", s2, si, s, third("b2", 2))
         turn(t, "bundle2")
-        act(B("S1"), si)
+        twin(B("S1"), si)
         spread(t, s)
-        for m in range(3):
-            turn(t, "index%d" % m)
-            index(str(m), si if m < 2 else s2, third("b%d" % m, 0), third("b%d" % m, 1), 2 if m == 0 else 1)
-            look(t, str(m), PIECES[m])
+        turn(t, "index0")
+        index("0", si, [third("b0", 0), third("b0", 1)], B("b1", 0, 256), HALVES[0])
+        look(t, "0", PIECES[0])
+        look(t, "1", PIECES[1])
+        turn(t, "index2")
+        index("2", s2, [third("b2", 0)], third("b2", 1), HALVES[2])
+        look(t, "2", PIECES[2])
         turn(t, "scanS")
         own_marks(t & 3, "b0")
         if t:
             mm(third("b1", 2), BO, place("S", 15))
-            act(cls("VR", (t - 1) & 3), third("b1", 2), AF.Identity, 1.0, VOFF)
+            mov("VR", cls("VR", (t - 1) & 3), third("b1", 2), 1.0, VOFF)
         firsts(t, s)
         turn(t, "pool")
         dif = B("b6", 160, 288)
@@ -742,8 +801,9 @@ def rank_program(g, core, T, topo):
         last = t == RO - 1
         mm(third("b1", 3), B("POLDA" if last else "POLD"), old, True, False)
         turn(t, "bundle2")
-        gat("s", B("CS"), cls("WIN", (t + 3) & 3), eight("VL", 2))
-        shift(B("WIN", 896, 1024), B("CS"), N - s, third("b2", 2))
+        w2, l2 = cls("WIN", (t + 3) & 3), eight("VL", 2)
+        op("v", [B("CS")], [w2, l2], lambda e, w2=w2, l2=l2: V.tensor_scalar(T.CS[:], ind(w2, l2), 2047.0, None, OP.add), 0.06 + 128 * CYC * GAT)
+        shift("C2", B("WIN", 896, 1024), B("CS"), N - s, third("b2", 2), 1.0, -2047.0)
         best = B("NONE")
         for m in range(3):
             best = verdict(t, m, best)
@@ -757,34 +817,29 @@ def rank_program(g, core, T, topo):
         mm(third("b2", 3), zx, B("IDN"))
         ts(eight("ZI", 0), B("b3", 440, 448), 1.0 / UNIT, OP.mult)
         ts(eight("ZI", 2), eight("ZI", 0), 1023, OP.bitwise_and)
-        ts(eight("ZI", 1), eight("ZI", 0), 10, OP.logical_shift_right, 15, OP.bitwise_and)
+        ts(eight("ZI", 1), eight("ZI", 0), 10, OP.logical_shift_right, 63, OP.bitwise_and)
         copy(B("LST"), eight("ZI", 2))
-        ts(eight("ZI", 3), eight("ZI", 0), 3, OP.logical_shift_right, 6144, OP.bitwise_and)
         tt(eight("ZT", 0), eight("CX", 0), eight("ZI", 1), OP.subtract)
-        tt(eight("ZT", 1), eight("ZT", 0), eight("ZI", 3), OP.subtract)
-        copy(B("LX"), eight("ZT", 1))
+        copy(B("LX"), eight("ZT", 0))
         nu, w, ls = B("NU"), B("WIN"), B("LST")
-        gat("s", nu, w, ls)
-        gat("s", B("NX"), B("X"), B("LX"))
+        gat(eng("NU"), nu, w, ls)
+        gat(eng("NX"), B("NX"), B("X", 0, 6144), B("LX"))
         mm(third("b4", 3), BO, B("NX"))
-        act(B("NV"), third("b4", 3), AF.Identity, 1.0, VOFF)
+        mov("NV", B("NV"), third("b4", 3), 1.0, VOFF)
         ts(B("KEEP1"), third("b2", 3), col(9), OP.subtract, 1.0, OP.min)
         act(B("KEEP"), third("b2", 3), AF.Sign, -1.0, col(9))
         turn(t, "indexS")
-        index("S", nu, third("b0", 2), third("b0", 3))
+        index("S", nu, [third("b0", 2)], third("b0", 3), HALVES[3])
         turn(t, "change")
         scamax(w, ls, B("S1"), B("KEEP1"))
-        if last:
-            turn(RO, "late")
-        sca(B("VR"), ls, B("NV"))
-        turn(RO if last else t, "index0" if last else "change")
+        sca(eng("SCA"), B("VR"), ls, B("NV"))
         tt(B("PP"), dif, B("KEEP"), OP.mult)
-        mm(third("b1", 3), B("PSELA" if last else "PSEL"), B("PP"), False, True)
+        mm(third("b1", 3), B("PSELA" if last else "PSEL"), B("PP"), False, last)
         if not last:
             turn(t + 1, "rows2")
-            act(old, nu)
+            twin(old, nu)
         look(t + 1, "S", LAST if last else PIECES[3])
-        turn(t + 1 - last, "indexS" if last else "lists2")
+        turn(t + 1 - last, "change" if last else "lists2")
         late(t)
     turn(RO, "names")
 
@@ -792,19 +847,21 @@ def rank_program(g, core, T, topo):
         return B(n, 160 * s + lo, 160 * s + hi)
 
     def tile(s, lo, hi, step=1):
-        return B(("b3", "b4", "b6", "b0")[s], lo, hi, step)
+        return B(("b6", "b7", "b3", "b4")[s], lo, hi, step)
 
     def home(s, k):
         for q in range(4):
             lo = 132 * peer(s) + 3 - q
-            mm(tile(s, 128, 160) if k == 4 else tile(s, k, 128, 4), B("HOME", lo, lo + 128),
-               B("WH", 128 * k + 32 * q, 128 * k + 32 * q + 32), q == 0, q == 3)
+            mm(tile(s, 128, 160) if k else tile(s, 0, 128), B("HOME", lo, lo + 128),
+               B("WH", 512 + 32 * q, 544 + 32 * q) if k else third("WH", q), q == 0, q == 3)
 
-    for k in (0, 1, 2, 3, 4):
-        ts(third("WH", k), third("b1", 3) if k == 4 else cls("WIN", k) if k else B("NU"), 2047.0, OP.add)
-        for s in range(1, N):
-            home(s, k)
+    ts(third("WH", 4), third("b1", 3), 2047.0, OP.add)
     for s in range(1, N):
+        home(s, 1)
+    for c in range(4):
+        ts(B("WH", c, 512, 4), cls("WIN", c) if c else B("NU"), 2047.0, OP.add)
+    for s in range(1, N):
+        home(s, 0)
         ts(piece("OU", s), tile(s, 0, 160), 2048.0, OP.add)
     send3(lambda s: piece("LO", s), lambda s: piece("OU", s), "w", 5.0)
     turn(RO, "verdict2")
@@ -812,25 +869,27 @@ def rank_program(g, core, T, topo):
         mm(B("b2", c, 32, 4), cls("VR", c), B("G0"))
     mm(B("b2", 0, 32, 4), B("IDN"), B("C64"), True, False)
     mm(B("b2", 0, 32, 4), place("S", 15), eight("GS", 0), False, True)
-    ts(B("VI"), B("b2", 0, 32), -VOFF, OP.add)
+    ts(B("VI"), B("b2", 0, 32), -VOFF - 2040.0, OP.add)
     copy(B("VT"), B("VI"))
+    send3(lambda s: eight("LV", rank), lambda s: eight("VT", peer(s)), "v", 4.5)
+    copy(eight("LV", rank), eight("VI", rank))
     turn(RO, "end")
-    for k in range(5):
+    for k in range(2):
         home(0, k)
     plus(piece("OUT", 0), tile(0, 0, 160), 2047.0)
-    turn(RO, "verdict2")
-    send3(lambda s: eight("LV", s - 1), lambda s: eight("VT", peer(s)), "v", 3.5)
     for s in range(N):
         r = peer(-s)
-        x = eight("LV", s - 1) if s else eight("VT", rank)
         if s:
             arrive3(piece("LO", s), "w", s)
             ts(piece("OUT", s), piece("LO", s), -1.0, OP.add)
-            arrive3(x, "v", s)
+            arrive3(eight("LV", r), "v", s)
         dma("y", [], [piece("OUT", s)], T.yb[rows(r), :], piece("OUT", s, 0, 128)[0])
-        dma("s", [], [piece("OUT", s)], T.yp[2 * r:2 * r + 2, :], T.OUT[0:128:17, 160 * s + 128:160 * s + 160])
-        for h in range(2):
-            dma("ys"[h], [], [x], T.yv[2 * r + h, :], part(x, 4 * h, 4 * h + 4)[0])
+        dma("y", [], [piece("OUT", s)], T.yp[2 * r:2 * r + 2, :], T.OUT[0:128:17, 160 * s + 128:160 * s + 160])
+    turn(RO, "change")
+    for c in range(4):
+        mm((T.b1[0:8, c:512:4], "b1", 0, 512), B("LV", c, 32, 4), third("PG", 0))
+    op("s", [B("BF")], [B("b1")], lambda e: S_.activation(T.BF[0:8, :], T.b1[0:8, :], AF.Identity, bias=2040.0), 512 * CYC)
+    dma("s", [], [B("BF")], T.yv[:], T.BF[0:8, :])
     flush()
     for k in dmas:
         if known["y"].get(k, 0) < 16:

@@ -4,22 +4,28 @@ from concourse.mybir import AluOpType as OP, ActivationFunctionType as AF, AxisL
 
 F, H, G, I, U = "float32", "bfloat16", "float16", "int32", "uint16"
 RO = 5
-CYC, PEC, WAKE, SELF, ISSUE, GAT, SCA, SLACK, SCAN = 0.00083, 0.0008, 0.15, 0.2, 1.2, 1.45, 3.8, (0.2, 0.8, 1.2), 1.0
-VFIX, CAP, PASSES = 0.02, 0.15, 0
+CYC, PEC, WAKE, SELF, ISSUE, GAT, SCA, SLACK = 0.00083, 0.0008, 0.15, 0.2, 1.2, 1.45, 3.8, (0.2, 1.0, 1.4)
+VFIX, CAP, PROP, PASSES = 0.02, 0.2, "vstgyr", 1
+APART = True
+SOON = 2
+DUE = (7.0, 8.0, 9.0, 10.0, 12.0, 3.5, 5.0, 3.0, 5.0, 2.5, 7.0, 7.0, 4.5)
 CH = 64
-PIECES = ((("s", 64), ("v", 64)), (("s", 64), ("s", 64)), (("s", 56), ("s", 40), ("v", 16), ("s", 16)), (("s", 32), ("s", 48), ("s", 48)))
-FIRST = ((("v", 32), ("s", 48), ("s", 48)), (("s", 64), ("s", 64)), (("v", 40), ("s", 64), ("v", 24)),
-         (("v", 40), ("s", 24), ("s", 48), ("s", 16)))
-HALVES = (2, 1, 1, 2)
-TILES = ((0, 128),)
-ON = ("KM", "NXb", "WIN")
-LAST = (("s", 48), ("s", 40), ("s", 24), ("s", 16))
-TURNS = ("names index0 index1 lists rows2 lists2 rows0 index2 rows1 first1 gatherS helpS value0 late first0 first2 scanS gather0 value1 "
-         "pool value2 help0 scan0 gather1 help1 scan1 verdict0 verdict1 help2 scan2 gather2 bundle2 verdict2 decide indexS change end").split()
+PIECES = ((("s", 24), ("s", 40), ("s", 64)), (("v", 32), ("v", 32), ("s", 16), ("s", 48)), (("v", 32), ("s", 64), ("s", 16), ("s", 16)),
+          (("s", 16), ("s", 48), ("s", 64)))
+FIRST = ((("s", 56), ("v", 24), ("s", 48)), (("s", 64), ("s", 64)), (("s", 64), ("s", 64)), (("v", 40), ("s", 32), ("v", 56)))
+LAST = (("s", 48), ("v", 16), ("s", 40), ("s", 24))
+EARLY = ((("s", 64), ("s", 16), ("s", 48)), (("s", 32), ("s", 56), ("v", 40)), (("s", 48), ("v", 48), ("v", 16), ("s", 16)), ())
+HALVES = (1, 1, 1, 2)
+TILES = ((0, 96), (96, 128))
+ON = ("KM", "WIN", "CODE2", "VJ1")
+TURNS = ("names indexS help0 index0 lists index1 rows first0 code0 code1 code2 pool firsts bundle2 help1 gather0 scan2 back gather2 gatherS "
+         "first1 gather1 value1 verdict0 decide scanS help2 index2 change helpS scan1 value2 first2 scan0 verdict2 verdict1 value0 pass end").split()
 SEG = 19
 NV_ = 8 * SEG
-UNIT = 2.0 ** -22
-VOFF = 64.0
+UNIT = 2.0 ** -24
+TW = 4112
+EMPTY = 0x3FFFF
+LOW = 3948.0
 
 SCRATCH = {}
 
@@ -28,97 +34,90 @@ def _sb(name, w, d):
     SCRATCH[name] = ("sbuf", [128, w], d)
 
 
-_sb("TAB", 4112, H)
+_sb("TAB", 4 * TW, H)
 for _m, _w, _d in (("T", 1024, H), ("P", 2, I)):
     SCRATCH["D" + _m] = ("dram", [4, 128, _w], _d)
     SCRATCH["L" + _m] = ("dram", [4, 128, _w], _d)
-_sb("TAB0", 4112, H)
+_sb("TAB0", TW, H)
 _sb("RAW0", 512, I)
-for _m, _w in (("VA", 16), ("LVA", 16), ("VB", 32), ("LVB", 32)):
+for _m, _w in (("LVA", 16), ("ZH", 24), ("LZ", 96), ("VH", 384), ("VK", 512), ("OH", 128), ("SH", 128)):
     _sb(_m, _w, F)
+_sb("POTH", 128, I)
+_sb("EXI", 32, I)
 _sb("EXV", 32, U)
-_sb("SU", 512, G)
-_sb("LB", 512, G)
+UW = 136
+_sb("SU", 4 * UW, G)
+_sb("LB", 4 * UW, G)
 _sb("BG", 512, G)
 _sb("REV", 256, F)
 _sb("RG", 256, G)
-_sb("CL", 8, H)
 _sb("POTI", 128, I)
 _sb("PL0", 128, F)
 _sb("BF", 512, F)
 _sb("KC", 512, H)
-_sb("WIN", 1024, F)
-_sb("VR", 1024, F)
-BASE = (0, 256, 384, 640)
+_sb("WIN", 1152, F)
+_sb("VR", 1152, F)
 _sb("NU", 128, F)
 _sb("XI", 512, I)
 _sb("XJ", 512, I)
 _sb("OFF", 512, U)
 _sb("X", 8192, H)
 _sb("RST", 16 * CH, H)
-_sb("S2", 256, F)
-for _m in ("S1", "KEEP1", "KEEP2", "NV", "NVb", "PP", "ZM", "TMP", "MSK", "DIF", "PSEL", "POLD", "PSELA", "POLDA", "IXP", "KS"):
+for _m in ("S1", "KEEP1", "PP", "ZM", "ZX", "TMP", "MSK", "DIF", "PSEL", "POLD", "PSELA", "POLDA", "IXP", "KS", "IDU"):
     _sb(_m, 128, F)
-_sb("KT", 128, I)
-_sb("KI", 128, I)
+for _m in ("KT", "KI", "NI", "NJ"):
+    _sb(_m, 128, I)
 _sb("KB", 128, H)
 _sb("KRB", 384, H)
 _sb("KM", 384, H)
 _sb("LF", 24, H)
 _sb("VL", 24, U)
+_sb("FS", 24, H)
 _sb("VJ", 384, F)
 _sb("EB", 3072, H)
 _sb("CODE", 3 * NV_, F)
 _sb("ZS", 3 * NV_, F)
-_sb("ZX", 128, H)
-_sb("ZI", 64, I)
+_sb("ZI", 16, I)
 _sb("ZT", 32, F)
-for _m in ("LX", "LXb", "LST", "LST2", "EXL"):
+for _m in ("LST", "EXL"):
     _sb(_m, 8, U)
-_sb("NX", 128, H)
-_sb("NXb", 128, H)
-_sb("WH", 640, G)
+_sb("WA", 640, F)
+_sb("WH", 768, G)
 _sb("HOME", 4 * 132, G)
-_sb("OU", 640, U)
-_sb("LO", 640, U)
-_sb("OUT", 640, F)
-_sb("VT", 32, G)
-_sb("LV", 32, G)
+_sb("HV", 4 * 132, H)
+_sb("WV", 512, G)
+_sb("OU", 4 * 288, U)
+_sb("LO", 4 * 288, U)
+_sb("OUT", 4 * 288, F)
 _sb("II", 8, I)
 _sb("FF", 132, F)
 _sb("FX", 128, F)
 _sb("FG", 128, F)
 _sb("SLOT", NV_, F)
 _sb("T19", NV_, F)
-_sb("C64", 8, H)
-_sb("VI", 32, I)
-_sb("U19", NV_, F)
-_sb("NEGV", 2 * NV_, F)
-_sb("CD", NV_, H)
-_sb("QX", 2 * NV_, H)
+_sb("U19", 132, F)
+_sb("NEGV", NV_, F)
+_sb("CD", 6 * NV_, H)
+_sb("QX", 3 * NV_, H)
 _sb("COL", 32, F)
-_sb("RW", 48, F)
 _sb("CA", 8, F)
 _sb("CAI", 8, I)
 _sb("W8", 8, F)
-_sb("WG", 128, H)
+_sb("WG", 64, H)
 _sb("BO", 256, H)
 _sb("PI", 256, F)
 _sb("IDN", 128, H)
 _sb("BIAS", 384, H)
-_sb("PH", 256, H)
 _sb("PG", 256, G)
 _sb("KEEP", 128, H)
-_sb("CS", 128, G)
 _sb("GF", 16, F)
-_sb("GS", 16, H)
+_sb("GS", 8, H)
 _sb("GB", 16, H)
-_sb("G0", 8, F)
-_sb("SEL", 512, H)
-_sb("MA", 512, H)
-_sb("MW", 512, H)
-_sb("IL", 24, F)
-_sb("CX", 16, F)
+_sb("G0", 16, F)
+_sb("GU", 8, F)
+_sb("SEL", 384, H)
+_sb("MA", 384, H)
+_sb("IL", 8, F)
 _sb("NONE", 8, F)
 for _m in range(8):
     SCRATCH["b%d" % _m] = ("psum", [128, 512], F)
@@ -154,7 +153,7 @@ def rank_program(g, core, T, topo):
                 for (alo, ahi, aw, ae, j) in acc.get(n, []):
                     if psum(n) and ae == "t" and eng == "t":
                         pre.setdefault(j, False)
-                    elif (psum(n) and (ae != eng or len(eng) > 1)) or (alo < hi and lo < ahi and (aw or wr)):
+                    elif (psum(n) and ae != eng) or (alo < hi and lo < ahi and (aw or wr)):
                         pre[j] = True
         for wr, lst in ((False, ins), (True, outs)):
             for (_, n, lo, hi) in lst:
@@ -194,10 +193,10 @@ def rank_program(g, core, T, topo):
                 succ[j].append((k, w))
         cost = [o["cost"] for o in ops]
         hold = [{"arr": 0.0, "dma": 0.1, "rem": ISSUE}.get(o["kind"], o["cost"]) for o in ops]
-
         key = [o["lead"] for o in ops]
         for k in range(n - 1, -1, -1):
-            key[k] = min([key[k]] + [key[j] for j, w in succ[k]])
+            if ops[k]["eng"] in PROP or key[k] < 0:
+                key[k] = min([key[k]] + [key[j] for j, w in succ[k]])
         on = [o["eng"] for o in ops]
 
         def gap(i, w):
@@ -290,19 +289,11 @@ def rank_program(g, core, T, topo):
             return op("v", [o], [x] + cols(s1), lambda e: V.tensor_scalar(o[0], x[0], a_(s1), None, f1), el(o, x))
         return op("v", [o], [x] + cols(s1, s2), lambda e: V.tensor_scalar(o[0], x[0], a_(s1), a_(s2), f1, f2), el(o, x))
 
-    def scaled(o, x, c):
-        return op("vs", [o], [x, c], lambda e: V.tensor_scalar(o[0], x[0], c[0], None, OP.mult) if e == "v"
-                  else S_.activation(o[0], x[0], AF.Copy, scale=c[0]), el(o))
-
-    def plus(o, x, c):
-        return op("s", [o], [x], lambda e: V.tensor_scalar(o[0], x[0], c, None, OP.add) if e == "v"
-                  else S_.activation(o[0], x[0], AF.Identity, bias=c), el(o))
-
     def fill(o, c):
         return op("v", [o], [], lambda e: V.memset(o[0], c), el(o, o))
 
     def scan(o, d0, d1, f0, f1):
-        return op("v", [o], [d0, d1], lambda e: V.tensor_tensor_scan(o[0], d0[0], d1[0], 0.0, f0, f1), SCAN * el(o, d0, d1))
+        return op("v", [o], [d0, d1], lambda e: V.tensor_tensor_scan(o[0], d0[0], d1[0], 0.0, f0, f1), el(o, d0, d1))
 
     def act(o, i, func=AF.Copy, scale=1.0, bias=0.0):
         if isinstance(bias, float) and bias == 0.0:
@@ -331,9 +322,8 @@ def rank_program(g, core, T, topo):
         return op(eng, [o], [w, off], lambda e: V.tensor_copy(o[0], ind(w, off)) if e == "v"
                   else S_.activation(o[0], ind(w, off), AF.Copy), 0.06 + 16 * off[0].shape[1] * CYC * GAT)
 
-    def sca(en, w, off, i):
-        return op(en, [w], [i, off], lambda e: V.tensor_copy(ind(w, off), i[0]) if e == "v" else S_.activation(ind(w, off), i[0], AF.Silu),
-                  0.06 + 128 * CYC * SCA)
+    def sca(w, off, i):
+        return op("v", [w], [i, off], lambda e: V.tensor_copy(ind(w, off), i[0]), 0.06 + 128 * CYC * SCA)
 
     def scamax(w, off, x, y):
         return op("v", [w], [x, y, off], lambda e: V.tensor_tensor(ind(w, off), x[0], y[0], OP.max), 0.06 + 128 * CYC * SCA)
@@ -374,6 +364,18 @@ def rank_program(g, core, T, topo):
         for s in range(1, N):
             sends[sem + str(s)] = k
 
+    def share_out(src, land, sem, cost):
+        w = src[3] - src[2]
+        m = topo.mask(core, T.cores[peer(1)])
+        to = [DstId(rid=topo.addr(T.cores[peer(s)])[0], pnc=topo.addr(T.cores[peer(s)])[1]) for s in range(1, N)]
+        mine = B(land, w * rank, w * rank + w)
+        tr = [RemoteDMATransfer(dst_ids=to, dma_engine_mask=m, remote_sem=T.sem[sem], srcs=[src[0]], dsts=[mine[0]] * 3)]
+        k = len(topo.engines(core, T.cores[peer(1)]))
+        sent[0] += k
+        sends[sem] = op("g", [], [src], lambda: g.remote_dma_fused(tr, local_sem=T.sem["snd"]), cost, "rem")
+        copy(mine, src)
+        op("r", [B(land, w * peer(s), w * peer(s) + w) for s in range(1, N)], [], None, 0.0, "arr", sem, 3 * k, [sends[sem]])
+
     def arrive3(x, sem, s):
         arrive(x, sem + str(s), len(share(T.cores[peer(-s)], core, s)))
 
@@ -382,9 +384,6 @@ def rank_program(g, core, T, topo):
 
     def isx(k):
         return B("MSK", k, k + 1)
-
-    def cls(n, c):
-        return B(n, BASE[c], BASE[c] + 128)
 
     def third(n, m):
         return B(n, 128 * m, 128 * m + 128)
@@ -395,18 +394,25 @@ def rank_program(g, core, T, topo):
     def seg(n, m):
         return B(n, NV_ * m, NV_ * (m + 1))
 
-    def ahead(n, s, lo=0):
-        return B(n, lo + 128 - 32 * s, lo + 256 - 32 * s)
+    def ahead(n, s):
+        return B(n, 128 - 32 * s, 256 - 32 * s)
 
     def rows(r):
         return slice(32 * r, 32 * r + 32)
 
+    def turn(t, name):
+        lead[0] = 100.0 * t + TURNS.index(name)
+
     def slot(n, r):
         return (T[n][r], n, r, r + 1)
 
+    HALF = ((slice(16, 2064), slice(2048, 4096), slice(0, 64)), (slice(2064, TW), slice(0, 2048), slice(64, 128)))
+
+    def tab(r, i):
+        return (None, "TAB", TW * i + 16 + 1024 * r, TW * i + 16 + 1024 * r + 1024)
+
     dma("s", [(None, "DP", 0, N)], [], T.DP[:], T.pots[:])
     dma("s", [slot("LP", rank)], [], T.LP[rank], T.pots[2 * rank:2 * rank + 2, :])
-    dma("s", [B("RAW0")], [], T.RAW0[:], T.bun[:], 6.5)
     send3(lambda s: slot("LP", rank), lambda s: slot("DP", peer(s)), "p", 7.0)
     order = []
 
@@ -414,35 +420,64 @@ def rank_program(g, core, T, topo):
         order.append(dma("y", outs, ins, out, in_, cost, order[-1:]))
 
     def table(s, cost):
-        x = slot("DT", peer(s))
-        load([x], [], x[0], T.sight[rows(peer(s)), :], cost)
-        send(s, slot("LT", rank), x, "t%d" % s, 5.5)
+        r = peer(s)
+        for k, (_, a, b) in enumerate(HALF):
+            load([(None, "DT", r + k / 2, r + k / 2 + 0.5)], [], T.DT[r, b], T.sight[rows(r), a], cost)
+        send(s, slot("LT", rank), slot("DT", r), "t%d" % s, DUE[8] + DUE[9] * s)
 
-    def land(s):
+    def half(x, k):
+        return (None, x[1], x[2] + k * (x[3] - x[2]) / 2, x[2] + (k + 1) * (x[3] - x[2]) / 2)
+
+    def land(s, i, after=()):
         r = peer(-s)
-        arrive(slot("LT", r), "t%d" % s, len(topo.engines(T.cores[r], core)))
-        load([(None, "TAB", 1024 * r, 1024 * r + 1024)], [slot("LT", r)], T.TAB[rows(r), 0:4096], T.LT[r], 4.0)
+        for k, (w, _, b) in enumerate(HALF):
+            load([half(tab(r, i), k)], [slot("LT", r)] + list(after), T.TAB[rows((r - i) % N), TW * i + w.start:TW * i + w.stop], T.LT[r, b], DUE[5])
 
-    table(1, 3.8)
-    table(2, 6.8)
-    load([B("TAB0", 0, 4096)], [], T.TAB0[:, 0:4096], T.sight[:], 12.5)
-    table(3, 14.0)
-    load([(None, "TAB", 1024 * rank, 1024 * rank + 1024)], [], T.TAB[rows(rank), 0:4096], T.sight[rows(rank), :], 15.5)
+    fill(B("POTH"), 0)
+    load([B("RAW0")], [], T.RAW0[:], T.bun[:], DUE[7])
+    load([B("POTH")], [], T.POTH[0:128:16, :], T.pots[:], DUE[7])
+    for k, (w, a, _) in enumerate(HALF):
+        load([B("TAB0", w.start, w.stop)], [], T.TAB0[:, w], T.sight[:, a], DUE[0])
+    for s in range(1, N):
+        table(s, DUE[s])
+    for i in (1, 0):
+        for k, (w, a, _) in enumerate(HALF):
+            load([half(tab(rank, i), k)], [], T.TAB[rows((rank - i) % N), TW * i + w.start:TW * i + w.stop], T.sight[rows(rank), a], DUE[4])
     fill(B("POTI"), 0)
-    fill(B("TAB", 4096, 4112), 0.0)
-    fill(B("TAB0", 4096, 4112), 0.0)
+    for s in range(N):
+        fill(B("TAB", TW * s, TW * s + 16), 0.0)
+    fill(B("TAB0", 0, 16), 0.0)
     for s in range(1, N):
         arrive3(slot("LP", peer(-s)), "p", s)
     load([B("POTI")], [(None, "LP", 0, N)], T.POTI[0:128:16, :], T.LP[:], 6.0)
     for s in range(1, N):
-        land(s)
+        arrive(slot("LT", peer(-s)), "t%d" % s, len(topo.engines(T.cores[peer(-s)], core)))
+        land(s, 1)
+        if s < SOON:
+            land(s, 0)
 
+    def windows():
+        for s in range(SOON, N):
+            land(s, 0, [B("LZ")])
+        for s in (2, 3):
+            lo, k = TW * s + 16, 32 * s
+            x, y = B("TAB", lo, lo + 4096), B("TAB", 16, TW)
+            load([half(x, 0)], [y, B("LZ")], T.TAB[0:128 - k, lo:lo + 4096], T.TAB[k:128, 16:TW], DUE[6] * (s - 1))
+            load([half(x, 1)], [y], T.TAB[128 - k:128, lo:lo + 4096], T.TAB[0:k, 16:TW], DUE[6] * (s - 1))
+
+    lead[0] = 1000.0
     iota(B("II", 0, 1), [[1, 1]], 0, 1)
     iota(B("FF"), [[1, 132]], 0, 0)
     iota(B("FX"), [[0, 8], [1, 16]], 0, 0)
     iota(B("FG"), [[1, 8], [0, 16]], 0, 0)
     iota(B("SLOT"), [[0, 8], [1, SEG]], 0, 0)
     iota(B("T19", 0, NV_), [[1, 8], [0, SEG]], 0, 0)
+    iota(B("EXI", 0, 8), [[1, 4], [4, 2]], 0, 0)
+    iota(B("EXI", 8, 24), [[8, 2], [24, 4], [1, 2]], 2 * rank + 8, 0)
+    iota(B("EXI", 24, 30), [[1, 3], [4, 2]], 9, 0)
+    iota(B("EXI", 30, 32), [[4, 2]], 8, 0)
+    fill(B("SU", 128, 4 * UW), 0.0)
+    copy(B("EXV"), B("EXI"))
     ts(B("II", 1, 2), B("II", 0, 1), 15, OP.bitwise_and)
     ts(B("II", 2, 3), B("II", 0, 1), 4, OP.logical_shift_right)
     copy(B("COL", 0, 3), B("II", 0, 3))
@@ -460,90 +495,60 @@ def rank_program(g, core, T, topo):
     ts(IDF, B("FF", 0, 128), col(0), OP.is_equal)
     act(third("PI", 1), IDF)
     act(B("IDN"), IDF)
+    act(B("IDU"), IDF, AF.Copy, 1.0 / UNIT)
     for h in range(2):
         ts(eight("GF", h), B("FF", 0, 8), col(2), OP.is_equal)
-    act(B("GS"), B("GF"))
-    act(B("GB"), B("GF"), AF.Copy, 2.0)
-    act(B("G0"), BLK, AF.Copy, isx(0))
+    act(B("GS"), BLK)
+    act(eight("GB", 0), BLK, AF.Copy, 4.0)
+    act(eight("GB", 1), BLK, AF.Copy, UNIT)
+    act(B("GU"), BLK, AF.Copy, 1.0 / UNIT)
     ts(B("EXL"), B("FF", 0, 8), float(SEG), OP.mult, SEG - 1.0, OP.add)
     ts(col(4), col(1), 0.0, OP.is_gt)
     ts(col(8), col(1), 13.0, OP.is_ge)
+    ts(col(9), col(1), -4.0 * 2 ** 19, OP.mult, 32.5 * 2 ** 19, OP.add)
     for m in range(3):
         act(third("BIAS", m), B("MSK"), AF.Identity, 512.0, -512.0)
-    act(B("PH"), B("PI"))
     copy(B("PG"), B("PI"))
-    for k in range(3):
-        fill(B("RW", k, 16, 3), float(k))
-    for k, pieces in ((1, ((0, 3, 8), (3, 6, 37), (6, 8, 128), (8, 16, 0))), (2, ((0, 3, 5), (3, 8, 0), (8, 10, 1), (10, 16, 0)))):
-        for lo, hi, v in pieces:
-            fill(B("RW", 16 * k + lo, 16 * k + hi), float(v))
-    for k in range(3):
-        x, y = B("RW", 16 * k, 16 * k + 16), col(17 + k)
-        tt(x, x, B("MSK", 0, 16), OP.mult)
-        op("v", [y], [x], lambda e, x=x, y=y: V.tensor_reduce(y[0], x[0], AX.X, OP.add), 64 * CYC)
-    ts(B("CAI"), B("FF", 0, 8), col(17), OP.add, 1.0, OP.add)
+    ts(col(17), col(1), 3.0, OP.is_lt)
+    ts(B("CAI"), B("FF", 0, 8), col(1), OP.add, 1.0, OP.add)
     ts(B("CAI"), B("CAI"), 3, OP.bitwise_and)
-    ts(B("CA"), B("CAI"), col(18), OP.mult, col(19), OP.add)
-    ts(B("CAI"), B("CAI"), 1.0, OP.add)
-    ts(B("CAI"), B("CAI"), 1, OP.logical_shift_right)
-    ts(col(27), isx(6), isx(7), OP.add, 128.0, OP.mult)
-    ts(B("ZT", 0, 8), B("CAI"), col(27), OP.mult)
-    tt(B("CA"), B("CA"), B("ZT", 0, 8), OP.add)
+    ts(B("CA"), B("CAI"), 8.0, OP.mult, 5.0, OP.add)
+    ts(B("CA"), B("CA"), col(17), OP.mult)
     for c in range(4):
         act(third("KC", c), B("FF", 0, 128), AF.Identity, col(8), B("CA", (c + 3) & 3, ((c + 3) & 3) + 1))
     for m in range(3):
-        w = 256 if m == 2 else 128
         ts(col(20 + m), isx(15 - m), -32.0, OP.mult, isx(m), OP.subtract)
-        ts(col(23 + m), isx(15 - m), 148.0, OP.mult, isx(3 + m), OP.add)
-        act(B("MA", 128 * m, 128 * m + w), B("BO", 0, w), AF.Copy, col(20 + m))
-        act(B("MW", 128 * m, 128 * m + w), B("BO", 0, w), AF.Copy, col(23 + m))
-        act(B("SEL", 128 * m, 128 * m + w), B("BO", 0, w), AF.Copy, isx(15 - m))
-    IL = eight("IL", 0)
+        act(third("MA", m), BO, AF.Copy, col(20 + m))
+        act(third("SEL", m), BO, AF.Copy, isx(15 - m))
+    IL = B("IL")
     ts(IL, B("FF", 0, 8), 16.0, OP.mult, col(1), OP.add)
-    act(eight("IL", 1), IL, AF.Identity, 1.0, 128.0)
-    act(eight("IL", 2), IL, AF.Identity, 1.0, 872.0)
-    act(eight("CX", 0), IL, AF.Identity, 32.0, 47.0)
-    act(B("TMP", 0, 8), B("FF", 0, 8), AF.Identity, -256.0, 4096.0 - 32.0)
-    ts(col(3), col(1), -16.0, OP.mult)
-    act(B("CL"), B("TMP", 0, 8), AF.Identity, 1.0, col(3))
     act(B("IXP"), IDF, AF.Copy, col(4))
     copy(B("RG"), B("REV"))
-    ts(col(7), col(0), 768.0, OP.add, UNIT, OP.mult)
+    ts(col(7), col(0), 4096.0 * UNIT, OP.mult, -1.0, OP.add)
     act(B("NONE"), B("FF", 0, 8), AF.Identity, 0.0, col(7))
     fill(col(14), 63 * math.log(2.0))
     fill(col(15), 63 * math.log(2.0) + math.log(2.5))
-    fill(col(10), 67.5 * 16384)
     act(B("W8"), IL, AF.Exp, -math.log(2.0), col(14))
-    k = act(col(16), col(0), AF.Exp, -math.log(2.0), col(15))
-    op("s", [col(9)], [col(1), col(10), B("W8"), col(16)], lambda e: S_.activation(col(9)[0], col(1)[0], AF.Silu, bias=col(10)[0], scale=-4.0 * 16384), 1.5)
+    act(col(16), col(0), AF.Exp, -math.log(2.0), col(15))
     for c in range(8):
-        act(B("WG", 16 * c, 16 * c + 16), B("GF"), AF.Copy, B("W8", c, c + 1))
-    t19 = seg("T19", 0)
+        act(eight("WG", c), BLK, AF.Copy, B("W8", c, c + 1))
+    t19 = B("T19")
     ts(t19, t19, col(2), OP.is_equal)
     for k in (0, SEG - 2, SEG - 1):
         fill(B("T19", k, NV_, SEG), 0.0)
-    ts(col(11), isx(0), -2.0, OP.mult)
-    for h in range(2):
-        act(seg("NEGV", h), t19, AF.Copy, col(11))
-    fill(B("CD"), 2.0 * VOFF - 1.0)
-    for k, v in ((0, 1.0), (SEG - 2, -1.0), (SEG - 1, 0.0)):
-        fill(B("CD", k, NV_, SEG), v)
-    ts(col(26), isx(8), 64.0, OP.mult, isx(9), OP.add)
-    ts(col(26), col(26), 1024.0 * UNIT, OP.mult)
-    for m in range(2):
-        ts(col(27), isx(8), (2 - m) * 16.0, OP.mult, isx(9), OP.subtract)
-        ts(col(27), col(27), 1024.0, OP.mult, isx(15 - m), OP.add)
-        ts(col(27), col(27), isx(6 + m), OP.add, UNIT, OP.mult)
-        act(B("U19"), B("SLOT"), AF.Identity, col(26), col(27))
-        tt(seg("QX", m), B("U19"), t19, OP.mult)
-        act(B("QX", NV_ * m + SEG - 1, NV_ * (m + 1), SEG), BLK, AF.Copy, isx(8))
-    ts(col(27), col(0), 896.0 - 1024.0, OP.add, UNIT, OP.mult)
-    act(seg("CODE", 2), B("SLOT"), AF.Identity, (65536.0 + 1024.0) * UNIT, col(27))
-    fill(B("CODE", 2 * NV_, 3 * NV_, SEG), 0.0)
-    fill(B("CODE", 2 * NV_ + SEG - 1, 3 * NV_, SEG), 1.0)
-    for x in (B("WIN", 128, 256), B("WIN", 512, 640), B("VR", 128, 256), B("VR", 512, 640), B("VR", 768, 896), B("VR", 896, 1024)):
-        act(x, B("FX"))
-    ts(col(5), isx(0), -1.0, OP.mult)
+    ts(col(11), isx(0), -4.0, OP.mult)
+    act(B("NEGV"), t19, AF.Copy, col(11))
+    fill(B("CD"), -2.0)
+    fill(B("CD", 0, 6 * NV_, SEG), 2.0)
+    fill(B("CD", SEG - 1, 6 * NV_, SEG), 0.0)
+    for m in range(3):
+        act(seg("CD", 2 * m + 1), B("SLOT"), AF.Identity, 0.125, (-33.0 - m) / 32)
+        fill(B("CD", NV_ * (2 * m + 1) + SEG - 2, NV_ * (2 * m + 2), SEG), 0.0)
+        if m == 1:
+            fill(B("CD", 2 * NV_ + SEG - 1, 3 * NV_, SEG), -2.0)
+        ts(col(23 + m), isx(15 - m), 4096.0 * UNIT, OP.mult)
+        act(seg("QX", m), t19, AF.Copy, col(23 + m))
+    act(B("VR", 0, 640), B("RST", 0, 640))
     act(B("PSELA"), ahead("BO", 1), AF.Copy, 0.5)
     ts(col(6), col(1), 2.0, OP.is_lt)
     act(B("POLDA"), B("PSELA"), AF.Copy, col(6))
@@ -560,49 +565,39 @@ def rank_program(g, core, T, topo):
     copy(B("COL", 28, 30), B("II", 3, 5))
     ts(col(28), col(28), 16.0, OP.mult, col(12), OP.add)
     ts(col(28), col(28), 4.0, OP.mult, 3.0, OP.add)
-    ts(B("U19", 0, 132), B("FF", 0, 132), col(28), OP.is_equal)
-    ts(B("ZT", 8, 12), B("FF", 0, 4), col(29), OP.is_equal, -1.0, OP.mult)
+    ts(B("U19"), B("FF", 0, 132), col(28), OP.is_equal)
+    ts(B("ZT", 8, 12), B("FF", 0, 4), col(29), OP.is_equal)
     for r in range(N):
-        ts(B("HOME", 132 * r, 132 * r + 132), B("U19", 0, 132), B("ZT", 8 + r, 9 + r), OP.mult)
-    fill(B("C64"), VOFF)
-    copy(eight("ZI", 0), B("FF", 0, 8))
-    ts(eight("ZI", 1), eight("ZI", 0), 1, OP.logical_shift_right)
-    tt(eight("ZT", 2), eight("ZI", 0), eight("ZI", 1), OP.add)
-    tt(eight("ZT", 3), eight("ZT", 2), eight("ZI", 1), OP.add)
-    copy(eight("EXV", 0), eight("ZT", 3))
-    tt(eight("ZT", 3), eight("ZT", 3), eight("ZI", 0), OP.add)
-    tt(eight("ZT", 3), eight("ZT", 3), eight("ZI", 0), OP.add)
-    for c in range(1, 4):
-        ts(eight("EXV", c), eight("ZT", 3), c - 1.0, OP.add)
+        ts(B("HOME", 132 * r, 132 * r + 132), B("U19"), B("ZT", 8 + r, 9 + r), OP.mult)
+    iota(B("TMP"), [[8, 2], [0, 16], [1, 4]], 0, 0)
+    ts(col(27), B("II", 3, 4), 8.0, OP.mult, 3.0, OP.add)
+    fill(B("HV"), 0.0)
+    for r in range(N):
+        ts(B("HV", 132 * r, 132 * r + 128), B("TMP"), col(27), OP.is_equal, B("ZT", 8 + r, 9 + r), OP.mult)
+    fill(B("WV", 0, 512, 4), -2047.0)
+    MID = (EMPTY - 2 * LOW - 1) / 2
+    fill(col(10), -MID)
 
-    FLAG = (1 << 19) | 4095
+    FLAG = (1 << 26) | 4095
 
     def part(x, lo, hi):
         return B(x[1], x[2] + lo, x[2] + hi)
 
-    def index(tag, s, a, w, halves=1):
+    def index(tag, s, a, c, halves=1):
         n = 128 // halves
-        k = len(a)
         for lo in range(0, 128, n):
-            o = 128 * "012S".index(tag) + k * lo
-            xi, xj = B("XI", o, o + k * n), B("XJ", o, o + k * n)
-            for m in range(k):
-                tt(B("XI", o + m, o + k * n, k), s if halves == 1 else part(s, lo, lo + n), part(a[m], lo, lo + n), OP.mult)
-            ts(xj, xi, 5, OP.arith_shift_right, FLAG, OP.bitwise_and)
-            tt(xi, xj, part(w, k * lo, k * (lo + n)), OP.add)
-            ts(xj, xi, FLAG, OP.bitwise_and)
-            ts(B("OFF", o, o + k * n), xj, 4096.0, OP.min)
+            o = 128 * "012S".index(tag) + lo
+            xi, xj = B("XI", o, o + n), B("XJ", o, o + n)
+            tt(xi, s if halves == 1 else part(s, lo, lo + n), part(a, lo, lo + n), OP.mult)
+            ts(xj, xi, 721635.0 - 4096.0 * (8 * c + 5), OP.add)
+            ts(xi, xj, 5, OP.arith_shift_right, FLAG, OP.bitwise_and)
+            ts(B("OFF", o, o + n), xi, -1.0, OP.mult, TW - 1.0, OP.add)
 
-    TABW = B("TAB", 0, 4097)
+    def place(tag, k, lo=0, hi=128):
+        m = 2048 * "012S".index(tag)
+        return B("X", m + 16 * lo + k, m + 16 * hi, 16)
 
-    def place(tag, k, pair=False):
-        m = "012S".index(tag)
-        return B("X", 16 * m + k, 4096, 32) if pair else B("X", 2048 * m + k, 2048 * m + 2048, 16)
-
-    def turn(t, name):
-        lead[0] = 100.0 * t + TURNS.index(name)
-
-    def look(t, tag, pieces, tab=TABW):
+    def look(t, tag, pieces, tab):
         a = 128 * "012S".index(tag)
         for eng, n in pieces:
             x = B("X", 16 * a, 16 * (a + n))
@@ -612,239 +607,216 @@ def rank_program(g, core, T, topo):
             scan(x, B("RST", 0, 16 * n), x, OP.mult, OP.max)
             a += n
 
-    def own_marks(c, bank):
-        mm(third(bank, 2), third("MA", 0), third("KC", c))
-        mm(third(bank, 3), third("MW", 0), third("KC", c))
+    def window(s):
+        return B("TAB", TW * s, TW * s + TW)
 
-    fill(B("VA"), 0.0)
-    fill(B("VB"), 0.0)
-    turn(-4, "names")
-    ts(B("BF"), B("RAW0"), -1.0, OP.mult)
+    turn(-6, "names")
+    ts(B("RAW0"), B("RAW0"), EMPTY, OP.bitwise_and)
+    ts(B("BF"), B("RAW0"), -LOW, OP.add)
 
     def some(x, r):
         return (T[x[1]][rows(r), x[2]:x[3]],) + x[1:]
 
     turn(-3, "end")
-    ts(B("BG"), B("RAW0"), -1.0, OP.mult, 2047.0, OP.add)
+    ts(B("BG"), B("RAW0"), -2047.0, OP.add, 0.125, OP.mult)
     for s in (1, 2, 3, 0):
         o = third(("b7", "b0", "b1", "b2")[s], 0)
         for q in range(4):
             mm(o, some(ahead("PG", (q - peer(s)) % N), peer(s)), some(third("BG", q), peer(s)), q == 0, q == 3)
-        copy(third("SU" if s else "LB", s), o)
-    send3(lambda s: third("LB", s), lambda s: third("SU", s), "u", 7.0)
-    for c, tag in enumerate("S012"):
+        copy(B("SU" if s else "LB", UW * peer(s), UW * peer(s) + 128), o)
+    for c in (0, 3, 1, 2):
+        tag = "S012"[c]
         bank = "b%d" % (3 + c)
-        turn(-3 + (c > 0), "index" + tag if c else "names")
-        own_marks(c, bank)
-        index(tag, B("BF", c, 512, 4), [third(bank, 2)], third(bank, 3))
-        look(-3 + (c > 0), tag, FIRST[c], B("TAB0", 0, 4097))
-        mm(B(bank, 0, 8), place(tag, 15), eight("GS", 0))
-        ts(B("VB", c - 1, 24, 3) if c else B("VA", 0, 8), B(bank, 0, 8), VOFF, OP.add)
-        if c in (0, 3):
-            n, w, k = ("VA", 2, 4) if c == 0 else ("VB", 6, 8)
-            send3(lambda s: B("L" + n, k * rank, k * rank + k), lambda s: B(n, w * peer(s), w * peer(s) + k), n, 8.0 if c == 0 else 4.5)
-            copy(B("L" + n, k * rank, k * rank + k), B(n, w * rank, w * rank + k))
-            for s in range(1, N):
-                arrive3(B("L" + n, k * peer(-s), k * peer(-s) + k), n, s)
-    turn(-2, "end")
-    for s in range(1, N):
-        arrive3(third("LB", s), "u", s)
-    for q in range(4):
-        for s in range(N):
-            k = mm(third("b2", q), some(ahead("RG", (peer(-s) - q) % N), q), some(third("LB", s), q), s == 0, s == N - 1)
-            if s == 0 and q:
-                ops[k]["pre"][k - 1] = True
-    for c in range(4):
-        turn(-1, "pool")
-        mov("WIN", cls("WIN", c), B("b2", c, 512, 4), 1.0, -2047.0)
-        turn(0 if c else -1, ("names", "value0", "value1", "value2")[c])
-        gat("s", third("VJ", c % 3), B("LVB" if c else "LVA"), eight("EXV", c))
-        mm(third("b7", 1 + c % 3), third("VJ", c % 3), IDF)
-        act(cls("VR", c), third("b7", 1 + c % 3))
-    turn(-1, "end")
-    ts(B("PL0"), B("POTI"), col(5), OP.mult)
+        when = (-5, -3, -3, -4)[c]
+        turn(when, "index" + tag if c else "names")
+        mm(third(bank, 2), third("MA", 0), third("KC", c))
+        index(tag, B("BF", c, 512, 4), third(bank, 2), c)
+        look(when, tag, FIRST[c], B("TAB0"))
+        if c < 3:
+            mm(third(bank, 1), BO, place(tag, 15))
+            act(third("VH", c), third(bank, 1))
+        mm(B(bank, 0, 8), place(tag, 15), B("GS"))
+        if c in (1, 2):
+            copy(eight("ZH", c), B(bank, 0, 8))
+            continue
+        for h in range(2):
+            ts(B("SU", 128 + 2 * (c // 3) + h, 4 * UW, UW), B(bank, h, 8, 2), -2047.0, OP.add)
+        if c:
+            send3(lambda s: B("LB", UW * rank, UW * rank + UW), lambda s: B("SU", UW * peer(s), UW * peer(s) + UW), "u", DUE[11])
+            copy(B("LB", UW * rank + 128, UW * rank + UW), B("SU", UW * rank + 128, UW * rank + UW))
 
-    def shift(name, o, x, s, via, scale=1.0, bias=0.0):
-        mm(via, ahead({F: "PI", H: "PH", G: "PG"}[SCRATCH[x[1]][2]], s), x)
-        mov(name, o, via, scale, bias)
-
-    def kpart(t):
-        c = t & 3
-        mov("KS", B("KS"), cls("WIN", c), -1.0, 13.0 * t - VOFF)
-        tt(B("KT"), B("KS"), cls("VR", c), OP.add)
-        ts(B("KI"), B("KT"), 127, OP.bitwise_and)
-        ts(B("KB"), B("KI"), col(8), OP.mult, B("CA", t, t + 1), OP.add)
-
-    def of(n, m, s):
-        return third(n, m) if m < 2 else ahead(n, s, 256)
-
-    def spread(t, s):
-        kb = B("KB")
-        turn(t, "index0")
-        for m in range(2):
-            mm(third("b0", m), of("MA", m, s), kb)
-        for m in range(2):
-            mm(B("b1", m, 256, 2), of("MW", m, s), kb)
-        turn(t, "index2")
-        mm(third("b2", 0), of("MA", 2, s), kb)
-        mm(third("b2", 1), of("MW", 2, s), kb)
-        turn(t, "lists")
-        mm(B("b3", 0, 384), B("IDN"), B("BIAS"), True, False)
-        for m in range(3):
-            mm(third("b3", m), kb, of("SEL", m, s), False, m == 2)
-        if "KM" in ON:
-            ts(B("KM"), B("b3", 0, 384), 0.0, OP.max)
-        else:
-            act(B("KM"), B("b3", 0, 384), AF.Relu)
-        for m in range(3):
-            mm(B("b3", 384 + m * 8, 392 + m * 8), third("KM", m), eight("GS", 0))
-        mov("LF", B("LF"), B("b3", 384, 408))
-        copy(B("VL"), B("b3", 384, 408))
-        for m in range(3):
-            bank = "b%d" % (4 + m)
-            turn(t, "rows%d" % m)
-            mm(third(bank, 3), of("SEL", m, s), kb)
-            if m < 2:
-                mm(B(bank, 160, 160 + NV_), kb, seg("QX", m))
-                mov("CODE", seg("CODE", m), B(bank, 160, 160 + NV_))
-            mov("KRB", third("KRB", m), third(bank, 3))
-
-    def firsts(t, s):
-        for m in range(3):
-            turn(t, "first%d" % m)
-            sh = 2 * s if m == 2 else 0
-            for c in range(8):
-                x = third("EB", 8 * m + c)
-                ts(x, third("KRB", m), B("LF", m * 8 + c, m * 8 + c + 1), OP.is_equal)
-                mm(eight("b7", m), x, B("WG", 16 * c + sh, 16 * c + sh + 8), c == 0, c == 7)
-        act(B("CODE", SEG - 2, 3 * NV_, SEG), B("b7", 0, 24), AF.Sign, -1.0, col(16))
-
-    def verdict(t, m, best):
-        bank = "b%d" % (4 + m)
-        sh = 2 * (1 + t % 3) if m == 2 else 0
-        turn(t, "value%d" % m)
-        gat(eng("VJ%d" % m), third("VJ", m), cls("VR", (t + 1 + m) & 3), eight("VL", m))
-        o = B(bank, 0, NV_)
-        mm(o, B("IDN"), B("CD"), True, False)
-        mm(o, third("VJ", m), B("NEGV", SEG * sh, SEG * sh + NV_), False, False)
-        turn(t, "verdict%d" % m)
-        tiles = TILES if m == 2 else ((0, 128),)
-        for lo, hi in tiles:
-            if hi == 128 and m != 1:
-                mm(B(bank, SEG - 1, NV_, SEG), IDF, best, False, False)
-            for k in range(16):
-                x = place(str(m), k, m < 2)
-                if m == 2:
-                    x = B("X", 4096 + 16 * lo + k, 4096 + 16 * hi, 16)
-                mm((T[bank][lo:hi, 16 - k:NV_:SEG], bank, 0, NV_), x, B("GB", sh, sh + 8), False, k == 15 and m != 1 and hi == 128)
-        if m == 1:
-            mm(B(bank, SEG - 1, NV_, SEG), IDF, best, False, True)
-        scan(seg("ZS", m), o, seg("CODE", m), OP.max, OP.min)
-        return B("ZS", NV_ * m + SEG - 1, NV_ * (m + 1), SEG)
-
-    def late(t):
-        s = 1 + t % 3
-        c = (t + 3) & 3
-        lo = BASE[c] - 128 * (c & 1)
-        odd = c & 1
-        ts(eight("ZT", 2), eight("ZI", 2), 896.0, OP.is_ge if odd else OP.is_lt, 1000.0, OP.mult)
-        mm(B("b5", 320, 328), B("IDN"), B("CL"), True, False)
-        mm(B("b5", 320, 328), ahead("PI", s), eight("ZT", 0), False, True)
-        mm(B("b5", 328, 336), B("IDN"), eight("LF", 2), True, False)
-        mm(B("b5", 328, 336), ahead("PI", s), eight("ZT", 2), False, True)
-        copy(B("LXb"), B("b5", 320, 328))
-        tt(eight("ZT", 3), B("b5", 328, 336), eight("IL", 1 + odd), OP.max if odd else OP.min)
-        ts(B("LST2"), eight("ZT", 3), -872.0 * odd, OP.add)
-        shift("KEEP2", B("KEEP2"), B("KEEP"), s, third("b6", 3), -4096.5, -4095.5)
-        if t == RO - 1:
-            scamax(B("WIN", lo, lo + 256), B("LST2"), third("S2", t & 1), B("KEEP2"))
-            turn(t, "change")
-        gat(eng("NXb") if t < RO - 1 else "s", B("NXb"), B("X", 0, 6144), B("LXb"))
-        mm(third("b5", 3), BO, B("NXb"))
-        mov("NVb" if t < RO - 1 else "", B("NVb"), third("b5", 3), 1.0, VOFF)
-        turn(t + (t < RO - 1), "late" if t < RO - 1 else "end")
-        if t < RO - 1:
-            scamax(B("WIN", lo, lo + 256), B("LST2"), third("S2", t & 1), B("KEEP2"))
-        sca(eng("SCA2"), B("VR", lo, lo + 256), B("LST2"), B("NVb"))
-
-    for t in range(RO):
-        s = 1 + t % 3
-        old = cls("WIN", t & 3)
-        si, s2 = B("WIN", 768, 896), third("S2", t & 1)
+    def names(t, si, old, v, pool=None):
         turn(t, "names")
-        if t == 0:
+        if pool:
+            ts(pool, pool, EMPTY, OP.bitwise_and)
+            ts(B("PL0"), pool, -LOW, OP.add, isx(0), OP.mult)
             mm(third("b1", 3), IDF, B("PL0"), True, False)
         mm(third("b1", 3), B("IXP"), old, False, True)
         mov("SI", si, third("b1", 3))
-        kpart(t)
-        turn(t, "rows2")
-        shift("S2", s2, si, s, third("b2", 2))
+        mov("KS", B("KS"), v, 1.0, LOW + 13.0 * max(t, 0))
+        tt(B("KT"), B("KS"), old, OP.add)
+        ts(B("KI"), B("KT"), 127, OP.bitwise_and)
+        ts(B("KB"), B("KI"), col(8), OP.mult, B("CA", max(t, 0), max(t, 0) + 1), OP.add)
+
+    def spread(t, ms):
+        kb = B("KB")
+        lo, hi = ms[0], ms[-1] + 1
+        for m in ms:
+            turn(t, "index%d" % m)
+            mm(third("b0", m), third("MA", m), kb)
+        turn(t, "lists")
+        x = B("b3", 128 * lo, 128 * hi)
+        mm(x, B("IDN"), B("BIAS", 128 * lo, 128 * hi), True, False)
+        for m in ms:
+            mm(third("b3", m), kb, third("SEL", m), False, m == ms[-1])
+        if "KM" in ON:
+            ts(B("KM", 128 * lo, 128 * hi), x, 0.0, OP.max)
+        else:
+            act(B("KM", 128 * lo, 128 * hi), x, AF.Relu)
+        for m in ms:
+            mm(B("b3", 384 + m * 8, 392 + m * 8), third("KM", m), B("GS"))
+        mov("LF", B("LF", 8 * lo, 8 * hi), B("b3", 384 + 8 * lo, 384 + 8 * hi))
+        copy(B("VL", 8 * lo, 8 * hi), B("b3", 384 + 8 * lo, 384 + 8 * hi))
+        turn(t, "rows")
+        for m in ms:
+            mm(third("b2", m), third("SEL", m), kb)
+        mov("KRB", B("KRB", 128 * lo, 128 * hi), B("b2", 128 * lo, 128 * hi))
+
+    def firsts(t, ms):
+        for m in ms:
+            turn(t, "first%d" % m)
+            for c in range(8):
+                x = third("EB", 8 * m + c)
+                ts(x, third("KRB", m), B("LF", m * 8 + c, m * 8 + c + 1), OP.is_equal)
+                mm(eight("b7", m), x, eight("WG", c), c == 0, c == 7)
+        turn(t, "firsts")
+        act(B("FS", 8 * ms[0], 8 * ms[-1] + 8), B("b7", 8 * ms[0], 8 * ms[-1] + 8), AF.Sign, -1.0, col(16))
+
+    def verdict(t, m, v, best):
+        bank = "b%d" % (4 + m)
+        turn(t, "value%d" % m)
+        gat(eng("VJ%d" % m), third("VJ", m), v, eight("VL", m))
+        d, c = seg(bank, 0), seg(bank, 1)
+        mm(B(bank, 0, 2 * NV_), B("IDN"), B("CD", 2 * NV_ * m, 2 * NV_ * (m + 1)), True, False)
+        mm(c, B("KB"), seg("QX", m), False, False)
+        mm(d, third("VJ", m), B("NEGV"), False, False)
+        turn(t, "verdict%d" % m)
+
+        for lo, hi in TILES if m == 2 else ((0, 128),):
+            for k, x in enumerate(best if hi == 128 else ()):
+                mm(B(bank, SEG * k + SEG - 1, NV_, SEG * len(best)), IDF, x, False, False)
+            for k in range(16):
+                mm((T[bank][lo:hi, 16 - k:2 * NV_:SEG], bank, 0, 2 * NV_), place(str(m), k, lo, hi), B("GB"), False, False)
+        mm(B(bank, NV_ + SEG - 2, 2 * NV_, SEG), B("IDN"), eight("FS", m), False, True)
+        turn(t, "code%d" % m)
+        mov("CODE%d" % m, seg("CODE", m), c)
+        scan(seg("ZS", m), d, seg("CODE", m), OP.max, OP.min)
+        return B("ZS", NV_ * m + SEG - 1, NV_ * (m + 1), SEG)
+
+    turn(-5, "names")
+    mm(third("b1", 0), ahead("RG", 0), B("BG", 0, 512, 4))
+    mov("WIN", B("OH"), third("b1", 0), 8.0, 2047.0 - LOW)
+    names(-2, B("SH"), B("OH"), third("VH", 0), B("POTH"))
+    spread(-2, (0, 1))
+    for m in range(2):
+        turn(-2, "index%d" % m)
+        index(str(m), B("SH"), third("b0", m), 1 + m, HALVES[m])
+        look(-2, str(m), EARLY[m], B("TAB0"))
+    firsts(-2, (0, 1))
+    tt(eight("ZH", 0), verdict(-2, 0, third("VH", 1), [B("NONE")]), verdict(-2, 1, third("VH", 2), []), OP.max)
+    share_out(B("ZH"), "LZ", "VB1", DUE[12])
+    turn(-1, "names")
+    for s in range(1, N):
+        arrive3(B("LB", UW * peer(-s), UW * peer(-s) + UW), "u", s)
+    windows()
+    for k in range(4):
+        ts(B("LVA", 4 * k, 4 * k + 4), B("LB", 128 + k, 4 * UW, UW), 2047.0, OP.add)
+    for q in range(4):
+        for s in range(N):
+            k = mm(third("b2", q), some(ahead("RG", (s - q) % N), q), some(B("LB", UW * s, UW * s + 128), q), s == 0, s == N - 1)
+            if s == 0 and q:
+                ops[k]["pre"][k - 1] = True
+
+    def values(c, via):
+        gat("s", third("VK", c), B("LZ" if c in (1, 2) else "LVA"), eight("EXV", c))
+        mm(via, third("VK", c), IDF)
+        act(third("VR", 8 - c), via)
+
+    for c in (0, 3, 1, 2):
+        turn(0 if c else -1, "pool")
+        mov("WIN", third("WIN", 8 - c) if c < 3 else B("NU"), B("b2", c, 512, 4), 8.0, 2047.0 - LOW)
+        if c in (0, 3):
+            values(c, third("b3", c % 2))
+
+    for t in range(RO):
+        s = 1 + t % 3
+        last = t == RO - 1
+        ms = (0, 1, 2) if t else (2,)
+        si, old = third("WIN", 4 - t), third("WIN", 8 - t)
+        names(t, si, old, third("VR", 8 - t), None if t else B("POTI"))
         turn(t, "bundle2")
         twin(B("S1"), si)
-        spread(t, s)
-        turn(t, "index0")
-        index("0", si, [third("b0", 0), third("b0", 1)], B("b1", 0, 256), HALVES[0])
-        look(t, "0", PIECES[0])
-        look(t, "1", PIECES[1])
-        turn(t, "index2")
-        index("2", s2, [third("b2", 0)], third("b2", 1), HALVES[2])
-        look(t, "2", PIECES[2])
-        turn(t, "scanS")
-        own_marks(t & 3, "b0")
+        spread(t, ms)
+        turn(t, "back")
+        mm(third("b1", 0), ahead("PI", N - s), B("NU"))
         if t:
-            mm(third("b1", 2), BO, place("S", 15))
-            mov("VR", cls("VR", (t - 1) & 3), third("b1", 2), 1.0, VOFF)
-        firsts(t, s)
+            for k, n in enumerate(("WIN", "VR")):
+                mm(third("b1", 1 + k), ahead("PI", 1 + (t - 1) % 3), third(n, 6 - t))
+            mov("BACKV", third("VR", 6 - t), third("b1", 2))
+        k = 256 if t else 128
+        mov("BACK", B("WIN", 128 * (5 - t), 128 * (5 - t) + k), B("b1", 0, k))
+        for m in ms:
+            turn(t, "index%d" % m)
+            index(str(m), si, third("b0", m), (t + 1 + m) & 3, HALVES[m])
+            look(t, str(m), PIECES[m] if t else EARLY[m], window(s if m == 2 else 0))
+        turn(t, "scanS")
+        mm(third("b0", 3), third("MA", 0), third("KC", t & 3))
+        if t:
+            mm(third("b3", 0), ahead("BO", N - s), place("S", 15))
+            mov("VR", third("VR", 5 - t), third("b3", 0))
+        firsts(t, ms)
         turn(t, "pool")
-        dif = B("b6", 160, 288)
+        for c in () if t else (1, 2):
+            values(c, third("b7", 1 + c))
+        dif = third("b7", 1)
         mm(dif, B("DIF"), old)
-        last = t == RO - 1
         mm(third("b1", 3), B("POLDA" if last else "POLD"), old, True, False)
-        turn(t, "bundle2")
-        w2, l2 = cls("WIN", (t + 3) & 3), eight("VL", 2)
-        op("v", [B("CS")], [w2, l2], lambda e, w2=w2, l2=l2: V.tensor_scalar(T.CS[:], ind(w2, l2), 2047.0, None, OP.add), 0.06 + 128 * CYC * GAT)
-        shift("C2", B("WIN", 896, 1024), B("CS"), N - s, third("b2", 2), 1.0, -2047.0)
-        best = B("NONE")
-        for m in range(3):
-            best = verdict(t, m, best)
+        if t:
+            tt(eight("ZT", 0), verdict(t, 0, third("VR", 7 - t), [B("NONE")]), verdict(t, 1, third("VR", 6 - t), []), OP.max)
+        verdict(t, 2, third("VR", 5 - t), [eight("ZT", 0)] if t else [B("LZ", 2 * rank + h, 96, 24) for h in range(2)])
         turn(t, "decide")
         zq, zx, zm = seg("ZS", 2), B("ZX"), B("ZM")
-        op("s", [zx], [zq, B("EXL")], lambda e, zq=zq: S_.activation(T.ZX[:], zq[0].indirect(T.EXL[:]), AF.Copy, scale=1.0 / UNIT),
-           0.06 + 128 * CYC * GAT)
+        gat("s", zx, zq, B("EXL"))
         op("v", [zm], [zq, B("EXL"), B("MSK")], lambda e, zq=zq: V.tensor_tensor(T.ZM[:], zq[0].indirect(T.EXL[:]), T.MSK[:], OP.mult),
            0.06 + 128 * CYC * GAT)
-        mm(B("b3", 440, 448), zm, BLK)
-        mm(third("b2", 3), zx, B("IDN"))
-        ts(eight("ZI", 0), B("b3", 440, 448), 1.0 / UNIT, OP.mult)
-        ts(eight("ZI", 2), eight("ZI", 0), 1023, OP.bitwise_and)
-        ts(eight("ZI", 1), eight("ZI", 0), 10, OP.logical_shift_right, 63, OP.bitwise_and)
-        copy(B("LST"), eight("ZI", 2))
-        tt(eight("ZT", 0), eight("CX", 0), eight("ZI", 1), OP.subtract)
-        copy(B("LX"), eight("ZT", 0))
-        nu, w, ls = B("NU"), B("WIN"), B("LST")
+        mm(B("b3", 440, 448), zm, B("GU"))
+        z = third("b2", 3)
+        mm(z, zx, B("IDU"))
+        copy(eight("ZI", 0), B("b3", 440, 448))
+        ts(eight("ZI", 1), eight("ZI", 0), 12, OP.arith_shift_right, 511, OP.bitwise_and)
+        copy(B("LST"), eight("ZI", 1))
+        nu, ls = B("NU"), B("LST")
+        w, wv = (B(n, 128 * (4 - t), 128 * (8 - t)) for n in ("WIN", "VR"))
+        copy(B("NI"), z)
+        ts(B("KEEP1"), z, col(9), OP.subtract, EMPTY - LOW, OP.min)
+        act(B("KEEP"), z, AF.Sign, -1.0, col(9))
+        ts(B("NJ"), B("NI"), 4095, OP.bitwise_and)
         gat(eng("NU"), nu, w, ls)
-        gat(eng("NX"), B("NX"), B("X", 0, 6144), B("LX"))
-        mm(third("b4", 3), BO, B("NX"))
-        mov("NV", B("NV"), third("b4", 3), 1.0, VOFF)
-        ts(B("KEEP1"), third("b2", 3), col(9), OP.subtract, 1.0, OP.min)
-        act(B("KEEP"), third("b2", 3), AF.Sign, -1.0, col(9))
-        turn(t, "indexS")
-        index("S", nu, [third("b0", 2)], third("b0", 3), HALVES[3])
+        sca(wv, ls, B("NJ"))
         turn(t, "change")
         scamax(w, ls, B("S1"), B("KEEP1"))
-        sca(eng("SCA"), B("VR"), ls, B("NV"))
+        turn(t, "pass")
         tt(B("PP"), dif, B("KEEP"), OP.mult)
         mm(third("b1", 3), B("PSELA" if last else "PSEL"), B("PP"), False, last)
-        if not last:
-            turn(t + 1, "rows2")
-            twin(old, nu)
-        look(t + 1, "S", LAST if last else PIECES[3])
-        turn(t + 1 - last, "change" if last else "lists2")
-        late(t)
+        turn(t + 1, "indexS")
+        index("S", nu, third("b0", 3), t & 3, HALVES[3])
+        look(t + 1, "S", LAST if last else PIECES[3], window(0))
     turn(RO, "names")
 
-    def piece(n, s, lo=0, hi=160):
-        return B(n, 160 * s + lo, 160 * s + hi)
+    s3 = 1 + (RO - 1) % 3
+
+    def piece(n, s, lo=0, hi=288):
+        return B(n, 288 * s + lo, 288 * s + hi)
 
     def tile(s, lo, hi, step=1):
         return B(("b6", "b7", "b3", "b4")[s], lo, hi, step)
@@ -852,44 +824,45 @@ def rank_program(g, core, T, topo):
     def home(s, k):
         for q in range(4):
             lo = 132 * peer(s) + 3 - q
-            mm(tile(s, 128, 160) if k else tile(s, 0, 128), B("HOME", lo, lo + 128),
-               B("WH", 512 + 32 * q, 544 + 32 * q) if k else third("WH", q), q == 0, q == 3)
+            x = (third("WV", q), B("WH", 512 + 32 * q, 544 + 32 * q), third("WH", q), place("S", 15, 32 * q, 32 * q + 32))[k]
+            o = (tile(s, 160, 288), tile(s, 128, 160), tile(s, 0, 128), tile(s, 160, 288, 4))[k]
+            mm(o, B("HV" if k == 3 else "HOME", lo, lo + 128), x, k + q == 0, k + q == 6)
 
-    ts(third("WH", 4), third("b1", 3), 2047.0, OP.add)
-    for s in range(1, N):
-        home(s, 1)
-    for c in range(4):
-        ts(B("WH", c, 512, 4), cls("WIN", c) if c else B("NU"), 2047.0, OP.add)
-    for s in range(1, N):
-        home(s, 0)
-        ts(piece("OU", s), tile(s, 0, 160), 2048.0, OP.add)
-    send3(lambda s: piece("LO", s), lambda s: piece("OU", s), "w", 5.0)
-    turn(RO, "verdict2")
+    def plain(o, x, k):
+        act(third("WA", k), x, AF.Abs, 1.0, col(10))
+        ts(o, third("WA", k), -1.0, OP.mult, MID + LOW - 2047.0, OP.add)
+
+    mm(third("b5", 0), ahead("PI", s3), third("VR", 1))
+    mm(third("b2", 0), ahead("PI", s3), third("WIN", 1))
     for c in range(1, 4):
-        mm(B("b2", c, 32, 4), cls("VR", c), B("G0"))
-    mm(B("b2", 0, 32, 4), B("IDN"), B("C64"), True, False)
-    mm(B("b2", 0, 32, 4), place("S", 15), eight("GS", 0), False, True)
-    ts(B("VI"), B("b2", 0, 32), -VOFF - 2040.0, OP.add)
-    copy(B("VT"), B("VI"))
-    send3(lambda s: eight("LV", rank), lambda s: eight("VT", peer(s)), "v", 4.5)
-    copy(eight("LV", rank), eight("VI", rank))
+        ts(B("WV", c, 512, 4), third("VR", 4 - c) if c < 3 else third("b5", 0), -2047.0, OP.add)
+    plain(third("WH", 4), third("b1", 3), 4)
+    for c in range(4):
+        plain(B("WH", c, 512, 4), (B("NU"), third("WIN", 3), third("WIN", 2), third("b2", 0))[c], c)
+    for k in range(4):
+        for s in (1, 2, 3, 0):
+            turn(RO, "names" if s else "end")
+            home(s, k)
+    turn(RO, "names")
+    for s in range(1, N):
+        ts(piece("OU", s), tile(s, 0, 288), 2048.0, OP.add)
+        if APART:
+            send(s, piece("LO", s), piece("OU", s), "w%d" % s, 3.0)
+    if not APART:
+        send3(lambda s: piece("LO", s), lambda s: piece("OU", s), "w", 5.0)
     turn(RO, "end")
-    for k in range(2):
-        home(0, k)
-    plus(piece("OUT", 0), tile(0, 0, 160), 2047.0)
+    act(piece("OUT", 0), tile(0, 0, 288), AF.Identity, 1.0, 2047.0)
     for s in range(N):
         r = peer(-s)
         if s:
-            arrive3(piece("LO", s), "w", s)
+            if APART:
+                arrive(piece("LO", s), "w%d" % s, len(topo.engines(T.cores[r], core)))
+            else:
+                arrive3(piece("LO", s), "w", s)
             ts(piece("OUT", s), piece("LO", s), -1.0, OP.add)
-            arrive3(eight("LV", r), "v", s)
         dma("y", [], [piece("OUT", s)], T.yb[rows(r), :], piece("OUT", s, 0, 128)[0])
-        dma("y", [], [piece("OUT", s)], T.yp[2 * r:2 * r + 2, :], T.OUT[0:128:17, 160 * s + 128:160 * s + 160])
-    turn(RO, "change")
-    for c in range(4):
-        mm((T.b1[0:8, c:512:4], "b1", 0, 512), B("LV", c, 32, 4), third("PG", 0))
-    op("s", [B("BF")], [B("b1")], lambda e: S_.activation(T.BF[0:8, :], T.b1[0:8, :], AF.Identity, bias=2040.0), 512 * CYC)
-    dma("s", [], [B("BF")], T.yv[:], T.BF[0:8, :])
+        dma("s", [], [piece("OUT", s)], T.yv[2 * r:2 * r + 2, :], T.OUT[0:128:17, 288 * s + 160:288 * s + 288])
+        dma("s", [], [piece("OUT", s)], T.yp[2 * r:2 * r + 2, :], T.OUT[0:128:17, 288 * s + 128:288 * s + 160])
     flush()
     for k in dmas:
         if known["y"].get(k, 0) < 16:

@@ -6,20 +6,69 @@ F, H, G, I, U = "float32", "bfloat16", "float16", "int32", "uint16"
 RO = 5
 CYC, PEC, WAKE, SELF, ISSUE, GAT, SCA, SLACK = 0.00083, 0.0008, 0.15, 0.2, 1.2, 1.45, 3.8, (0.2, 1.0, 1.4)
 VFIX, CAP, PROP, PASSES = 0.02, 0.2, "vstgyr", 1
-APART = True
-SOON = 2
-DUE = (7.0, 8.0, 9.0, 10.0, 12.0, 3.5, 5.0, 3.0, 5.0, 2.5, 7.0, 7.0, 4.5)
+CALLS = ((1, 2), (3,))
+FLEX = 0
+ORDER, MOVES, HEAT, MEAN = {}, 0, 0.05, 0.5
+TRIES, SHAKE, PLANNED, TAIL = 0, 0.3, [], 1
 CH = 64
-PIECES = ((("s", 24), ("s", 40), ("s", 64)), (("v", 32), ("v", 32), ("s", 16), ("s", 48)), (("v", 32), ("s", 64), ("s", 16), ("s", 16)),
-          (("s", 16), ("s", 48), ("s", 64)))
-FIRST = ((("s", 56), ("v", 24), ("s", 48)), (("s", 64), ("s", 64)), (("s", 64), ("s", 64)), (("v", 40), ("s", 32), ("v", 56)))
-LAST = (("s", 48), ("v", 16), ("s", 40), ("s", 24))
-EARLY = ((("s", 64), ("s", 16), ("s", 48)), (("s", 32), ("s", 56), ("v", 40)), (("s", 48), ("v", 48), ("v", 16), ("s", 16)), ())
-HALVES = (1, 1, 1, 2)
+
+
+def _cut(s):
+    return tuple(tuple((x[0], int(x[1:])) for x in p.split()) for p in s.split(","))
+
+
+_E = ["EB%d" % _m for _m in range(25)]
+STEPS = {"v": ("ZM1 ZI1 ZI2 NI1 LST1 KEEP11 XI1 NJ1 XJ1 PP1 XI2 XJ2 OFF1 VR1 XI3 WIN1 OFF2 KT1 X1 KI1 KB1 X2 XI4 XI6 XJ3 KM1 XI5 XJ4 OFF3 XI7 XI8 "
+               "VL1 OFF4 XJ5 EB1 X3 XI9".split() + _E[2:8] + ["OFF5"] + _E[8:23]
+               + "X7 EB23 X4 EB24 X10 X5 FS1 X6 X8 X9 X11 X12 ZS1 X13 X14 ZS2 CODE1 ZT1 ZS3 ZF1".split(), []),
+         "s": ("ZX1 KEEP1 NU1 X1 b01 X2 WIN1 X3 KRB1 LF1 X4 VR2 VR1 X5 VJ2 X6 VJ3 VJ1 X7 X8 CODE1 X9 X10 WIN2 CODE2".split(), [])}
+ZF, LAP = 1, -1
+TILE1 = ((0, 128),)
 TILES = ((0, 96), (96, 128))
-ON = ("KM", "WIN", "CODE2", "VJ1")
-TURNS = ("names indexS help0 index0 lists index1 rows first0 code0 code1 code2 pool firsts bundle2 help1 gather0 scan2 back gather2 gatherS "
-         "first1 gather1 value1 verdict0 decide scanS help2 index2 change helpS scan1 value2 first2 scan0 verdict2 verdict1 value0 pass end").split()
+SOON, AFTER, STAGE = 1, 3, (0, 1, 2, 3)
+DUE = (6.2, 6.0, 8.0, 11, 10.5, 1.0, 7.0, 2.7, 3, 1.5, 3.7, 4, 1.5)
+PIECES = _cut("s64 s64, s64 v32 s32, v48 s48 s16 s16, s32 s32 s64")
+FIRST = _cut("s48 v32 s48, s64 s64, s64 s64, s32 v64 v24 v8")
+EARLY = _cut("v40 s56 s24 s8, s64 s24 v40, s40 s8 v48 s32")
+LAST = _cut("v8 s32 v40 s16 v32")[0]
+HALVES = (1, 1, 1, 2)
+ON = "KM SU RG OUT3 CODE2 FS OUV1 OU0 OV3".split()
+TURNS = "names index0 gather0 lists index1 code0 scanS helpS verdict0 indexS value0 decide scan2 scan0 value2 back index2 bundle2 gather2 first2 pass change scan1 value1 pool gather1 verdict1 help2 verdict2 gatherS first1 firsts first0 code2 help0 help1 rows code1 end".split()
+BY = {}
+HANDS, HANDED = 2, ["30", "31", "21"]
+LOADS = (("R", 3.0), ("30", 3.0), ("10", 3.5), ("T", 6.5), ("31", 7.5), ("11", 8), ("21", 8.5), ("20", 9.0))
+POSTS = (("30", 10.0), ("10", 5.0), ("31", 9.0), ("p", 4.0), ("11", 6.0), ("21", 8.0), ("20", 5.0))
+LANDS = ("10", "p", "30", "11", "31", "20", "21")
+AFTER, SOON, PASSES = 3, 8, 2
+DUE = (2.5, 0, 0, 0, 0, 0, 6.0, 0, 0, 0, 3.5, 6, 6)
+FIRST = _cut("v48 v16 s64, s32 s32 s64, s64 v8 v56, s64 v48 s8 v8")
+EARLY = _cut("s64 s64, s32 s48 s48, s64 v32 s24 s8")
+LAST = _cut("v24 s24 v16 s24 v8 v32")[0]
+ON = "KM SU RG OU0 OUT2 OUT3 OV0 OU2 CODE2 FS".split()
+TURNS = "firsts index2 back index1 names lists first2 rows verdict0 first0 value1 change decide value2 code2 pool gather2 indexS helpS gather1 verdict1 scanS pass gatherS value0 help0 help2 gather0 verdict2 scan2 code0 scan0 index0 help1 first1 bundle2 scan1 code1 end".split()
+HANDED = []
+LOADS = (("10", 2.0), ("R", 2.9), ("11", 3.3), ("T", 7.2), ("20", 7.6), ("21", 8.0), ("30", 8.4), ("31", 8.8))
+POSTS = (("10", 6.5), ("11", 5.0), ("p", 5.0), ("20", 5.5), ("21", 7.0), ("30", 7.5), ("31", 9.0))
+LANDS = ("10", "11", "p", "20", "21", "30", "31")
+AFTER, PASSES = 5, 1
+CYC, PEC, WAKE, SELF, VFIX, GAT, SCA = 0.0009, 0.00046, 0.2, 0.23, 0.005, 1.35, 2.2
+DUE = (2.5, 0, 0, 0, 0, 0, 6, 0, 0, 0, 4.0, 5.0, 4.5)
+FIRST = _cut("v48 v16 s64, s8 s16 s40 s64, v8 s64 v56, v32 s64 v32")
+EARLY = _cut("s64 s64, s32 s48 s48, s64 v32 s24 s8")
+STEPS, ZF, SLACK, CAP = {}, 0, (0.1, 0.8, 2.0), 0.5
+PIECES = _cut("s16 s64 s48, v32 v40 s56, v32 s64 s32, s16 s48 s16 v16 s32")
+HALVES = (2, 2, 1, 2)
+ON = "KM VJ1 SU RG OU0 OUT2 OUT3 OV0 OU2".split()
+TURNS = "first2 index2 help2 bundle2 verdict0 back value2 value1 gather0 gather2 firsts code2 first1 decide scan0 help0 names verdict1 scan1 gather1 first0 help1 value0 rows pass index0 verdict2 scan2 code1 pool lists gatherS indexS change index1 helpS code0 scanS end".split()
+PASSES = 1
+TILES, SLACK, CAP = ((0, 64), (64, 96), (96, 128)), (0.1, 0.6, 2.2), 0.55
+PIECES = _cut("s32 s64 s32, v48 s40 s40, v48 s24 s24 v16 s16, s16 s48 v16 s48")
+FIRST = _cut("v56 v8 s64, s8 s16 s40 s64, v8 v56 s64, v32 s64 v32")
+EARLY = _cut("s64 v64, v16 s16 s64 s32, s64 v32 s24 v8")
+LAST = _cut("s8 s24 s40 v40 v16")[0]
+HALVES = (2, 1, 1, 2)
+ON = "KM RG OUT3 OU2 WH0 WH1 OU3 OUT1 OUT2 OV3 PG".split()
+TURNS = "first2 help0 help2 bundle2 verdict0 gatherS index0 back value2 index1 first1 decide first0 code2 gather2 help1 helpS gather0 rows code1 code0 names scan0 change scan2 indexS value1 gather1 verdict2 verdict1 scan1 firsts pool scanS lists index2 pass value0 end".split()
 SEG = 19
 NV_ = 8 * SEG
 UNIT = 2.0 ** -24
@@ -35,10 +84,9 @@ def _sb(name, w, d):
 
 
 _sb("TAB", 4 * TW, H)
-for _m, _w, _d in (("T", 1024, H), ("P", 2, I)):
-    SCRATCH["D" + _m] = ("dram", [4, 128, _w], _d)
-    SCRATCH["L" + _m] = ("dram", [4, 128, _w], _d)
-_sb("TAB0", TW, H)
+for _m, _k, _w, _d in (("T", 8, 512, H), ("P", 4, 2, I)):
+    SCRATCH["D" + _m] = ("dram", [_k, 128, _w], _d)
+    SCRATCH["L" + _m] = ("dram", [_k, 128, _w], _d)
 _sb("RAW0", 512, I)
 for _m, _w in (("LVA", 16), ("ZH", 24), ("LZ", 96), ("VH", 384), ("VK", 512), ("OH", 128), ("SH", 128)):
     _sb(_m, _w, F)
@@ -49,7 +97,7 @@ UW = 136
 _sb("SU", 4 * UW, G)
 _sb("LB", 4 * UW, G)
 _sb("BG", 512, G)
-_sb("REV", 256, F)
+_sb("AS", 512, F)
 _sb("RG", 256, G)
 _sb("POTI", 128, I)
 _sb("PL0", 128, F)
@@ -73,21 +121,23 @@ _sb("KM", 384, H)
 _sb("LF", 24, H)
 _sb("VL", 24, U)
 _sb("FS", 24, H)
-_sb("VJ", 384, F)
+_sb("VJ", 384, G)
 _sb("EB", 3072, H)
 _sb("CODE", 3 * NV_, F)
 _sb("ZS", 3 * NV_, F)
 _sb("ZI", 16, I)
 _sb("ZT", 32, F)
+_sb("ZF", 8, F)
 for _m in ("LST", "EXL"):
     _sb(_m, 8, U)
 _sb("WA", 640, F)
 _sb("WH", 768, G)
 _sb("HOME", 4 * 132, G)
-_sb("HV", 4 * 132, H)
-_sb("WV", 512, G)
-_sb("OU", 4 * 288, U)
-_sb("LO", 4 * 288, U)
+_sb("HV", 160, H)
+_sb("HP", 160, G)
+_sb("WV", 640, G)
+_sb("OU", 4 * 288, G)
+_sb("LO", 4 * 288, G)
 _sb("OUT", 4 * 288, F)
 _sb("II", 8, I)
 _sb("FF", 132, F)
@@ -96,21 +146,21 @@ _sb("FG", 128, F)
 _sb("SLOT", NV_, F)
 _sb("T19", NV_, F)
 _sb("U19", 132, F)
-_sb("NEGV", NV_, F)
+_sb("NEGV", NV_, G)
 _sb("CD", 6 * NV_, H)
-_sb("QX", 3 * NV_, H)
+_sb("QX", 4 * NV_, H)
 _sb("COL", 32, F)
 _sb("CA", 8, F)
 _sb("CAI", 8, I)
-_sb("W8", 8, F)
+_sb("W8", 128, F)
 _sb("WG", 64, H)
 _sb("BO", 256, H)
 _sb("PI", 256, F)
 _sb("IDN", 128, H)
-_sb("BIAS", 384, H)
+_sb("BIAS", 128, H)
 _sb("PG", 256, G)
 _sb("KEEP", 128, H)
-_sb("GF", 16, F)
+_sb("GF", 8, F)
 _sb("GS", 8, H)
 _sb("GB", 16, H)
 _sb("G0", 16, F)
@@ -122,16 +172,35 @@ _sb("NONE", 8, F)
 for _m in range(8):
     SCRATCH["b%d" % _m] = ("psum", [128, 512], F)
 
-SEMAPHORES = ["cv", "cs", "ct", "cg", "snd", "t1", "t2", "t3", "u1", "u2", "u3", "w1", "w2", "w3", "v1", "v2", "v3", "p1", "p2", "p3",
-              "VA1", "VA2", "VA3", "VB1", "VB2", "VB3"]
+SEMAPHORES = ["cv", "cs", "ct", "cg", "snd", "u1", "u2", "u3", "w1", "w2", "w3", "p1", "p2", "p3", "VB1"]
+SEMAPHORES += [_m + _s + _k for _m in "th" for _s in "123" for _k in "01"]
 SEMAPHORES += ["d%d" % _m for _m in range(90)]
 TWO = (H, G, U)
+
+
+def hands(core, topo):
+    return [c for c in topo.cores_of(core) if topo.die(c) != topo.die(core)][:HANDS]
+
+
+def hand_on(g, core, T, topo):
+    N = len(T.cores)
+    for rank, c in enumerate(T.cores):
+        if core in hands(c, topo):
+            sent = 0
+            for x in HANDED[hands(c, topo).index(core)::HANDS]:
+                r, k = (rank + int(x[0])) % N, int(x[1])
+                to = T.cores[r]
+                g.wait_ge(T.sem["h" + x], len([e for e in topo.engines(c, core) if e not in topo.engines(c, to)]))
+                rid, pid = topo.addr(to)[:2]
+                g.remote_dma(T.LT[2 * rank + k], T.DT[2 * r + k], T.sem["t" + x], T.sem["snd"], pid, rid, topo.mask(core, to))
+                sent += len(topo.engines(core, to))
+            g.wait_ge(T.sem["snd"], sent)
 
 
 def rank_program(g, core, T, topo):
     rank = T.rank_of(core)
     if rank is None:
-        return
+        return hand_on(g, core, T, topo)
     N = len(T.cores)
     Q = {"v": g.vector, "s": g.scalar, "t": g.tensor, "g": g, "y": g.sync}
     ops = []
@@ -139,6 +208,13 @@ def rank_program(g, core, T, topo):
     cnt, clk = {}, {}
     lead = [-1000.0]
     known = {e: {} for e in Q}
+    seen = {"cycle": -1}
+    marks = {}
+
+    def mark(name, late=0.0):
+        if name in BY:
+            marks[len(ops) - 1] = BY[name] + late
+    behind = []
 
     def psum(n):
         return n[0] == "b" and len(n) == 2
@@ -146,14 +222,14 @@ def rank_program(g, core, T, topo):
     def op(eng, outs, ins, call, cost, kind="c", sem=None, inc=1, extra=()):
         k = len(ops)
         pre = {}
-        for j in extra:
+        for j in list(extra) + behind:
             pre[j] = False
         for wr, lst in ((True, outs), (False, ins)):
             for (_, n, lo, hi) in lst:
                 for (alo, ahi, aw, ae, j) in acc.get(n, []):
                     if psum(n) and ae == "t" and eng == "t":
                         pre.setdefault(j, False)
-                    elif (psum(n) and ae != eng) or (alo < hi and lo < ahi and (aw or wr)):
+                    elif (psum(n) and (ae != eng or len(eng) > 1)) or (alo < hi and lo < ahi and (aw or wr)):
                         pre[j] = True
         for wr, lst in ((False, ins), (True, outs)):
             for (_, n, lo, hi) in lst:
@@ -163,7 +239,9 @@ def rank_program(g, core, T, topo):
                 if wr:
                     a[:] = [x for x in a if not (lo <= x[0] and x[1] <= hi)]
                 a.append((lo, hi, wr, eng, k))
-        ops.append({"eng": eng, "call": call, "cost": cost + (VFIX if eng == "v" else 0.0), "pre": pre, "kind": kind, "sem": sem, "inc": inc, "lead": lead[0]})
+        name = outs[0][1] if outs else ""
+        seen[eng[0] + name] = seen.get(eng[0] + name, 0) + 1
+        ops.append({"step": (seen["cycle"], name + str(seen[eng[0] + name])), "eng": eng, "call": call, "cost": cost + (VFIX if eng == "v" else 0.0), "pre": pre, "kind": kind, "sem": sem, "inc": inc, "lead": lead[0]})
         return k
 
     def learn(eng, tk):
@@ -186,29 +264,35 @@ def rank_program(g, core, T, topo):
 
     def flush():
         n = len(ops)
-        pre = [[(j, (SELF if ops[j]["eng"] == o["eng"] else WAKE) if w else 0.0) for j, w in o["pre"].items()] for o in ops]
+        for e in STEPS:
+            for t in range(RO):
+                mine = {o["step"][1]: k for k, o in enumerate(ops) if o["step"][0] == t and o["eng"][0] == e}
+                row = [mine[x] for x in STEPS[e][t == RO - 1] if x in mine]
+                for j, k in zip(row, row[1:]):
+                    ops[k]["pre"].setdefault(j, False)
+        pre = [[(j, (SELF if ops[j]["eng"][0] == o["eng"][0] else WAKE) if w else None if w is None else 0.0) for j, w in o["pre"].items()] for o in ops]
         succ = [[] for _ in ops]
         for k in range(n):
             for j, w in pre[k]:
                 succ[j].append((k, w))
         cost = [o["cost"] for o in ops]
         hold = [{"arr": 0.0, "dma": 0.1, "rem": ISSUE}.get(o["kind"], o["cost"]) for o in ops]
+        hold[[o["kind"] for o in ops].index("rem")] = DUE[10]
         key = [o["lead"] for o in ops]
         for k in range(n - 1, -1, -1):
-            if ops[k]["eng"] in PROP or key[k] < 0:
-                key[k] = min([key[k]] + [key[j] for j, w in succ[k]])
+            key[k] = min([key[k]] + [key[j] for j, w in succ[k]])
         on = [o["eng"] for o in ops]
 
         def gap(i, w):
-            return cost[i] + w if w or ops[i]["kind"] != "dma" else hold[i]
+            return hold[i] if w is None else cost[i] + w if w or ops[i]["kind"] != "dma" else hold[i]
 
         def plan(key, back):
             before, after = (succ, pre) if back else (pre, succ)
             left = [len(x) for x in before]
             ready = {e: {} for e in "vstgyr"}
             for k in range(n):
-                if left[k] == 0:
-                    ready[on[k]][k] = cost[k] - hold[k] if back else 0.0
+                for e in on[k][0] if left[k] == 0 else "":
+                    ready[e][k] = cost[k] - hold[k] if back else 0.0
             free = {e: 0.0 for e in ready}
             at, seq = [0.0] * n, []
             while len(seq) < n:
@@ -218,24 +302,92 @@ def rank_program(g, core, T, topo):
                 k = next(k for k in mine if ready[e][k] <= t0 + min(CAP, SLACK["vst".find(e)] * hold[now]))
                 at[k] = max(t0, ready[e].pop(k))
                 free[e] = at[k] + hold[k]
-                seq.append(k)
+                seq.append((k, e))
                 for j, _ in after[k]:
                     left[j] -= 1
-                    if left[j] == 0:
-                        ready[on[j]][j] = (max(at[i] + hold[i] + gap(j, w) - hold[j] for i, w in succ[j]) if back
-                                           else max(at[i] + gap(i, w) for i, w in pre[j]))
+                    for x in on[j][0] if left[j] == 0 else "":
+                        ready[x][j] = (max(at[i] + hold[i] + gap(j, w) - hold[j] for i, w in succ[j]) if back
+                                       else max(at[i] + gap(i, w) for i, w in pre[j]))
             return max(at[k] + cost[k] for k in range(n)), seq, at
 
+        if BY:
+            for k, _ in reversed(plan(key, False)[1]):
+                key[k] = min([marks.get(k, 1e4)] + [key[j] - gap(k, w) for j, w in succ[k]])
         best = now = plan(key, False)
         for _ in range(PASSES):
             at = plan([-now[2][k] - hold[k] for k in range(n)], True)[2]
             now = plan([-at[k] - hold[k] for k in range(n)], False)
             best = min(best, now)
+        for i in range(TRIES):
+            at = plan([-best[2][k] - hold[k] + SHAKE * math.sin(7.0 * i + 0.7 * k * (i + 1)) for k in range(n)], True)[2]
+            best = min(best, plan([-at[k] - hold[k] for k in range(n)], False))
         seq = best[1]
+
+        def clock(seq):
+            at, why, last = [0.0] * n, [-1] * n, {}
+            for k, e in seq:
+                t0, j0 = 0.0, -1
+                if e in last:
+                    j0 = last[e]
+                    t0 = at[j0] + hold[j0]
+                for j, d in lag[k]:
+                    if at[j] + d > t0:
+                        t0, j0 = at[j] + d, j
+                at[k], why[k], last[e] = t0, j0, k
+            k = max(range(n), key=lambda k: at[k] + cost[k])
+            return at[k] + cost[k] + MEAN * sum(at) / n, k, why, at
+
+        lag = [[(j, gap(j, w)) for j, w in pre[k]] for k in range(n)]
+        if True:
+            now = clock(seq)
+            rnd = 1
+            goal = [o["step"] for o in ops].index((0, "ZM1"))
+            for i in range(MOVES):
+                where = {k: p for p, (k, e) in enumerate(seq)}
+                held, k = [], goal if rnd >> 18 & 1 else rnd % goal
+                while now[2][k] >= 0:
+                    j = now[2][k]
+                    if j not in ops[k]["pre"]:
+                        held.append((j, k))
+                    k = j
+                rnd = rnd * 48271 % 2147483647
+                if not held:
+                    continue
+                j, k = held[rnd % len(held)]
+                a, b = where[j], where[k]
+                between = seq[a:b + 1]
+                if rnd >> 20 & 1 and len(on[j] + on[k]) > 2:
+                    x = j if len(on[j]) > 1 and (len(on[k]) == 1 or rnd >> 12 & 1) else k
+                    new = [(y, "vs".replace(e, "") if y == x else e) for y, e in between]
+                elif rnd >> 12 & 1:
+                    mv = {k}
+                    for x, _ in reversed(between):
+                        if x not in mv and any(y in mv for y, _ in succ[x]):
+                            mv.add(x)
+                    if j in mv:
+                        continue
+                    new = [x for x in between if x[0] in mv] + [x for x in between if x[0] not in mv]
+                else:
+                    mv = {j}
+                    for x, _ in between:
+                        if x not in mv and any(y in mv for y, _ in pre[x]):
+                            mv.add(x)
+                    if k in mv:
+                        continue
+                    new = [x for x in between if x[0] not in mv] + [x for x in between if x[0] in mv]
+                seq[a:b + 1] = new
+                c = clock(seq)
+                if c[0] <= now[0] + HEAT * (1 - i / MOVES) * (rnd >> 14 & 7) / 7:
+                    now = c
+                    seq.sort(key=lambda x: c[3][x[0]])
+                else:
+                    seq[a:b + 1] = between
+            ORDER[n] = seq
+            PLANNED.append((best[0], now[0] - MEAN * sum(now[3]) / n))
+        seq = ORDER[n]
         tok = {}
-        for k in seq:
+        for k, e in seq:
             o = ops[k]
-            e = on[k]
             if o["kind"] == "arr":
                 tok[k] = (o["sem"], o["inc"])
                 clk[tok[k]] = {o["sem"]: o["inc"]}
@@ -301,15 +453,22 @@ def rank_program(g, core, T, topo):
         return op("s", [o], [i] + cols(bias, scale), lambda e: S_.activation(o[0], i[0], func, bias=a_(bias), scale=a_(scale)), el(o))
 
     def mov(name, o, i, scale=1.0, bias=0.0):
-        if name in ON:
-            return ts(o, i, scale, OP.mult, bias, OP.add)
-        return act(o, i, AF.Identity if bias else AF.Copy, scale, bias)
+        def call(e):
+            if e == "v":
+                return V.tensor_scalar(o[0], i[0], a_(scale), a_(bias), OP.mult, OP.add)
+            if isinstance(bias, float) and bias == 0.0:
+                return S_.activation(o[0], i[0], AF.Copy, scale=a_(scale))
+            return S_.activation(o[0], i[0], AF.Identity, bias=a_(bias), scale=a_(scale))
+        return op(eng(name), [o], [i] + cols(scale, bias), call, el(o) + VFIX * (eng(name) != "v"))
+
+    def put(o, c):
+        return act(o, B("FF", 0, o[0].shape[1]), AF.Identity if c else AF.Copy, 0.0, c)
 
     def twin(o, i):
         return op("g", [o], [i], lambda e: g.affine_select(o[0], i[0], [[0, 128]], OP.is_ge, 0.0, 0, 0), 0.17 + 2 * el(o))
 
     def eng(name):
-        return "v" if name in ON else "s"
+        return ("vs" if name in ON else "sv")[:1 + FLEX]
 
     def mm(o, l, r, start=True, stop=True):
         n = max(min(64, l[0].shape[1]), r[0].shape[1])
@@ -406,67 +565,95 @@ def rank_program(g, core, T, topo):
     def slot(n, r):
         return (T[n][r], n, r, r + 1)
 
-    HALF = ((slice(16, 2064), slice(2048, 4096), slice(0, 64)), (slice(2064, TW), slice(0, 2048), slice(64, 128)))
+    HALF = ((slice(16, 2064), slice(2048, 4096)), (slice(2064, TW), slice(0, 2048)))
 
-    def tab(r, i):
-        return (None, "TAB", TW * i + 16 + 1024 * r, TW * i + 16 + 1024 * r + 1024)
+    def tab(s, k, i):
+        lo = TW * i + 16 + 1024 * s + 512 * k
+        return (None, "TAB", lo, lo + 512)
 
     dma("s", [(None, "DP", 0, N)], [], T.DP[:], T.pots[:])
     dma("s", [slot("LP", rank)], [], T.LP[rank], T.pots[2 * rank:2 * rank + 2, :])
-    send3(lambda s: slot("LP", rank), lambda s: slot("DP", peer(s)), "p", 7.0)
-    order = []
+    order, posts = [], []
 
     def load(outs, ins, out, in_, cost):
         order.append(dma("y", outs, ins, out, in_, cost, order[-1:]))
 
-    def table(s, cost):
-        r = peer(s)
-        for k, (_, a, b) in enumerate(HALF):
-            load([(None, "DT", r + k / 2, r + k / 2 + 0.5)], [], T.DT[r, b], T.sight[rows(r), a], cost)
-        send(s, slot("LT", rank), slot("DT", r), "t%d" % s, DUE[8] + DUE[9] * s)
+    def post(x, cost):
+        if x == "p":
+            send3(lambda s: slot("LP", rank), lambda s: slot("DP", peer(s)), "p", cost)
+        else:
+            s, k = int(x[0]), int(x[1])
+            src = slot("DT", 2 * peer(s) + k)
+            if x in HANDED:
+                to = hands(core, topo)[HANDED.index(x) % HANDS]
+                en = [e for e in topo.engines(core, to) if e not in topo.engines(core, T.cores[peer(s)])]
+                rid, pid = topo.addr(to)[:2]
+                sends["t" + x] = op("g", [], [src], lambda: g.remote_dma(src[0], src[0], T.sem["h" + x], T.sem["snd"], pid, rid, sum(1 << e for e in en)),
+                                    cost, "rem")
+                sent[0] += len(en)
+            else:
+                send(s, slot("LT", 2 * rank + k), src, "t" + x, cost)
+        for j in posts[-1:]:
+            ops[-1]["pre"][j] = None
+        posts.append(len(ops) - 1)
 
     def half(x, k):
         return (None, x[1], x[2] + k * (x[3] - x[2]) / 2, x[2] + (k + 1) * (x[3] - x[2]) / 2)
 
-    def land(s, i, after=()):
-        r = peer(-s)
-        for k, (w, _, b) in enumerate(HALF):
-            load([half(tab(r, i), k)], [slot("LT", r)] + list(after), T.TAB[rows((r - i) % N), TW * i + w.start:TW * i + w.stop], T.LT[r, b], DUE[5])
+    def land(x, i, after=()):
+        s, k = int(x[0]), int(x[1])
+        r, w = peer(-s), HALF[k][0]
+        load([tab(s, k, i)], [slot("LT", 2 * r + k)] + list(after), T.TAB[rows((r - i) % N), TW * i + w.start:TW * i + w.stop], T.LT[2 * r + k], DUE[0])
 
     fill(B("POTH"), 0)
-    load([B("RAW0")], [], T.RAW0[:], T.bun[:], DUE[7])
-    load([B("POTH")], [], T.POTH[0:128:16, :], T.pots[:], DUE[7])
-    for k, (w, a, _) in enumerate(HALF):
-        load([B("TAB0", w.start, w.stop)], [], T.TAB0[:, w], T.sight[:, a], DUE[0])
-    for s in range(1, N):
-        table(s, DUE[s])
-    for i in (1, 0):
-        for k, (w, a, _) in enumerate(HALF):
-            load([half(tab(rank, i), k)], [], T.TAB[rows((rank - i) % N), TW * i + w.start:TW * i + w.stop], T.sight[rows(rank), a], DUE[4])
+    for x, due in LOADS:
+        if x == "R":
+            load([B("RAW0")], [], T.RAW0[:], T.bun[:], due)
+            load([B("POTH")], [], T.POTH[0:128:16, :], T.pots[:], due)
+        elif x == "T":
+            for w, a in HALF:
+                load([B("TAB", w.start, w.stop)], [], T.TAB[:, w], T.sight[:, a], due)
+        else:
+            s, k = int(x[0]), int(x[1])
+            load([slot("DT", 2 * peer(s) + k)], [], T.DT[2 * peer(s) + k], T.sight[rows(peer(s)), HALF[k][1]], due)
+    load([(None, "TAB", TW + 16, TW + 1040)], [B("TAB", 16, TW)], T.TAB[rows(peer(-1)), TW + 16:2 * TW], T.TAB[rows(rank), 16:TW], DUE[0])
+    for x, due in POSTS[:AFTER]:
+        post(x, due)
     fill(B("POTI"), 0)
     for s in range(N):
         fill(B("TAB", TW * s, TW * s + 16), 0.0)
-    fill(B("TAB0", 0, 16), 0.0)
-    for s in range(1, N):
-        arrive3(slot("LP", peer(-s)), "p", s)
-    load([B("POTI")], [(None, "LP", 0, N)], T.POTI[0:128:16, :], T.LP[:], 6.0)
-    for s in range(1, N):
-        arrive(slot("LT", peer(-s)), "t%d" % s, len(topo.engines(T.cores[peer(-s)], core)))
-        land(s, 1)
-        if s < SOON:
-            land(s, 0)
+
+    def lands():
+        posts.append(sends["u1"])
+        for x, due in POSTS[AFTER:]:
+            post(x, due)
+        for x in LANDS:
+            if x == "p":
+                for s in range(1, N):
+                    arrive3(slot("LP", peer(-s)), "p", s)
+                load([B("POTI")], [(None, "LP", 0, N)], T.POTI[0:128:16, :], T.LP[:], DUE[0])
+                continue
+            arrive(slot("LT", 2 * peer(-int(x[0])) + int(x[1])), "t" + x, len(topo.engines(T.cores[peer(-int(x[0]))], core)))
+            land(x, 1)
 
     def windows():
-        for s in range(SOON, N):
-            land(s, 0, [B("LZ")])
+        for s in range(1, N):
+            for k in range(2):
+                land("%d%d" % (s, k), 0, [B("LZ") if 2 * s + k >= SOON else B("TAB", TW + 16, 2 * TW)])
         for s in (2, 3):
             lo, k = TW * s + 16, 32 * s
-            x, y = B("TAB", lo, lo + 4096), B("TAB", 16, TW)
-            load([half(x, 0)], [y, B("LZ")], T.TAB[0:128 - k, lo:lo + 4096], T.TAB[k:128, 16:TW], DUE[6] * (s - 1))
-            load([half(x, 1)], [y], T.TAB[128 - k:128, lo:lo + 4096], T.TAB[0:k, 16:TW], DUE[6] * (s - 1))
+            x, y = B("TAB", lo, lo + 4096), [B("TAB", 16, TW), B("LZ")] + [B("TAB", 2 * TW + 16, 3 * TW)] * (s - 2)
+            load([half(x, 0)], y, T.TAB[0:128 - k, lo:lo + 4096], T.TAB[k:128, 16:TW], DUE[6])
+            load([half(x, 1)], y, T.TAB[128 - k:128, lo:lo + 4096], T.TAB[0:k, 16:TW], DUE[6])
 
     lead[0] = 1000.0
+    iota(col(0), [[1, 1]], 0, 1)
+    lead[0] = -2000.0
+    fill(col(15), 63 * math.log(2.0) + math.log(2.5))
+    act(col(16), col(0), AF.Exp, -math.log(2.0), col(15))
+    lead[0] = 1000.0
     iota(B("II", 0, 1), [[1, 1]], 0, 1)
+    iota(B("AS"), [[-8, 4], [-32, 128]], -5, 0)
     iota(B("FF"), [[1, 132]], 0, 0)
     iota(B("FX"), [[0, 8], [1, 16]], 0, 0)
     iota(B("FG"), [[1, 8], [0, 16]], 0, 0)
@@ -474,109 +661,110 @@ def rank_program(g, core, T, topo):
     iota(B("T19", 0, NV_), [[1, 8], [0, SEG]], 0, 0)
     iota(B("EXI", 0, 8), [[1, 4], [4, 2]], 0, 0)
     iota(B("EXI", 8, 24), [[8, 2], [24, 4], [1, 2]], 2 * rank + 8, 0)
-    iota(B("EXI", 24, 30), [[1, 3], [4, 2]], 9, 0)
-    iota(B("EXI", 30, 32), [[4, 2]], 8, 0)
     fill(B("SU", 128, 4 * UW), 0.0)
-    copy(B("EXV"), B("EXI"))
+    copy(B("EXV", 0, 24), B("EXI", 0, 24))
     ts(B("II", 1, 2), B("II", 0, 1), 15, OP.bitwise_and)
     ts(B("II", 2, 3), B("II", 0, 1), 4, OP.logical_shift_right)
-    copy(B("COL", 0, 3), B("II", 0, 3))
+    copy(B("COL", 1, 3), B("II", 1, 3))
     fill(B("RST"), 1.0)
     fill(B("RST", 0, 16 * CH, 16), 0.0)
     BO = B("BO", 0, 128)
     ts(BO, B("FG"), col(2), OP.is_equal)
     act(B("BO", 128, 256), BO)
     ts(B("MSK"), B("FX", 0, 128), col(1), OP.is_equal)
-    ts(col(12), col(1), -1.0, OP.mult, 15.0, OP.add)
-    ts(B("TMP"), B("FX", 0, 128), col(12), OP.is_equal)
-    tt(third("REV", 0), BO, B("TMP"), OP.mult)
-    act(third("REV", 1), third("REV", 0))
-    IDF, BLK = third("PI", 0), eight("GF", 0)
+    act(col(12), col(1), AF.Identity, -1.0, 15.0)
+    act(col(3), col(2), AF.Identity, 16.0, col(12))
+    ts(third("RG", 0), B("FF", 0, 128), col(3), OP.is_equal)
+    mov("RG", third("RG", 1), third("RG", 0))
+    IDF, BLK = third("PI", 0), B("GF")
     ts(IDF, B("FF", 0, 128), col(0), OP.is_equal)
     act(third("PI", 1), IDF)
     act(B("IDN"), IDF)
     act(B("IDU"), IDF, AF.Copy, 1.0 / UNIT)
-    for h in range(2):
-        ts(eight("GF", h), B("FF", 0, 8), col(2), OP.is_equal)
+    ts(BLK, B("FF", 0, 8), col(2), OP.is_equal)
     act(B("GS"), BLK)
     act(eight("GB", 0), BLK, AF.Copy, 4.0)
     act(eight("GB", 1), BLK, AF.Copy, UNIT)
     act(B("GU"), BLK, AF.Copy, 1.0 / UNIT)
-    ts(B("EXL"), B("FF", 0, 8), float(SEG), OP.mult, SEG - 1.0, OP.add)
+    ts(B("EXL"), B("FF", 0, 8), 1.0 if ZF else float(SEG), OP.mult, 0.0 if ZF else SEG - 1.0, OP.add)
     ts(col(4), col(1), 0.0, OP.is_gt)
     ts(col(8), col(1), 13.0, OP.is_ge)
-    ts(col(9), col(1), -4.0 * 2 ** 19, OP.mult, 32.5 * 2 ** 19, OP.add)
-    for m in range(3):
-        act(third("BIAS", m), B("MSK"), AF.Identity, 512.0, -512.0)
-    copy(B("PG"), B("PI"))
+    act(col(9), col(1), AF.Identity, -4.0 * 2 ** 19, 32.5 * 2 ** 19)
+    act(B("BIAS"), B("MSK"), AF.Identity, 512.0, -512.0)
+    mov("PG", B("PG"), B("PI"))
     ts(col(17), col(1), 3.0, OP.is_lt)
     ts(B("CAI"), B("FF", 0, 8), col(1), OP.add, 1.0, OP.add)
     ts(B("CAI"), B("CAI"), 3, OP.bitwise_and)
     ts(B("CA"), B("CAI"), 8.0, OP.mult, 5.0, OP.add)
-    ts(B("CA"), B("CA"), col(17), OP.mult)
-    for c in range(4):
-        act(third("KC", c), B("FF", 0, 128), AF.Identity, col(8), B("CA", (c + 3) & 3, ((c + 3) & 3) + 1))
+    ts(B("CA"), B("CA"), col(17), OP.mult, isx(8), OP.add)
     for m in range(3):
         ts(col(20 + m), isx(15 - m), -32.0, OP.mult, isx(m), OP.subtract)
         act(third("MA", m), BO, AF.Copy, col(20 + m))
         act(third("SEL", m), BO, AF.Copy, isx(15 - m))
-    IL = B("IL")
-    ts(IL, B("FF", 0, 8), 16.0, OP.mult, col(1), OP.add)
     act(B("IXP"), IDF, AF.Copy, col(4))
-    copy(B("RG"), B("REV"))
-    ts(col(7), col(0), 4096.0 * UNIT, OP.mult, -1.0, OP.add)
+    act(col(7), col(0), AF.Identity, 4096.0 * UNIT, -1.0)
     act(B("NONE"), B("FF", 0, 8), AF.Identity, 0.0, col(7))
-    fill(col(14), 63 * math.log(2.0))
-    fill(col(15), 63 * math.log(2.0) + math.log(2.5))
-    act(B("W8"), IL, AF.Exp, -math.log(2.0), col(14))
-    act(col(16), col(0), AF.Exp, -math.log(2.0), col(15))
-    for c in range(8):
-        act(eight("WG", c), BLK, AF.Copy, B("W8", c, c + 1))
+    act(col(14), col(1), AF.Identity, -math.log(2.0), 63 * math.log(2.0))
+    iota(B("W8", 0, 64), [[16, 8], [0, 8]], 0, 0)
+    iota(B("W8", 64, 128), [[0, 8], [1, 8]], 0, 0)
+    act(B("W8", 0, 64), B("W8", 0, 64), AF.Exp, -math.log(2.0), col(14))
+    ts(B("W8", 64, 128), B("W8", 64, 128), col(2), OP.is_equal)
+    tt(B("WG"), B("W8", 0, 64), B("W8", 64, 128), OP.mult)
     t19 = B("T19")
     ts(t19, t19, col(2), OP.is_equal)
     for k in (0, SEG - 2, SEG - 1):
-        fill(B("T19", k, NV_, SEG), 0.0)
-    ts(col(11), isx(0), -4.0, OP.mult)
+        put(B("T19", k, NV_, SEG), 0.0)
+    act(col(11), isx(0), AF.Copy, -4.0)
     act(B("NEGV"), t19, AF.Copy, col(11))
     fill(B("CD"), -2.0)
-    fill(B("CD", 0, 6 * NV_, SEG), 2.0)
-    fill(B("CD", SEG - 1, 6 * NV_, SEG), 0.0)
+    put(B("CD", 0, 6 * NV_, SEG), 2.0)
+    put(B("CD", SEG - 1, 6 * NV_, SEG), 0.0)
+    act(B("COL", 23, 26), B("MSK", 13, 16), AF.Copy, 4096.0 * UNIT)
     for m in range(3):
         act(seg("CD", 2 * m + 1), B("SLOT"), AF.Identity, 0.125, (-33.0 - m) / 32)
-        fill(B("CD", NV_ * (2 * m + 1) + SEG - 2, NV_ * (2 * m + 2), SEG), 0.0)
+        put(B("CD", NV_ * (2 * m + 1) + SEG - 2, NV_ * (2 * m + 2), SEG), -1.0 if "FS" in ON else 0.0)
+        if m == 2 and ZF:
+            put(B("CD", 4 * NV_ + SEG - 1, 5 * NV_, SEG), -2.0)
         if m == 1:
-            fill(B("CD", 2 * NV_ + SEG - 1, 3 * NV_, SEG), -2.0)
-        ts(col(23 + m), isx(15 - m), 4096.0 * UNIT, OP.mult)
-        act(seg("QX", m), t19, AF.Copy, col(23 + m))
-    act(B("VR", 0, 640), B("RST", 0, 640))
+            put(B("CD", 2 * NV_ + SEG - 1, 3 * NV_, SEG), -2.0)
+        act(seg("QX", m), t19, AF.Copy, col(25 - m))
+    act(col(18), isx(8), AF.Copy, -8192.0)
+    act(seg("QX", 3), t19, AF.Copy, col(18))
     act(B("PSELA"), ahead("BO", 1), AF.Copy, 0.5)
     ts(col(6), col(1), 2.0, OP.is_lt)
-    act(B("POLDA"), B("PSELA"), AF.Copy, col(6))
-    fill(B("PSEL"), 0.0)
+    put(B("PSEL"), 0.0)
     act(B("PSEL", 0, 128, 16), B("PSELA", 0, 128, 16))
     act(B("POLD"), B("PSEL"), AF.Copy, col(6))
-    ts(col(13), isx(0), 16.0, OP.mult, col(1), OP.add)
-    ts(B("TMP"), B("FX", 0, 128), 1.0, OP.add, col(13), OP.is_equal)
-    tt(B("TMP"), B("TMP"), B("MSK"), OP.subtract)
-    tt(B("DIF"), B("TMP"), BO, OP.mult)
-    fill(B("DIF", 0, 128, 16), 0.0)
-    ts(B("II", 3, 4), B("II", 2, 3), 1, OP.bitwise_and)
-    ts(B("II", 4, 5), B("II", 2, 3), 1, OP.logical_shift_right)
-    copy(B("COL", 28, 30), B("II", 3, 5))
-    ts(col(28), col(28), 16.0, OP.mult, col(12), OP.add)
-    ts(col(28), col(28), 4.0, OP.mult, 3.0, OP.add)
-    ts(B("U19"), B("FF", 0, 132), col(28), OP.is_equal)
-    ts(B("ZT", 8, 12), B("FF", 0, 4), col(29), OP.is_equal)
-    for r in range(N):
-        ts(B("HOME", 132 * r, 132 * r + 132), B("U19"), B("ZT", 8 + r, 9 + r), OP.mult)
-    iota(B("TMP"), [[8, 2], [0, 16], [1, 4]], 0, 0)
-    ts(col(27), B("II", 3, 4), 8.0, OP.mult, 3.0, OP.add)
-    fill(B("HV"), 0.0)
-    for r in range(N):
-        ts(B("HV", 132 * r, 132 * r + 128), B("TMP"), col(27), OP.is_equal, B("ZT", 8 + r, 9 + r), OP.mult)
-    fill(B("WV", 0, 512, 4), -2047.0)
+    act(col(13), isx(0), AF.Identity, 16.0, col(0))
+    ts(B("TMP"), B("FF", 1, 129), col(13), OP.is_equal)
+    tt(B("DIF"), B("TMP"), IDF, OP.subtract)
+    put(B("DIF", 0, 128, 16), 0.0)
+    for k, o in enumerate(ops):
+        if o["eng"] == "g" and o["kind"] == "c" and o["step"][1][:2] in ("II", "CO", "FF", "FG", "FX", "AS"):
+            ops[posts[0]]["pre"][k] = None
     MID = (EMPTY - 2 * LOW - 1) / 2
-    fill(col(10), -MID)
+
+    def closing(t):
+        if t == 0:
+            ts(B("II", 3, 4), B("II", 2, 3), 1, OP.bitwise_and)
+            ts(B("II", 4, 5), B("II", 2, 3), 1, OP.logical_shift_right)
+            copy(B("COL", 28, 30), B("II", 3, 5))
+            act(col(27), col(2), AF.Identity, 4.0, 3.0)
+            act(col(26), col(12), AF.Identity, 4.0, 3.0)
+            act(col(26), col(28), AF.Identity, 64.0, col(26))
+            iota(B("U19", 0, 64), [[0, 2], [1, 32]], 0, 0)
+            put(col(10), -MID)
+        if t == 1:
+            fill(B("HV"), 0.0)
+            ts(B("HV", 0, 64), B("U19", 0, 64), col(27), OP.is_equal)
+            mov("HOME", B("HP"), B("HV"), isx(0))
+            fill(B("WV", 0, 512, 4), -2047.0)
+            fill(B("WV", 3, 512, 4), 0.0)
+        if t == 2:
+            ts(B("ZT", 8, 12), B("FF", 0, 4), col(29), OP.is_equal)
+            ts(B("U19"), B("FF", 0, 132), col(26), OP.is_equal)
+            for r in range(N):
+                mov("HOME", B("HOME", 132 * r, 132 * r + 132), B("U19"), B("ZT", 8 + r, 9 + r))
 
     FLAG = (1 << 26) | 4095
 
@@ -588,10 +776,13 @@ def rank_program(g, core, T, topo):
         for lo in range(0, 128, n):
             o = 128 * "012S".index(tag) + lo
             xi, xj = B("XI", o, o + n), B("XJ", o, o + n)
-            tt(xi, s if halves == 1 else part(s, lo, lo + n), part(a, lo, lo + n), OP.mult)
+            if s:
+                tt(xi, s if halves == 1 else part(s, lo, lo + n), part(a, lo, lo + n), OP.mult)
             ts(xj, xi, 721635.0 - 4096.0 * (8 * c + 5), OP.add)
             ts(xi, xj, 5, OP.arith_shift_right, FLAG, OP.bitwise_and)
             ts(B("OFF", o, o + n), xi, -1.0, OP.mult, TW - 1.0, OP.add)
+            if seen["cycle"] < 0:
+                mark("OFF%d" % seen["vOFF"])
 
     def place(tag, k, lo=0, hi=128):
         m = 2048 * "012S".index(tag)
@@ -601,8 +792,8 @@ def rank_program(g, core, T, topo):
         a = 128 * "012S".index(tag)
         for eng, n in pieces:
             x = B("X", 16 * a, 16 * (a + n))
-            turn(t, ("gather" if eng == "s" else "help") + tag)
-            gat(eng, x, tab, B("OFF", a, a + n))
+            turn(t, ("help" if eng == "v" else "gather") + tag)
+            gat(("vs" if eng == "v" else "sv")[:1 + FLEX], x, tab, B("OFF", a, a + n))
             turn(t, "scan" + tag)
             scan(x, B("RST", 0, 16 * n), x, OP.mult, OP.max)
             a += n
@@ -618,32 +809,31 @@ def rank_program(g, core, T, topo):
         return (T[x[1]][rows(r), x[2]:x[3]],) + x[1:]
 
     turn(-3, "end")
-    ts(B("BG"), B("RAW0"), -2047.0, OP.add, 0.125, OP.mult)
+    mov("BG", B("BG"), B("BF"), 0.125, (LOW - 2047.0) / 8)
     for s in (1, 2, 3, 0):
         o = third(("b7", "b0", "b1", "b2")[s], 0)
         for q in range(4):
             mm(o, some(ahead("PG", (q - peer(s)) % N), peer(s)), some(third("BG", q), peer(s)), q == 0, q == 3)
-        copy(B("SU" if s else "LB", UW * peer(s), UW * peer(s) + 128), o)
-    for c in (0, 3, 1, 2):
+        mov("SU", B("SU" if s else "LB", UW * peer(s), UW * peer(s) + 128), o)
+    for c in range(3):
         tag = "S012"[c]
         bank = "b%d" % (3 + c)
         when = (-5, -3, -3, -4)[c]
         turn(when, "index" + tag if c else "names")
-        mm(third(bank, 2), third("MA", 0), third("KC", c))
-        index(tag, B("BF", c, 512, 4), third(bank, 2), c)
-        look(when, tag, FIRST[c], B("TAB0"))
-        if c < 3:
-            mm(third(bank, 1), BO, place(tag, 15))
-            act(third("VH", c), third(bank, 1))
+        index(tag, B("BF", c, 512, 4), third("AS", c), c)
+        look(when, tag, FIRST[c], window(0))
+        mm(third(bank, 1), BO, place(tag, 15))
+        act(third("VH", c), third(bank, 1))
         mm(B(bank, 0, 8), place(tag, 15), B("GS"))
-        if c in (1, 2):
-            copy(eight("ZH", c), B(bank, 0, 8))
-            continue
-        for h in range(2):
-            ts(B("SU", 128 + 2 * (c // 3) + h, 4 * UW, UW), B(bank, h, 8, 2), -2047.0, OP.add)
         if c:
+            copy(eight("ZH", c), B(bank, 0, 8))
+        else:
+            for h in range(2):
+                ts(B("SU", 128 + h, 4 * UW, UW), B(bank, h, 8, 2), -2047.0, OP.add)
             send3(lambda s: B("LB", UW * rank, UW * rank + UW), lambda s: B("SU", UW * peer(s), UW * peer(s) + UW), "u", DUE[11])
+            mark("u")
             copy(B("LB", UW * rank + 128, UW * rank + UW), B("SU", UW * rank + 128, UW * rank + UW))
+            lands()
 
     def names(t, si, old, v, pool=None):
         turn(t, "names")
@@ -653,8 +843,8 @@ def rank_program(g, core, T, topo):
             mm(third("b1", 3), IDF, B("PL0"), True, False)
         mm(third("b1", 3), B("IXP"), old, False, True)
         mov("SI", si, third("b1", 3))
-        mov("KS", B("KS"), v, 1.0, LOW + 13.0 * max(t, 0))
-        tt(B("KT"), B("KS"), old, OP.add)
+        mov("KS", third("b0", 3), v, 1.0, LOW + 13.0 * max(t, 0))
+        tt(B("KT"), third("b0", 3), old, OP.add)
         ts(B("KI"), B("KT"), 127, OP.bitwise_and)
         ts(B("KB"), B("KI"), col(8), OP.mult, B("CA", max(t, 0), max(t, 0) + 1), OP.add)
 
@@ -666,7 +856,8 @@ def rank_program(g, core, T, topo):
             mm(third("b0", m), third("MA", m), kb)
         turn(t, "lists")
         x = B("b3", 128 * lo, 128 * hi)
-        mm(x, B("IDN"), B("BIAS", 128 * lo, 128 * hi), True, False)
+        for m in ms:
+            mm(third("b3", m), B("IDN"), B("BIAS"), m == lo, False)
         for m in ms:
             mm(third("b3", m), kb, third("SEL", m), False, m == ms[-1])
         if "KM" in ON:
@@ -690,19 +881,28 @@ def rank_program(g, core, T, topo):
                 ts(x, third("KRB", m), B("LF", m * 8 + c, m * 8 + c + 1), OP.is_equal)
                 mm(eight("b7", m), x, eight("WG", c), c == 0, c == 7)
         turn(t, "firsts")
-        act(B("FS", 8 * ms[0], 8 * ms[-1] + 8), B("b7", 8 * ms[0], 8 * ms[-1] + 8), AF.Sign, -1.0, col(16))
+        o, x = B("FS", 8 * ms[0], 8 * ms[-1] + 8), B("b7", 8 * ms[0], 8 * ms[-1] + 8)
+        if "FS" in ON:
+            ts(o, x, col(16), OP.is_lt, 2.0, OP.mult)
+        else:
+            act(o, x, AF.Sign, -1.0, col(16))
+        mark("F%d" % t if t <= 0 else "F", 15.5 * max(t, 0))
 
     def verdict(t, m, v, best):
         bank = "b%d" % (4 + m)
         turn(t, "value%d" % m)
-        gat(eng("VJ%d" % m), third("VJ", m), v, eight("VL", m))
+        o, ls = third("VJ", m), eight("VL", m)
+        op(eng("VJ%d" % m), [o], [v, ls], lambda e: V.tensor_scalar(o[0], ind(v, ls), -2048.0, None, OP.add) if e == "v"
+           else S_.activation(o[0], ind(v, ls), AF.Identity, bias=-2048.0), 0.06 + 128 * CYC * GAT)
         d, c = seg(bank, 0), seg(bank, 1)
         mm(B(bank, 0, 2 * NV_), B("IDN"), B("CD", 2 * NV_ * m, 2 * NV_ * (m + 1)), True, False)
         mm(c, B("KB"), seg("QX", m), False, False)
+        mm(d, B("KB"), seg("QX", 3), False, False)
         mm(d, third("VJ", m), B("NEGV"), False, False)
+        mark("V%d" % t if t <= 0 else "V", 15.5 * max(t, 0))
         turn(t, "verdict%d" % m)
 
-        for lo, hi in TILES if m == 2 else ((0, 128),):
+        for lo, hi in TILES if m == 2 else TILE1 if m else ((0, 128),):
             for k, x in enumerate(best if hi == 128 else ()):
                 mm(B(bank, SEG * k + SEG - 1, NV_, SEG * len(best)), IDF, x, False, False)
             for k in range(16):
@@ -718,18 +918,21 @@ def rank_program(g, core, T, topo):
     mov("WIN", B("OH"), third("b1", 0), 8.0, 2047.0 - LOW)
     names(-2, B("SH"), B("OH"), third("VH", 0), B("POTH"))
     spread(-2, (0, 1))
+    early = []
     for m in range(2):
         turn(-2, "index%d" % m)
         index(str(m), B("SH"), third("b0", m), 1 + m, HALVES[m])
-        look(-2, str(m), EARLY[m], B("TAB0"))
+        early.append(len(ops))
+        look(-2, str(m), EARLY[m], window(0))
     firsts(-2, (0, 1))
     tt(eight("ZH", 0), verdict(-2, 0, third("VH", 1), [B("NONE")]), verdict(-2, 1, third("VH", 2), []), OP.max)
+    mark("Z")
     share_out(B("ZH"), "LZ", "VB1", DUE[12])
     turn(-1, "names")
     for s in range(1, N):
         arrive3(B("LB", UW * peer(-s), UW * peer(-s) + UW), "u", s)
     windows()
-    for k in range(4):
+    for k in range(2):
         ts(B("LVA", 4 * k, 4 * k + 4), B("LB", 128 + k, 4 * UW, UW), 2047.0, OP.add)
     for q in range(4):
         for s in range(N):
@@ -738,15 +941,21 @@ def rank_program(g, core, T, topo):
                 ops[k]["pre"][k - 1] = True
 
     def values(c, via):
-        gat("s", third("VK", c), B("LZ" if c in (1, 2) else "LVA"), eight("EXV", c))
+        gat("s", third("VK", c), B("LZ") if c else B("LVA", 0, 8), eight("EXV", c))
         mm(via, third("VK", c), IDF)
         act(third("VR", 8 - c), via)
 
     for c in (0, 3, 1, 2):
         turn(0 if c else -1, "pool")
         mov("WIN", third("WIN", 8 - c) if c < 3 else B("NU"), B("b2", c, 512, 4), 8.0, 2047.0 - LOW)
-        if c in (0, 3):
-            values(c, third("b3", c % 2))
+        if c == 0:
+            values(0, third("b3", 0))
+        if c == 3:
+            mm(third("b6", 3), ahead("PI", N - 1), B("NU"))
+            mov("BACK", third("WIN", 5), third("b6", 3))
+            turn(0, "indexS")
+            index("S", third("WIN", 5), third("AS", 3), 3)
+            look(0, "S", FIRST[3], window(1))
 
     for t in range(RO):
         s = 1 + t % 3
@@ -754,41 +963,54 @@ def rank_program(g, core, T, topo):
         ms = (0, 1, 2) if t else (2,)
         si, old = third("WIN", 4 - t), third("WIN", 8 - t)
         names(t, si, old, third("VR", 8 - t), None if t else B("POTI"))
+        if t == 0 and LAP >= 0:
+            ops[early[1] + 2 * LAP]["pre"][len(ops) - 1] = False
         turn(t, "bundle2")
-        twin(B("S1"), si)
+        k = twin(B("S1"), si)
+        if t == 0:
+            ops[k]["pre"][sends["VB1"]] = None
         spread(t, ms)
+        turn(t, "pool")
+        dif = third("b7", 1)
+        mm(dif, B("DIF"), old)
+        mm(third("b1", 3), B("POLD"), old, True, False)
         turn(t, "back")
-        mm(third("b1", 0), ahead("PI", N - s), B("NU"))
         if t:
-            for k, n in enumerate(("WIN", "VR")):
-                mm(third("b1", 1 + k), ahead("PI", 1 + (t - 1) % 3), third(n, 6 - t))
-            mov("BACKV", third("VR", 6 - t), third("b1", 2))
-        k = 256 if t else 128
-        mov("BACK", B("WIN", 128 * (5 - t), 128 * (5 - t) + k), B("b1", 0, k))
+            mm(third("b2", 2), ahead("PI", 1 + (t - 1) % 3), third("VR", 6 - t))
+            mov("BACKV", third("VR", 6 - t), third("b2", 2))
+            mm(third("b2", 1), ahead("PI", 1 + (t - 1) % 3), third("WIN", 6 - t))
+            mm(third("b2", 0), ahead("PI", N - s), B("NU"))
+            mov("BACK", B("WIN", 128 * (5 - t), 128 * (7 - t)), B("b2", 0, 256))
         for m in ms:
             turn(t, "index%d" % m)
             index(str(m), si, third("b0", m), (t + 1 + m) & 3, HALVES[m])
             look(t, str(m), PIECES[m] if t else EARLY[m], window(s if m == 2 else 0))
         turn(t, "scanS")
-        mm(third("b0", 3), third("MA", 0), third("KC", t & 3))
-        if t:
-            mm(third("b3", 0), ahead("BO", N - s), place("S", 15))
-            mov("VR", third("VR", 5 - t), third("b3", 0))
+        mm(third("b3", 0), ahead("BO", N - s) if t else BO, place("S", 15))
+        mov("VR", third("VR", 5 - t), third("b3", 0))
         firsts(t, ms)
         turn(t, "pool")
         for c in () if t else (1, 2):
             values(c, third("b7", 1 + c))
-        dif = third("b7", 1)
-        mm(dif, B("DIF"), old)
-        mm(third("b1", 3), B("POLDA" if last else "POLD"), old, True, False)
         if t:
             tt(eight("ZT", 0), verdict(t, 0, third("VR", 7 - t), [B("NONE")]), verdict(t, 1, third("VR", 6 - t), []), OP.max)
-        verdict(t, 2, third("VR", 5 - t), [eight("ZT", 0)] if t else [B("LZ", 2 * rank + h, 96, 24) for h in range(2)])
+        if ZF:
+            for h in () if t else (0, 1):
+                copy(B("ZT", h, 8, 2), B("LZ", 2 * rank + h, 96, 24))
+            tt(B("ZF"), verdict(t, 2, third("VR", 5 - t), []), eight("ZT", 0), OP.max)
+        else:
+            verdict(t, 2, third("VR", 5 - t), [eight("ZT", 0)] if t else [B("LZ", 2 * rank + h, 96, 24) for h in range(2)])
         turn(t, "decide")
-        zq, zx, zm = seg("ZS", 2), B("ZX"), B("ZM")
+        zq, zx, zm = B("ZF") if ZF else seg("ZS", 2), B("ZX"), B("ZM")
+        seen.clear()
+        seen["cycle"] = t
         gat("s", zx, zq, B("EXL"))
         op("v", [zm], [zq, B("EXL"), B("MSK")], lambda e, zq=zq: V.tensor_tensor(T.ZM[:], zq[0].indirect(T.EXL[:]), T.MSK[:], OP.mult),
            0.06 + 128 * CYC * GAT)
+        mark("ZM", 15.5 * t)
+        behind.append(len(ops) - 1)
+        closing(t)
+        behind.pop()
         mm(B("b3", 440, 448), zm, B("GU"))
         z = third("b2", 3)
         mm(z, zx, B("IDU"))
@@ -802,14 +1024,16 @@ def rank_program(g, core, T, topo):
         act(B("KEEP"), z, AF.Sign, -1.0, col(9))
         ts(B("NJ"), B("NI"), 4095, OP.bitwise_and)
         gat(eng("NU"), nu, w, ls)
+        xs, a = third("XI", 3), third("AS", t & 3)
+        op("v", [xs], [w, ls, a], lambda e, w=w, a=a: V.tensor_tensor(xs[0], ind(w, ls), a[0], OP.mult), 0.06 + 128 * CYC * GAT)
         sca(wv, ls, B("NJ"))
         turn(t, "change")
         scamax(w, ls, B("S1"), B("KEEP1"))
         turn(t, "pass")
         tt(B("PP"), dif, B("KEEP"), OP.mult)
-        mm(third("b1", 3), B("PSELA" if last else "PSEL"), B("PP"), False, last)
+        mm(third("b1", 3), B("PSEL"), B("PP"), False, last)
         turn(t + 1, "indexS")
-        index("S", nu, third("b0", 3), t & 3, HALVES[3])
+        index("S", None, None, t & 3, HALVES[3])
         look(t + 1, "S", LAST if last else PIECES[3], window(0))
     turn(RO, "names")
 
@@ -821,48 +1045,53 @@ def rank_program(g, core, T, topo):
     def tile(s, lo, hi, step=1):
         return B(("b6", "b7", "b3", "b4")[s], lo, hi, step)
 
-    def home(s, k):
-        for q in range(4):
-            lo = 132 * peer(s) + 3 - q
-            x = (third("WV", q), B("WH", 512 + 32 * q, 544 + 32 * q), third("WH", q), place("S", 15, 32 * q, 32 * q + 32))[k]
-            o = (tile(s, 160, 288), tile(s, 128, 160), tile(s, 0, 128), tile(s, 160, 288, 4))[k]
-            mm(o, B("HV" if k == 3 else "HOME", lo, lo + 128), x, k + q == 0, k + q == 6)
-
     def plain(o, x, k):
         act(third("WA", k), x, AF.Abs, 1.0, col(10))
-        ts(o, third("WA", k), -1.0, OP.mult, MID + LOW - 2047.0, OP.add)
+        mov("WH%d" % k, o, third("WA", k), -1.0, MID + LOW - 2047.0)
 
-    mm(third("b5", 0), ahead("PI", s3), third("VR", 1))
     mm(third("b2", 0), ahead("PI", s3), third("WIN", 1))
     for c in range(1, 4):
-        ts(B("WV", c, 512, 4), third("VR", 4 - c) if c < 3 else third("b5", 0), -2047.0, OP.add)
+        mov("WV", B("WV", c, 512, 4) if c < 3 else third("WV", 4), third("VR", 4 - c), 1.0, -2047.0)
     plain(third("WH", 4), third("b1", 3), 4)
     for c in range(4):
         plain(B("WH", c, 512, 4), (B("NU"), third("WIN", 3), third("WIN", 2), third("b2", 0))[c], c)
     for k in range(4):
-        for s in (1, 2, 3, 0):
-            turn(RO, "names" if s else "end")
-            home(s, k)
+        for q in range(4):
+            x = (third("WV", q), B("WV", 512 + 32 * q, 544 + 32 * q), B("WH", 512 + 32 * q, 544 + 32 * q), place("S", 15, 32 * q, 32 * q + 32))[k]
+            o = (B("b5", 32, 160), B("b5", 35, 160, 4), B("b5", 0, 32), B("b5", 32, 160, 4))[k]
+            lo = 3 - q + (32 - 8 * s3) * (k == 1)
+            mm(o, B("HV" if k == 3 else "HP", lo, lo + 128), x, k + q == 0, k + q == 6)
+    for s in (1, 2, 3, 0):
+        turn(RO, "names" if s else "end")
+        for q in range(4):
+            lo = 132 * peer(s) + 3 - q
+            mm(tile(s, 0, 128), B("HOME", lo, lo + 128), third("WH", q), q == 0, q == 3)
+        mov("OU%d" % s, piece("OU" if s else "OUT", s, 0, 128), tile(s, 0, 128), 1.0, 0.0 if s else 2047.0)
+        mov("OV%d" % s, piece("OU" if s else "OUT", s, 128), B("b5", 0, 160), 1.0, 0.0 if s else 2047.0)
     turn(RO, "names")
-    for s in range(1, N):
-        ts(piece("OU", s), tile(s, 0, 288), 2048.0, OP.add)
-        if APART:
-            send(s, piece("LO", s), piece("OU", s), "w%d" % s, 3.0)
-    if not APART:
-        send3(lambda s: piece("LO", s), lambda s: piece("OU", s), "w", 5.0)
+    for to in CALLS:
+        tr = []
+        for i, s in enumerate(to):
+            en = topo.engines(core, T.cores[peer(s)])
+            en = en[i * len(en) // len(to):(i + 1) * len(en) // len(to)]
+            rid, pid = topo.addr(T.cores[peer(s)])[:2]
+            tr.append(RemoteDMATransfer(dst_ids=[DstId(rid=rid, pnc=pid)], dma_engine_mask=sum(1 << e for e in en),
+                                        remote_sem=T.sem["w%d" % s], srcs=[piece("OU", s)[0]], dsts=[piece("LO", s)[0]]))
+            sent[0] += len(en)
+        k = op("g", [], [piece("OU", s) for s in to], lambda tr=tr: g.remote_dma_fused(tr, local_sem=T.sem["snd"]), 2.0 + len(to), "rem")
+        for s in to:
+            sends["w%d" % s] = k
+            arrive(piece("LO", s), "w%d" % s, len(topo.engines(T.cores[peer(-s)], core)) // len(to))
+    mark("end")
     turn(RO, "end")
-    act(piece("OUT", 0), tile(0, 0, 288), AF.Identity, 1.0, 2047.0)
     for s in range(N):
         r = peer(-s)
         if s:
-            if APART:
-                arrive(piece("LO", s), "w%d" % s, len(topo.engines(T.cores[r], core)))
-            else:
-                arrive3(piece("LO", s), "w", s)
-            ts(piece("OUT", s), piece("LO", s), -1.0, OP.add)
-        dma("y", [], [piece("OUT", s)], T.yb[rows(r), :], piece("OUT", s, 0, 128)[0])
-        dma("s", [], [piece("OUT", s)], T.yv[2 * r:2 * r + 2, :], T.OUT[0:128:17, 288 * s + 160:288 * s + 288])
-        dma("s", [], [piece("OUT", s)], T.yp[2 * r:2 * r + 2, :], T.OUT[0:128:17, 288 * s + 128:288 * s + 160])
+            mov("OUT%d" % s, piece("OUT", s, 0, 128), piece("LO", s, 0, 128), 1.0, 2047.0)
+            mov("OUV%d" % s, piece("OUT", s, 128), piece("LO", s, 128), 1.0, 2047.0)
+        dma("y", [], [piece("OUT", s, 0, 128)], T.yb[rows(r), :], piece("OUT", s, 0, 128)[0])
+        dma("s", [], [piece("OUT", s, 128)], T.yv[2 * r:2 * r + 2, :], T.OUT[8 * rank:8 * rank + 8, 288 * s + 160:288 * s + 288])
+        dma("s", [], [piece("OUT", s, 128)], T.yp[2 * r:2 * r + 2, :], T.OUT[8 * rank:8 * rank + 8, 288 * s + 128:288 * s + 160])
     flush()
     for k in dmas:
         if known["y"].get(k, 0) < 16:

import math
from concourse.bass import DstId, RemoteDMATransfer
from concourse.mybir import AluOpType as OP, ActivationFunctionType as AF, AxisListType as AX

F, H, G, I, U = "float32", "bfloat16", "float16", "int32", "uint16"
RO = 5
CYC, PEC, WAKE, SELF, ISSUE, GAT, SCA, SLACK = 0.00083, 0.0008, 0.15, 0.2, 1.2, 1.45, 3.8, (0.2, 1.0, 1.4)
VFIX, CAP, PROP, PASSES = 0.02, 0.2, "vstgyr", 1
CALLS = ((1, 2), (3,))
FLEX = 0
ORDER, MOVES, HEAT, MEAN = {}, 0, 0.05, 0.5
TRIES, SHAKE, PLANNED, TAIL = 0, 0.3, [], 1
CH = 64


def _cut(s):
    return tuple(tuple((x[0], int(x[1:])) for x in p.split()) for p in s.split(","))


_E = ["EB%d" % _m for _m in range(25)]
STEPS = {"v": ("ZM1 ZI1 ZI2 NI1 LST1 KEEP11 XI1 NJ1 XJ1 PP1 XI2 XJ2 OFF1 VR1 XI3 WIN1 OFF2 KT1 X1 KI1 KB1 X2 XI4 XI6 XJ3 KM1 XI5 XJ4 OFF3 XI7 XI8 "
               "VL1 OFF4 XJ5 EB1 X3 XI9".split() + _E[2:8] + ["OFF5"] + _E[8:23]
               + "X7 EB23 X4 EB24 X10 X5 FS1 X6 X8 X9 X11 X12 ZS1 X13 X14 ZS2 CODE1 ZT1 ZS3 ZF1".split(), []),
         "s": ("ZX1 KEEP1 NU1 X1 b01 X2 WIN1 X3 KRB1 LF1 X4 VR2 VR1 X5 VJ2 X6 VJ3 VJ1 X7 X8 CODE1 X9 X10 WIN2 CODE2".split(), [])}
ZF, LAP = 1, -1
TILE1 = ((0, 128),)
TILES = ((0, 96), (96, 128))
SOON, AFTER, STAGE = 1, 3, (0, 1, 2, 3)
DUE = (6.2, 6.0, 8.0, 11, 10.5, 1.0, 7.0, 2.7, 3, 1.5, 3.7, 4, 1.5)
PIECES = _cut("s64 s64, s64 v32 s32, v48 s48 s16 s16, s32 s32 s64")
FIRST = _cut("s48 v32 s48, s64 s64, s64 s64, s32 v64 v24 v8")
EARLY = _cut("v40 s56 s24 s8, s64 s24 v40, s40 s8 v48 s32")
LAST = _cut("v8 s32 v40 s16 v32")[0]
HALVES = (1, 1, 1, 2)
ON = "KM SU RG OUT3 CODE2 FS OUV1 OU0 OV3".split()
TURNS = "names index0 gather0 lists index1 code0 scanS helpS verdict0 indexS value0 decide scan2 scan0 value2 back index2 bundle2 gather2 first2 pass change scan1 value1 pool gather1 verdict1 help2 verdict2 gatherS first1 firsts first0 code2 help0 help1 rows code1 end".split()
BY = {}
HANDS, HANDED = 2, ["30", "31", "21"]
LOADS = (("R", 3.0), ("30", 3.0), ("10", 3.5), ("T", 6.5), ("31", 7.5), ("11", 8), ("21", 8.5), ("20", 9.0))
POSTS = (("30", 10.0), ("10", 5.0), ("31", 9.0), ("p", 4.0), ("11", 6.0), ("21", 8.0), ("20", 5.0))
LANDS = ("10", "p", "30", "11", "31", "20", "21")
AFTER, SOON, PASSES = 3, 8, 2
DUE = (2.5, 0, 0, 0, 0, 0, 6.0, 0, 0, 0, 3.5, 6, 6)
FIRST = _cut("v48 v16 s64, s32 s32 s64, s64 v8 v56, s64 v48 s8 v8")
EARLY = _cut("s64 s64, s32 s48 s48, s64 v32 s24 s8")
LAST = _cut("v24 s24 v16 s24 v8 v32")[0]
ON = "KM SU RG OU0 OUT2 OUT3 OV0 OU2 CODE2 FS".split()
TURNS = "firsts index2 back index1 names lists first2 rows verdict0 first0 value1 change decide value2 code2 pool gather2 indexS helpS gather1 verdict1 scanS pass gatherS value0 help0 help2 gather0 verdict2 scan2 code0 scan0 index0 help1 first1 bundle2 scan1 code1 end".split()
HANDED = []
LOADS = (("10", 2.0), ("R", 2.9), ("11", 3.3), ("T", 7.2), ("20", 7.6), ("21", 8.0), ("30", 8.4), ("31", 8.8))
POSTS = (("10", 6.5), ("11", 5.0), ("p", 5.0), ("20", 5.5), ("21", 7.0), ("30", 7.5), ("31", 9.0))
LANDS = ("10", "11", "p", "20", "21", "30", "31")
AFTER, PASSES = 5, 1
CYC, PEC, WAKE, SELF, VFIX, GAT, SCA = 0.0009, 0.00046, 0.2, 0.23, 0.005, 1.35, 2.2
DUE = (2.5, 0, 0, 0, 0, 0, 6, 0, 0, 0, 4.0, 5.0, 4.5)
FIRST = _cut("v48 v16 s64, s8 s16 s40 s64, v8 s64 v56, v32 s64 v32")
EARLY = _cut("s64 s64, s32 s48 s48, s64 v32 s24 s8")
STEPS, ZF, SLACK, CAP = {}, 0, (0.1, 0.8, 2.0), 0.5
PIECES = _cut("s16 s64 s48, v32 v40 s56, v32 s64 s32, s16 s48 s16 v16 s32")
HALVES = (2, 2, 1, 2)
ON = "KM VJ1 SU RG OU0 OUT2 OUT3 OV0 OU2".split()
TURNS = "first2 index2 help2 bundle2 verdict0 back value2 value1 gather0 gather2 firsts code2 first1 decide scan0 help0 names verdict1 scan1 gather1 first0 help1 value0 rows pass index0 verdict2 scan2 code1 pool lists gatherS indexS change index1 helpS code0 scanS end".split()
PASSES = 1
TILES, SLACK, CAP = ((0, 64), (64, 96), (96, 128)), (0.1, 0.6, 2.2), 0.55
PIECES = _cut("s32 s64 s32, v48 s40 s40, v48 s24 s24 v16 s16, s16 s48 v16 s48")
FIRST = _cut("v56 v8 s64, s8 s16 s40 s64, v8 v56 s64, v32 s64 v32")
EARLY = _cut("s64 v64, v16 s16 s64 s32, s64 v32 s24 v8")
LAST = _cut("s8 s24 s40 v40 v16")[0]
HALVES = (2, 1, 1, 2)
ON = "KM RG OUT3 OU2 WH0 WH1 OU3 OUT1 OUT2 OV3 PG".split()
TURNS = "first2 help0 help2 bundle2 verdict0 gatherS index0 back value2 index1 first1 decide first0 code2 gather2 help1 helpS gather0 rows code1 code0 names scan0 change scan2 indexS value1 gather1 verdict2 verdict1 scan1 firsts pool scanS lists index2 pass value0 end".split()
SEG = 19
NV_ = 8 * SEG
UNIT = 2.0 ** -24
TW = 4112
EMPTY = 0x3FFFF
LOW = 3948.0

SCRATCH = {}


def _sb(name, w, d):
    SCRATCH[name] = ("sbuf", [128, w], d)


_sb("TAB", 4 * TW, H)
for _m, _k, _w, _d in (("T", 8, 512, H), ("P", 4, 2, I)):
    SCRATCH["D" + _m] = ("dram", [_k, 128, _w], _d)
    SCRATCH["L" + _m] = ("dram", [_k, 128, _w], _d)
_sb("RAW0", 512, I)
for _m, _w in (("LVA", 16), ("ZH", 24), ("LZ", 96), ("VH", 384), ("VK", 512), ("OH", 128), ("SH", 128)):
    _sb(_m, _w, F)
_sb("POTH", 128, I)
_sb("EXI", 32, I)
_sb("EXV", 32, U)
UW = 136
_sb("SU", 4 * UW, G)
_sb("LB", 4 * UW, G)
_sb("BG", 512, G)
_sb("AS", 512, F)
_sb("RG", 256, G)
_sb("POTI", 128, I)
_sb("PL0", 128, F)
_sb("BF", 512, F)
_sb("KC", 512, H)
_sb("WIN", 1152, F)
_sb("VR", 1152, F)
_sb("NU", 128, F)
_sb("XI", 512, I)
_sb("XJ", 512, I)
_sb("OFF", 512, U)
_sb("X", 8192, H)
_sb("RST", 16 * CH, H)
for _m in ("S1", "KEEP1", "PP", "ZM", "ZX", "TMP", "MSK", "DIF", "PSEL", "POLD", "PSELA", "POLDA", "IXP", "KS", "IDU"):
    _sb(_m, 128, F)
for _m in ("KT", "KI", "NI", "NJ"):
    _sb(_m, 128, I)
_sb("KB", 128, H)
_sb("KRB", 384, H)
_sb("KM", 384, H)
_sb("LF", 24, H)
_sb("VL", 24, U)
_sb("FS", 24, H)
_sb("VJ", 384, G)
_sb("EB", 3072, H)
_sb("CODE", 3 * NV_, F)
_sb("ZS", 3 * NV_, F)
_sb("ZI", 16, I)
_sb("ZT", 32, F)
_sb("ZF", 8, F)
for _m in ("LST", "EXL"):
    _sb(_m, 8, U)
_sb("WA", 640, F)
_sb("WH", 768, G)
_sb("HOME", 4 * 132, G)
_sb("HV", 160, H)
_sb("HP", 160, G)
_sb("WV", 640, G)
_sb("OU", 4 * 288, G)
_sb("LO", 4 * 288, G)
_sb("OUT", 4 * 288, F)
_sb("II", 8, I)
_sb("FF", 132, F)
_sb("FX", 128, F)
_sb("FG", 128, F)
_sb("SLOT", NV_, F)
_sb("T19", NV_, F)
_sb("U19", 132, F)
_sb("NEGV", NV_, G)
_sb("CD", 6 * NV_, H)
_sb("QX", 4 * NV_, H)
_sb("COL", 32, F)
_sb("CA", 8, F)
_sb("CAI", 8, I)
_sb("W8", 128, F)
_sb("WG", 64, H)
_sb("BO", 256, H)
_sb("PI", 256, F)
_sb("IDN", 128, H)
_sb("BIAS", 128, H)
_sb("PG", 256, G)
_sb("KEEP", 128, H)
_sb("GF", 8, F)
_sb("GS", 8, H)
_sb("GB", 16, H)
_sb("G0", 16, F)
_sb("GU", 8, F)
_sb("SEL", 384, H)
_sb("MA", 384, H)
_sb("IL", 8, F)
_sb("NONE", 8, F)
for _m in range(8):
    SCRATCH["b%d" % _m] = ("psum", [128, 512], F)

SEMAPHORES = ["cv", "cs", "ct", "cg", "snd", "u1", "u2", "u3", "w1", "w2", "w3", "p1", "p2", "p3", "VB1"]
SEMAPHORES += [_m + _s + _k for _m in "th" for _s in "123" for _k in "01"]
SEMAPHORES += ["d%d" % _m for _m in range(90)]
TWO = (H, G, U)


def hands(core, topo):
    return [c for c in topo.cores_of(core) if topo.die(c) != topo.die(core)][:HANDS]


def hand_on(g, core, T, topo):
    N = len(T.cores)
    for rank, c in enumerate(T.cores):
        if core in hands(c, topo):
            sent = 0
            for x in HANDED[hands(c, topo).index(core)::HANDS]:
                r, k = (rank + int(x[0])) % N, int(x[1])
                to = T.cores[r]
                g.wait_ge(T.sem["h" + x], len([e for e in topo.engines(c, core) if e not in topo.engines(c, to)]))
                rid, pid = topo.addr(to)[:2]
                g.remote_dma(T.LT[2 * rank + k], T.DT[2 * r + k], T.sem["t" + x], T.sem["snd"], pid, rid, topo.mask(core, to))
                sent += len(topo.engines(core, to))
            g.wait_ge(T.sem["snd"], sent)


def rank_program(g, core, T, topo):
    rank = T.rank_of(core)
    if rank is None:
        return hand_on(g, core, T, topo)
    N = len(T.cores)
    Q = {"v": g.vector, "s": g.scalar, "t": g.tensor, "g": g, "y": g.sync}
    ops = []
    acc = {}
    cnt, clk = {}, {}
    lead = [-1000.0]
    known = {e: {} for e in Q}
    seen = {"cycle": -1}
    marks = {}

    def mark(name, late=0.0):
        if name in BY:
            marks[len(ops) - 1] = BY[name] + late
    behind = []

    def psum(n):
        return n[0] == "b" and len(n) == 2

    def op(eng, outs, ins, call, cost, kind="c", sem=None, inc=1, extra=()):
        k = len(ops)
        pre = {}
        for j in list(extra) + behind:
            pre[j] = False
        for wr, lst in ((True, outs), (False, ins)):
            for (_, n, lo, hi) in lst:
                for (alo, ahi, aw, ae, j) in acc.get(n, []):
                    if psum(n) and ae == "t" and eng == "t":
                        pre.setdefault(j, False)
                    elif (psum(n) and (ae != eng or len(eng) > 1)) or (alo < hi and lo < ahi and (aw or wr)):
                        pre[j] = True
        for wr, lst in ((False, ins), (True, outs)):
            for (_, n, lo, hi) in lst:
                a = acc.setdefault(n, [])
                if psum(n) and eng == "t":
                    a[:] = [x for x in a if x[3] == eng]
                if wr:
                    a[:] = [x for x in a if not (lo <= x[0] and x[1] <= hi)]
                a.append((lo, hi, wr, eng, k))
        name = outs[0][1] if outs else ""
        seen[eng[0] + name] = seen.get(eng[0] + name, 0) + 1
        ops.append({"step": (seen["cycle"], name + str(seen[eng[0] + name])), "eng": eng, "call": call, "cost": cost + (VFIX if eng == "v" else 0.0), "pre": pre, "kind": kind, "sem": sem, "inc": inc, "lead": lead[0]})
        return k

    def learn(eng, tk):
        Q[eng].wait_ge(T.sem[tk[0]], tk[1])
        for s, v in clk[tk].items():
            if known[eng].get(s, 0) < v:
                known[eng][s] = v

    def need(eng, toks):
        toks = sorted(toks)
        for tk in toks:
            if known[eng].get(tk[0], 0) >= tk[1]:
                continue
            if any(o != tk and clk[o].get(tk[0], 0) >= tk[1] and known[eng].get(o[0], 0) < o[1] for o in toks):
                continue
            learn(eng, tk)
        for tk in toks:
            if known[eng].get(tk[0], 0) < tk[1]:
                learn(eng, tk)

    def flush():
        n = len(ops)
        for e in STEPS:
            for t in range(RO):
                mine = {o["step"][1]: k for k, o in enumerate(ops) if o["step"][0] == t and o["eng"][0] == e}
                row = [mine[x] for x in STEPS[e][t == RO - 1] if x in mine]
                for j, k in zip(row, row[1:]):
                    ops[k]["pre"].setdefault(j, False)
        pre = [[(j, (SELF if ops[j]["eng"][0] == o["eng"][0] else WAKE) if w else None if w is None else 0.0) for j, w in o["pre"].items()] for o in ops]
        succ = [[] for _ in ops]
        for k in range(n):
            for j, w in pre[k]:
                succ[j].append((k, w))
        cost = [o["cost"] for o in ops]
        hold = [{"arr": 0.0, "dma": 0.1, "rem": ISSUE}.get(o["kind"], o["cost"]) for o in ops]
        hold[[o["kind"] for o in ops].index("rem")] = DUE[10]
        key = [o["lead"] for o in ops]
        for k in range(n - 1, -1, -1):
            key[k] = min([key[k]] + [key[j] for j, w in succ[k]])
        on = [o["eng"] for o in ops]

        def gap(i, w):
            return hold[i] if w is None else cost[i] + w if w or ops[i]["kind"] != "dma" else hold[i]

        def plan(key, back):
            before, after = (succ, pre) if back else (pre, succ)
            left = [len(x) for x in before]
            ready = {e: {} for e in "vstgyr"}
            for k in range(n):
                for e in on[k][0] if left[k] == 0 else "":
                    ready[e][k] = cost[k] - hold[k] if back else 0.0
            free = {e: 0.0 for e in ready}
            at, seq = [0.0] * n, []
            while len(seq) < n:
                t0, e = min((max(free[e], min(r.values())), e) for e, r in ready.items() if r)
                mine = sorted(ready[e], key=lambda k: (key[k], -k if back else k))
                now = next(k for k in mine if ready[e][k] <= t0)
                k = next(k for k in mine if ready[e][k] <= t0 + min(CAP, SLACK["vst".find(e)] * hold[now]))
                at[k] = max(t0, ready[e].pop(k))
                free[e] = at[k] + hold[k]
                seq.append((k, e))
                for j, _ in after[k]:
                    left[j] -= 1
                    for x in on[j][0] if left[j] == 0 else "":
                        ready[x][j] = (max(at[i] + hold[i] + gap(j, w) - hold[j] for i, w in succ[j]) if back
                                       else max(at[i] + gap(i, w) for i, w in pre[j]))
            return max(at[k] + cost[k] for k in range(n)), seq, at

        if BY:
            for k, _ in reversed(plan(key, False)[1]):
                key[k] = min([marks.get(k, 1e4)] + [key[j] - gap(k, w) for j, w in succ[k]])
        best = now = plan(key, False)
        for _ in range(PASSES):
            at = plan([-now[2][k] - hold[k] for k in range(n)], True)[2]
            now = plan([-at[k] - hold[k] for k in range(n)], False)
            best = min(best, now)
        for i in range(TRIES):
            at = plan([-best[2][k] - hold[k] + SHAKE * math.sin(7.0 * i + 0.7 * k * (i + 1)) for k in range(n)], True)[2]
            best = min(best, plan([-at[k] - hold[k] for k in range(n)], False))
        seq = best[1]

        def clock(seq):
            at, why, last = [0.0] * n, [-1] * n, {}
            for k, e in seq:
                t0, j0 = 0.0, -1
                if e in last:
                    j0 = last[e]
                    t0 = at[j0] + hold[j0]
                for j, d in lag[k]:
                    if at[j] + d > t0:
                        t0, j0 = at[j] + d, j
                at[k], why[k], last[e] = t0, j0, k
            k = max(range(n), key=lambda k: at[k] + cost[k])
            return at[k] + cost[k] + MEAN * sum(at) / n, k, why, at

        lag = [[(j, gap(j, w)) for j, w in pre[k]] for k in range(n)]
        if True:
            now = clock(seq)
            rnd = 1
            goal = [o["step"] for o in ops].index((0, "ZM1"))
            for i in range(MOVES):
                where = {k: p for p, (k, e) in enumerate(seq)}
                held, k = [], goal if rnd >> 18 & 1 else rnd % goal
                while now[2][k] >= 0:
                    j = now[2][k]
                    if j not in ops[k]["pre"]:
                        held.append((j, k))
                    k = j
                rnd = rnd * 48271 % 2147483647
                if not held:
                    continue
                j, k = held[rnd % len(held)]
                a, b = where[j], where[k]
                between = seq[a:b + 1]
                if rnd >> 20 & 1 and len(on[j] + on[k]) > 2:
                    x = j if len(on[j]) > 1 and (len(on[k]) == 1 or rnd >> 12 & 1) else k
                    new = [(y, "vs".replace(e, "") if y == x else e) for y, e in between]
                elif rnd >> 12 & 1:
                    mv = {k}
                    for x, _ in reversed(between):
                        if x not in mv and any(y in mv for y, _ in succ[x]):
                            mv.add(x)
                    if j in mv:
                        continue
                    new = [x for x in between if x[0] in mv] + [x for x in between if x[0] not in mv]
                else:
                    mv = {j}
                    for x, _ in between:
                        if x not in mv and any(y in mv for y, _ in pre[x]):
                            mv.add(x)
                    if k in mv:
                        continue
                    new = [x for x in between if x[0] not in mv] + [x for x in between if x[0] in mv]
                seq[a:b + 1] = new
                c = clock(seq)
                if c[0] <= now[0] + HEAT * (1 - i / MOVES) * (rnd >> 14 & 7) / 7:
                    now = c
                    seq.sort(key=lambda x: c[3][x[0]])
                else:
                    seq[a:b + 1] = between
            ORDER[n] = seq
            PLANNED.append((best[0], now[0] - MEAN * sum(now[3]) / n))
        seq = ORDER[n]
        tok = {}
        for k, e in seq:
            o = ops[k]
            if o["kind"] == "arr":
                tok[k] = (o["sem"], o["inc"])
                clk[tok[k]] = {o["sem"]: o["inc"]}
                continue
            need(e, set(tok[j] for j, w in o["pre"].items() if w))
            if o["kind"] == "rem":
                o["call"]()
                continue
            sem = o["sem"] or "c" + e
            cnt[sem] = cnt.get(sem, 0) + o["inc"]
            tok[k] = (sem, cnt[sem])
            o["call"](e).then_inc(T.sem[sem], o["inc"])
            c = dict(known[e])
            c[sem] = cnt[sem]
            clk[tok[k]] = c

    sent = [0]
    sends = {}
    dmas = []

    def arrive(x, key, val):
        op("r", [x], [], None, 0.0, "arr", key, val, [sends[key]])

    def B(n, lo=0, hi=None, step=1):
        hi = SCRATCH[n][1][1] if hi is None else hi
        return (T[n][:, lo:hi] if step == 1 else T[n][:, lo:hi:step], n, lo, hi)

    V, S_, P_ = g.vector, g.scalar, g.tensor

    def a_(x):
        return x[0] if isinstance(x, tuple) else x

    def cols(*xs):
        return [x for x in xs if isinstance(x, tuple)]

    def el(o, *xs):
        n = o[0].shape[1]
        if xs and all(SCRATCH[x[1]][2] in TWO for x in (o,) + xs):
            n = n // 2
        return max(64, n) * CYC

    def copy(o, i):
        return op("v", [o], [i], lambda e: V.tensor_copy(o[0], i[0]), el(o, i))

    def tt(o, x, y, f):
        c = el(o) if psum(x[1]) or psum(y[1]) or o[0].shape[1] <= 32 else 2 * el(o)
        return op("v", [o], [x, y], lambda e: V.tensor_tensor(o[0], x[0], y[0], f), c)

    def ts(o, x, s1, f1, s2=None, f2=None):
        if f2 is None:
            return op("v", [o], [x] + cols(s1), lambda e: V.tensor_scalar(o[0], x[0], a_(s1), None, f1), el(o, x))
        return op("v", [o], [x] + cols(s1, s2), lambda e: V.tensor_scalar(o[0], x[0], a_(s1), a_(s2), f1, f2), el(o, x))

    def fill(o, c):
        return op("v", [o], [], lambda e: V.memset(o[0], c), el(o, o))

    def scan(o, d0, d1, f0, f1):
        return op("v", [o], [d0, d1], lambda e: V.tensor_tensor_scan(o[0], d0[0], d1[0], 0.0, f0, f1), el(o, d0, d1))

    def act(o, i, func=AF.Copy, scale=1.0, bias=0.0):
        if isinstance(bias, float) and bias == 0.0:
            return op("s", [o], [i] + cols(scale), lambda e: S_.activation(o[0], i[0], func, scale=a_(scale)), el(o))
        return op("s", [o], [i] + cols(bias, scale), lambda e: S_.activation(o[0], i[0], func, bias=a_(bias), scale=a_(scale)), el(o))

    def mov(name, o, i, scale=1.0, bias=0.0):
        def call(e):
            if e == "v":
                return V.tensor_scalar(o[0], i[0], a_(scale), a_(bias), OP.mult, OP.add)
            if isinstance(bias, float) and bias == 0.0:
                return S_.activation(o[0], i[0], AF.Copy, scale=a_(scale))
            return S_.activation(o[0], i[0], AF.Identity, bias=a_(bias), scale=a_(scale))
        return op(eng(name), [o], [i] + cols(scale, bias), call, el(o) + VFIX * (eng(name) != "v"))

    def put(o, c):
        return act(o, B("FF", 0, o[0].shape[1]), AF.Identity if c else AF.Copy, 0.0, c)

    def twin(o, i):
        return op("g", [o], [i], lambda e: g.affine_select(o[0], i[0], [[0, 128]], OP.is_ge, 0.0, 0, 0), 0.17 + 2 * el(o))

    def eng(name):
        return ("vs" if name in ON else "sv")[:1 + FLEX]

    def mm(o, l, r, start=True, stop=True):
        n = max(min(64, l[0].shape[1]), r[0].shape[1])
        return op("t", [o], [l, r], lambda e: P_.matmul(o[0], l[0], r[0], start, stop), n * PEC * (4 if SCRATCH[l[1]][2] == F else 1))

    def ind(w, off):
        return w[0].indirect(off[0])

    def gat(eng, o, w, off):
        return op(eng, [o], [w, off], lambda e: V.tensor_copy(o[0], ind(w, off)) if e == "v"
                  else S_.activation(o[0], ind(w, off), AF.Copy), 0.06 + 16 * off[0].shape[1] * CYC * GAT)

    def sca(w, off, i):
        return op("v", [w], [i, off], lambda e: V.tensor_copy(ind(w, off), i[0]), 0.06 + 128 * CYC * SCA)

    def scamax(w, off, x, y):
        return op("v", [w], [x, y, off], lambda e: V.tensor_tensor(ind(w, off), x[0], y[0], OP.max), 0.06 + 128 * CYC * SCA)

    def iota(o, pattern, base, cm):
        c = 0.13 + 2 * el(o)
        if SCRATCH[o[1]][2] == I:
            return op("g", [o], [], lambda e: g.iota(o[0], pattern, base, cm), c)
        return op("g", [o], [], lambda e: g.iota(o[0], pattern, base, cm, allow_small_or_imprecise_dtypes=True), c)

    def dma(q, outs, ins, out, in_, cost=2.5, after=()):
        dmas.append("d%d" % len(dmas))
        return op(q, outs, ins, lambda e: Q[e].dma_start(out, in_), cost, "dma", dmas[-1], 16, after)

    def peer(s):
        return (rank + s) % N

    def send(s, dst, src, sem, cost):
        m = topo.mask(core, T.cores[peer(s)])
        rid, pid = topo.addr(T.cores[peer(s)])[:2]
        sends[sem] = op("g", [], [src], lambda: g.remote_dma(dst[0], src[0], T.sem[sem], T.sem["snd"], pid, rid, m), cost, "rem")
        sent[0] += len(topo.engines(core, T.cores[peer(s)]))

    def share(a, b, s):
        en = topo.engines(a, b)
        k = len(en) // 4
        return en[(s - 1) * k:s * k] if s < N - 1 else en[2 * k:]

    def send3(dst, src, sem, cost):
        tr = []
        for s in range(1, N):
            en = share(core, T.cores[peer(s)], s)
            rid, pid = topo.addr(T.cores[peer(s)])[:2]
            tr.append(RemoteDMATransfer(dst_ids=[DstId(rid=rid, pnc=pid)], dma_engine_mask=sum(1 << e for e in en),
                                        remote_sem=T.sem[sem + str(s)], srcs=[src(s)[0]], dsts=[dst(s)[0]]))
            sent[0] += len(en)
        k = op("g", [], [src(s) for s in range(1, N)], lambda: g.remote_dma_fused(tr, local_sem=T.sem["snd"]), cost, "rem")
        for s in range(1, N):
            sends[sem + str(s)] = k

    def share_out(src, land, sem, cost):
        w = src[3] - src[2]
        m = topo.mask(core, T.cores[peer(1)])
        to = [DstId(rid=topo.addr(T.cores[peer(s)])[0], pnc=topo.addr(T.cores[peer(s)])[1]) for s in range(1, N)]
        mine = B(land, w * rank, w * rank + w)
        tr = [RemoteDMATransfer(dst_ids=to, dma_engine_mask=m, remote_sem=T.sem[sem], srcs=[src[0]], dsts=[mine[0]] * 3)]
        k = len(topo.engines(core, T.cores[peer(1)]))
        sent[0] += k
        sends[sem] = op("g", [], [src], lambda: g.remote_dma_fused(tr, local_sem=T.sem["snd"]), cost, "rem")
        copy(mine, src)
        op("r", [B(land, w * peer(s), w * peer(s) + w) for s in range(1, N)], [], None, 0.0, "arr", sem, 3 * k, [sends[sem]])

    def arrive3(x, sem, s):
        arrive(x, sem + str(s), len(share(T.cores[peer(-s)], core, s)))

    def col(k):
        return B("COL", k, k + 1)

    def isx(k):
        return B("MSK", k, k + 1)

    def third(n, m):
        return B(n, 128 * m, 128 * m + 128)

    def eight(n, m):
        return B(n, 8 * m, 8 * m + 8)

    def seg(n, m):
        return B(n, NV_ * m, NV_ * (m + 1))

    def ahead(n, s):
        return B(n, 128 - 32 * s, 256 - 32 * s)

    def rows(r):
        return slice(32 * r, 32 * r + 32)

    def turn(t, name):
        lead[0] = 100.0 * t + TURNS.index(name)

    def slot(n, r):
        return (T[n][r], n, r, r + 1)

    HALF = ((slice(16, 2064), slice(2048, 4096)), (slice(2064, TW), slice(0, 2048)))

    def tab(s, k, i):
        lo = TW * i + 16 + 1024 * s + 512 * k
        return (None, "TAB", lo, lo + 512)

    dma("s", [(None, "DP", 0, N)], [], T.DP[:], T.pots[:])
    dma("s", [slot("LP", rank)], [], T.LP[rank], T.pots[2 * rank:2 * rank + 2, :])
    order, posts = [], []

    def load(outs, ins, out, in_, cost):
        order.append(dma("y", outs, ins, out, in_, cost, order[-1:]))

    def post(x, cost):
        if x == "p":
            send3(lambda s: slot("LP", rank), lambda s: slot("DP", peer(s)), "p", cost)
        else:
            s, k = int(x[0]), int(x[1])
            src = slot("DT", 2 * peer(s) + k)
            if x in HANDED:
                to = hands(core, topo)[HANDED.index(x) % HANDS]
                en = [e for e in topo.engines(core, to) if e not in topo.engines(core, T.cores[peer(s)])]
                rid, pid = topo.addr(to)[:2]
                sends["t" + x] = op("g", [], [src], lambda: g.remote_dma(src[0], src[0], T.sem["h" + x], T.sem["snd"], pid, rid, sum(1 << e for e in en)),
                                    cost, "rem")
                sent[0] += len(en)
            else:
                send(s, slot("LT", 2 * rank + k), src, "t" + x, cost)
        for j in posts[-1:]:
            ops[-1]["pre"][j] = None
        posts.append(len(ops) - 1)

    def half(x, k):
        return (None, x[1], x[2] + k * (x[3] - x[2]) / 2, x[2] + (k + 1) * (x[3] - x[2]) / 2)

    def land(x, i, after=()):
        s, k = int(x[0]), int(x[1])
        r, w = peer(-s), HALF[k][0]
        load([tab(s, k, i)], [slot("LT", 2 * r + k)] + list(after), T.TAB[rows((r - i) % N), TW * i + w.start:TW * i + w.stop], T.LT[2 * r + k], DUE[0])

    fill(B("POTH"), 0)
    for x, due in LOADS:
        if x == "R":
            load([B("RAW0")], [], T.RAW0[:], T.bun[:], due)
            load([B("POTH")], [], T.POTH[0:128:16, :], T.pots[:], due)
        elif x == "T":
            for w, a in HALF:
                load([B("TAB", w.start, w.stop)], [], T.TAB[:, w], T.sight[:, a], due)
        else:
            s, k = int(x[0]), int(x[1])
            load([slot("DT", 2 * peer(s) + k)], [], T.DT[2 * peer(s) + k], T.sight[rows(peer(s)), HALF[k][1]], due)
    load([(None, "TAB", TW + 16, TW + 1040)], [B("TAB", 16, TW)], T.TAB[rows(peer(-1)), TW + 16:2 * TW], T.TAB[rows(rank), 16:TW], DUE[0])
    for x, due in POSTS[:AFTER]:
        post(x, due)
    fill(B("POTI"), 0)
    for s in range(N):
        fill(B("TAB", TW * s, TW * s + 16), 0.0)

    def lands():
        posts.append(sends["u1"])
        for x, due in POSTS[AFTER:]:
            post(x, due)
        for x in LANDS:
            if x == "p":
                for s in range(1, N):
                    arrive3(slot("LP", peer(-s)), "p", s)
                load([B("POTI")], [(None, "LP", 0, N)], T.POTI[0:128:16, :], T.LP[:], DUE[0])
                continue
            arrive(slot("LT", 2 * peer(-int(x[0])) + int(x[1])), "t" + x, len(topo.engines(T.cores[peer(-int(x[0]))], core)))
            land(x, 1)

    def windows():
        for s in range(1, N):
            for k in range(2):
                land("%d%d" % (s, k), 0, [B("LZ") if 2 * s + k >= SOON else B("TAB", TW + 16, 2 * TW)])
        for s in (2, 3):
            lo, k = TW * s + 16, 32 * s
            x, y = B("TAB", lo, lo + 4096), [B("TAB", 16, TW), B("LZ")] + [B("TAB", 2 * TW + 16, 3 * TW)] * (s - 2)
            load([half(x, 0)], y, T.TAB[0:128 - k, lo:lo + 4096], T.TAB[k:128, 16:TW], DUE[6])
            load([half(x, 1)], y, T.TAB[128 - k:128, lo:lo + 4096], T.TAB[0:k, 16:TW], DUE[6])

    lead[0] = 1000.0
    iota(col(0), [[1, 1]], 0, 1)
    lead[0] = -2000.0
    fill(col(15), 63 * math.log(2.0) + math.log(2.5))
    act(col(16), col(0), AF.Exp, -math.log(2.0), col(15))
    lead[0] = 1000.0
    iota(B("II", 0, 1), [[1, 1]], 0, 1)
    iota(B("AS"), [[-8, 4], [-32, 128]], -5, 0)
    iota(B("FF"), [[1, 132]], 0, 0)
    iota(B("FX"), [[0, 8], [1, 16]], 0, 0)
    iota(B("FG"), [[1, 8], [0, 16]], 0, 0)
    iota(B("SLOT"), [[0, 8], [1, SEG]], 0, 0)
    iota(B("T19", 0, NV_), [[1, 8], [0, SEG]], 0, 0)
    iota(B("EXI", 0, 8), [[1, 4], [4, 2]], 0, 0)
    iota(B("EXI", 8, 24), [[8, 2], [24, 4], [1, 2]], 2 * rank + 8, 0)
    fill(B("SU", 128, 4 * UW), 0.0)
    copy(B("EXV", 0, 24), B("EXI", 0, 24))
    ts(B("II", 1, 2), B("II", 0, 1), 15, OP.bitwise_and)
    ts(B("II", 2, 3), B("II", 0, 1), 4, OP.logical_shift_right)
    copy(B("COL", 1, 3), B("II", 1, 3))
    fill(B("RST"), 1.0)
    fill(B("RST", 0, 16 * CH, 16), 0.0)
    BO = B("BO", 0, 128)
    ts(BO, B("FG"), col(2), OP.is_equal)
    act(B("BO", 128, 256), BO)
    ts(B("MSK"), B("FX", 0, 128), col(1), OP.is_equal)
    act(col(12), col(1), AF.Identity, -1.0, 15.0)
    act(col(3), col(2), AF.Identity, 16.0, col(12))
    ts(third("RG", 0), B("FF", 0, 128), col(3), OP.is_equal)
    mov("RG", third("RG", 1), third("RG", 0))
    IDF, BLK = third("PI", 0), B("GF")
    ts(IDF, B("FF", 0, 128), col(0), OP.is_equal)
    act(third("PI", 1), IDF)
    act(B("IDN"), IDF)
    act(B("IDU"), IDF, AF.Copy, 1.0 / UNIT)
    ts(BLK, B("FF", 0, 8), col(2), OP.is_equal)
    act(B("GS"), BLK)
    act(eight("GB", 0), BLK, AF.Copy, 4.0)
    act(eight("GB", 1), BLK, AF.Copy, UNIT)
    act(B("GU"), BLK, AF.Copy, 1.0 / UNIT)
    ts(B("EXL"), B("FF", 0, 8), 1.0 if ZF else float(SEG), OP.mult, 0.0 if ZF else SEG - 1.0, OP.add)
    ts(col(4), col(1), 0.0, OP.is_gt)
    ts(col(8), col(1), 13.0, OP.is_ge)
    act(col(9), col(1), AF.Identity, -4.0 * 2 ** 19, 32.5 * 2 ** 19)
    act(B("BIAS"), B("MSK"), AF.Identity, 512.0, -512.0)
    mov("PG", B("PG"), B("PI"))
    ts(col(17), col(1), 3.0, OP.is_lt)
    ts(B("CAI"), B("FF", 0, 8), col(1), OP.add, 1.0, OP.add)
    ts(B("CAI"), B("CAI"), 3, OP.bitwise_and)
    ts(B("CA"), B("CAI"), 8.0, OP.mult, 5.0, OP.add)
    ts(B("CA"), B("CA"), col(17), OP.mult, isx(8), OP.add)
    for m in range(3):
        ts(col(20 + m), isx(15 - m), -32.0, OP.mult, isx(m), OP.subtract)
        act(third("MA", m), BO, AF.Copy, col(20 + m))
        act(third("SEL", m), BO, AF.Copy, isx(15 - m))
    act(B("IXP"), IDF, AF.Copy, col(4))
    act(col(7), col(0), AF.Identity, 4096.0 * UNIT, -1.0)
    act(B("NONE"), B("FF", 0, 8), AF.Identity, 0.0, col(7))
    act(col(14), col(1), AF.Identity, -math.log(2.0), 63 * math.log(2.0))
    iota(B("W8", 0, 64), [[16, 8], [0, 8]], 0, 0)
    iota(B("W8", 64, 128), [[0, 8], [1, 8]], 0, 0)
    act(B("W8", 0, 64), B("W8", 0, 64), AF.Exp, -math.log(2.0), col(14))
    ts(B("W8", 64, 128), B("W8", 64, 128), col(2), OP.is_equal)
    tt(B("WG"), B("W8", 0, 64), B("W8", 64, 128), OP.mult)
    t19 = B("T19")
    ts(t19, t19, col(2), OP.is_equal)
    for k in (0, SEG - 2, SEG - 1):
        put(B("T19", k, NV_, SEG), 0.0)
    act(col(11), isx(0), AF.Copy, -4.0)
    act(B("NEGV"), t19, AF.Copy, col(11))
    fill(B("CD"), -2.0)
    put(B("CD", 0, 6 * NV_, SEG), 2.0)
    put(B("CD", SEG - 1, 6 * NV_, SEG), 0.0)
    act(B("COL", 23, 26), B("MSK", 13, 16), AF.Copy, 4096.0 * UNIT)
    for m in range(3):
        act(seg("CD", 2 * m + 1), B("SLOT"), AF.Identity, 0.125, (-33.0 - m) / 32)
        put(B("CD", NV_ * (2 * m + 1) + SEG - 2, NV_ * (2 * m + 2), SEG), -1.0 if "FS" in ON else 0.0)
        if m == 2 and ZF:
            put(B("CD", 4 * NV_ + SEG - 1, 5 * NV_, SEG), -2.0)
        if m == 1:
            put(B("CD", 2 * NV_ + SEG - 1, 3 * NV_, SEG), -2.0)
        act(seg("QX", m), t19, AF.Copy, col(25 - m))
    act(col(18), isx(8), AF.Copy, -8192.0)
    act(seg("QX", 3), t19, AF.Copy, col(18))
    act(B("PSELA"), ahead("BO", 1), AF.Copy, 0.5)
    ts(col(6), col(1), 2.0, OP.is_lt)
    put(B("PSEL"), 0.0)
    act(B("PSEL", 0, 128, 16), B("PSELA", 0, 128, 16))
    act(B("POLD"), B("PSEL"), AF.Copy, col(6))
    act(col(13), isx(0), AF.Identity, 16.0, col(0))
    ts(B("TMP"), B("FF", 1, 129), col(13), OP.is_equal)
    tt(B("DIF"), B("TMP"), IDF, OP.subtract)
    put(B("DIF", 0, 128, 16), 0.0)
    for k, o in enumerate(ops):
        if o["eng"] == "g" and o["kind"] == "c" and o["step"][1][:2] in ("II", "CO", "FF", "FG", "FX", "AS"):
            ops[posts[0]]["pre"][k] = None
    MID = (EMPTY - 2 * LOW - 1) / 2

    def closing(t):
        if t == 0:
            ts(B("II", 3, 4), B("II", 2, 3), 1, OP.bitwise_and)
            ts(B("II", 4, 5), B("II", 2, 3), 1, OP.logical_shift_right)
            copy(B("COL", 28, 30), B("II", 3, 5))
            act(col(27), col(2), AF.Identity, 4.0, 3.0)
            act(col(26), col(12), AF.Identity, 4.0, 3.0)
            act(col(26), col(28), AF.Identity, 64.0, col(26))
            iota(B("U19", 0, 64), [[0, 2], [1, 32]], 0, 0)
            put(col(10), -MID)
        if t == 1:
            fill(B("HV"), 0.0)
            ts(B("HV", 0, 64), B("U19", 0, 64), col(27), OP.is_equal)
            mov("HOME", B("HP"), B("HV"), isx(0))
            fill(B("WV", 0, 512, 4), -2047.0)
            fill(B("WV", 3, 512, 4), 0.0)
        if t == 2:
            ts(B("ZT", 8, 12), B("FF", 0, 4), col(29), OP.is_equal)
            ts(B("U19"), B("FF", 0, 132), col(26), OP.is_equal)
            for r in range(N):
                mov("HOME", B("HOME", 132 * r, 132 * r + 132), B("U19"), B("ZT", 8 + r, 9 + r))

    FLAG = (1 << 26) | 4095

    def part(x, lo, hi):
        return B(x[1], x[2] + lo, x[2] + hi)

    def index(tag, s, a, c, halves=1):
        n = 128 // halves
        for lo in range(0, 128, n):
            o = 128 * "012S".index(tag) + lo
            xi, xj = B("XI", o, o + n), B("XJ", o, o + n)
            if s:
                tt(xi, s if halves == 1 else part(s, lo, lo + n), part(a, lo, lo + n), OP.mult)
            ts(xj, xi, 721635.0 - 4096.0 * (8 * c + 5), OP.add)
            ts(xi, xj, 5, OP.arith_shift_right, FLAG, OP.bitwise_and)
            ts(B("OFF", o, o + n), xi, -1.0, OP.mult, TW - 1.0, OP.add)
            if seen["cycle"] < 0:
                mark("OFF%d" % seen["vOFF"])

    def place(tag, k, lo=0, hi=128):
        m = 2048 * "012S".index(tag)
        return B("X", m + 16 * lo + k, m + 16 * hi, 16)

    def look(t, tag, pieces, tab):
        a = 128 * "012S".index(tag)
        for eng, n in pieces:
            x = B("X", 16 * a, 16 * (a + n))
            turn(t, ("help" if eng == "v" else "gather") + tag)
            gat(("vs" if eng == "v" else "sv")[:1 + FLEX], x, tab, B("OFF", a, a + n))
            turn(t, "scan" + tag)
            scan(x, B("RST", 0, 16 * n), x, OP.mult, OP.max)
            a += n

    def window(s):
        return B("TAB", TW * s, TW * s + TW)

    turn(-6, "names")
    ts(B("RAW0"), B("RAW0"), EMPTY, OP.bitwise_and)
    ts(B("BF"), B("RAW0"), -LOW, OP.add)

    def some(x, r):
        return (T[x[1]][rows(r), x[2]:x[3]],) + x[1:]

    turn(-3, "end")
    mov("BG", B("BG"), B("BF"), 0.125, (LOW - 2047.0) / 8)
    for s in (1, 2, 3, 0):
        o = third(("b7", "b0", "b1", "b2")[s], 0)
        for q in range(4):
            mm(o, some(ahead("PG", (q - peer(s)) % N), peer(s)), some(third("BG", q), peer(s)), q == 0, q == 3)
        mov("SU", B("SU" if s else "LB", UW * peer(s), UW * peer(s) + 128), o)
    for c in range(3):
        tag = "S012"[c]
        bank = "b%d" % (3 + c)
        when = (-5, -3, -3, -4)[c]
        turn(when, "index" + tag if c else "names")
        index(tag, B("BF", c, 512, 4), third("AS", c), c)
        look(when, tag, FIRST[c], window(0))
        mm(third(bank, 1), BO, place(tag, 15))
        act(third("VH", c), third(bank, 1))
        mm(B(bank, 0, 8), place(tag, 15), B("GS"))
        if c:
            copy(eight("ZH", c), B(bank, 0, 8))
        else:
            for h in range(2):
                ts(B("SU", 128 + h, 4 * UW, UW), B(bank, h, 8, 2), -2047.0, OP.add)
            send3(lambda s: B("LB", UW * rank, UW * rank + UW), lambda s: B("SU", UW * peer(s), UW * peer(s) + UW), "u", DUE[11])
            mark("u")
            copy(B("LB", UW * rank + 128, UW * rank + UW), B("SU", UW * rank + 128, UW * rank + UW))
            lands()

    def names(t, si, old, v, pool=None):
        turn(t, "names")
        if pool:
            ts(pool, pool, EMPTY, OP.bitwise_and)
            ts(B("PL0"), pool, -LOW, OP.add, isx(0), OP.mult)
            mm(third("b1", 3), IDF, B("PL0"), True, False)
        mm(third("b1", 3), B("IXP"), old, False, True)
        mov("SI", si, third("b1", 3))
        mov("KS", third("b0", 3), v, 1.0, LOW + 13.0 * max(t, 0))
        tt(B("KT"), third("b0", 3), old, OP.add)
        ts(B("KI"), B("KT"), 127, OP.bitwise_and)
        ts(B("KB"), B("KI"), col(8), OP.mult, B("CA", max(t, 0), max(t, 0) + 1), OP.add)

    def spread(t, ms):
        kb = B("KB")
        lo, hi = ms[0], ms[-1] + 1
        for m in ms:
            turn(t, "index%d" % m)
            mm(third("b0", m), third("MA", m), kb)
        turn(t, "lists")
        x = B("b3", 128 * lo, 128 * hi)
        for m in ms:
            mm(third("b3", m), B("IDN"), B("BIAS"), m == lo, False)
        for m in ms:
            mm(third("b3", m), kb, third("SEL", m), False, m == ms[-1])
        if "KM" in ON:
            ts(B("KM", 128 * lo, 128 * hi), x, 0.0, OP.max)
        else:
            act(B("KM", 128 * lo, 128 * hi), x, AF.Relu)
        for m in ms:
            mm(B("b3", 384 + m * 8, 392 + m * 8), third("KM", m), B("GS"))
        mov("LF", B("LF", 8 * lo, 8 * hi), B("b3", 384 + 8 * lo, 384 + 8 * hi))
        copy(B("VL", 8 * lo, 8 * hi), B("b3", 384 + 8 * lo, 384 + 8 * hi))
        turn(t, "rows")
        for m in ms:
            mm(third("b2", m), third("SEL", m), kb)
        mov("KRB", B("KRB", 128 * lo, 128 * hi), B("b2", 128 * lo, 128 * hi))

    def firsts(t, ms):
        for m in ms:
            turn(t, "first%d" % m)
            for c in range(8):
                x = third("EB", 8 * m + c)
                ts(x, third("KRB", m), B("LF", m * 8 + c, m * 8 + c + 1), OP.is_equal)
                mm(eight("b7", m), x, eight("WG", c), c == 0, c == 7)
        turn(t, "firsts")
        o, x = B("FS", 8 * ms[0], 8 * ms[-1] + 8), B("b7", 8 * ms[0], 8 * ms[-1] + 8)
        if "FS" in ON:
            ts(o, x, col(16), OP.is_lt, 2.0, OP.mult)
        else:
            act(o, x, AF.Sign, -1.0, col(16))
        mark("F%d" % t if t <= 0 else "F", 15.5 * max(t, 0))

    def verdict(t, m, v, best):
        bank = "b%d" % (4 + m)
        turn(t, "value%d" % m)
        o, ls = third("VJ", m), eight("VL", m)
        op(eng("VJ%d" % m), [o], [v, ls], lambda e: V.tensor_scalar(o[0], ind(v, ls), -2048.0, None, OP.add) if e == "v"
           else S_.activation(o[0], ind(v, ls), AF.Identity, bias=-2048.0), 0.06 + 128 * CYC * GAT)
        d, c = seg(bank, 0), seg(bank, 1)
        mm(B(bank, 0, 2 * NV_), B("IDN"), B("CD", 2 * NV_ * m, 2 * NV_ * (m + 1)), True, False)
        mm(c, B("KB"), seg("QX", m), False, False)
        mm(d, B("KB"), seg("QX", 3), False, False)
        mm(d, third("VJ", m), B("NEGV"), False, False)
        mark("V%d" % t if t <= 0 else "V", 15.5 * max(t, 0))
        turn(t, "verdict%d" % m)

        for lo, hi in TILES if m == 2 else TILE1 if m else ((0, 128),):
            for k, x in enumerate(best if hi == 128 else ()):
                mm(B(bank, SEG * k + SEG - 1, NV_, SEG * len(best)), IDF, x, False, False)
            for k in range(16):
                mm((T[bank][lo:hi, 16 - k:2 * NV_:SEG], bank, 0, 2 * NV_), place(str(m), k, lo, hi), B("GB"), False, False)
        mm(B(bank, NV_ + SEG - 2, 2 * NV_, SEG), B("IDN"), eight("FS", m), False, True)
        turn(t, "code%d" % m)
        mov("CODE%d" % m, seg("CODE", m), c)
        scan(seg("ZS", m), d, seg("CODE", m), OP.max, OP.min)
        return B("ZS", NV_ * m + SEG - 1, NV_ * (m + 1), SEG)

    turn(-5, "names")
    mm(third("b1", 0), ahead("RG", 0), B("BG", 0, 512, 4))
    mov("WIN", B("OH"), third("b1", 0), 8.0, 2047.0 - LOW)
    names(-2, B("SH"), B("OH"), third("VH", 0), B("POTH"))
    spread(-2, (0, 1))
    early = []
    for m in range(2):
        turn(-2, "index%d" % m)
        index(str(m), B("SH"), third("b0", m), 1 + m, HALVES[m])
        early.append(len(ops))
        look(-2, str(m), EARLY[m], window(0))
    firsts(-2, (0, 1))
    tt(eight("ZH", 0), verdict(-2, 0, third("VH", 1), [B("NONE")]), verdict(-2, 1, third("VH", 2), []), OP.max)
    mark("Z")
    share_out(B("ZH"), "LZ", "VB1", DUE[12])
    turn(-1, "names")
    for s in range(1, N):
        arrive3(B("LB", UW * peer(-s), UW * peer(-s) + UW), "u", s)
    windows()
    for k in range(2):
        ts(B("LVA", 4 * k, 4 * k + 4), B("LB", 128 + k, 4 * UW, UW), 2047.0, OP.add)
    for q in range(4):
        for s in range(N):
            k = mm(third("b2", q), some(ahead("RG", (s - q) % N), q), some(B("LB", UW * s, UW * s + 128), q), s == 0, s == N - 1)
            if s == 0 and q:
                ops[k]["pre"][k - 1] = True

    def values(c, via):
        gat("s", third("VK", c), B("LZ") if c else B("LVA", 0, 8), eight("EXV", c))
        mm(via, third("VK", c), IDF)
        act(third("VR", 8 - c), via)

    for c in (0, 3, 1, 2):
        turn(0 if c else -1, "pool")
        mov("WIN", third("WIN", 8 - c) if c < 3 else B("NU"), B("b2", c, 512, 4), 8.0, 2047.0 - LOW)
        if c == 0:
            values(0, third("b3", 0))
        if c == 3:
            mm(third("b6", 3), ahead("PI", N - 1), B("NU"))
            mov("BACK", third("WIN", 5), third("b6", 3))
            turn(0, "indexS")
            index("S", third("WIN", 5), third("AS", 3), 3)
            look(0, "S", FIRST[3], window(1))

    for t in range(RO):
        s = 1 + t % 3
        last = t == RO - 1
        ms = (0, 1, 2) if t else (2,)
        si, old = third("WIN", 4 - t), third("WIN", 8 - t)
        names(t, si, old, third("VR", 8 - t), None if t else B("POTI"))
        if t == 0 and LAP >= 0:
            ops[early[1] + 2 * LAP]["pre"][len(ops) - 1] = False
        turn(t, "bundle2")
        k = twin(B("S1"), si)
        if t == 0:
            ops[k]["pre"][sends["VB1"]] = None
        spread(t, ms)
        turn(t, "pool")
        dif = third("b7", 1)
        mm(dif, B("DIF"), old)
        mm(third("b1", 3), B("POLD"), old, True, False)
        turn(t, "back")
        if t:
            mm(third("b2", 2), ahead("PI", 1 + (t - 1) % 3), third("VR", 6 - t))
            mov("BACKV", third("VR", 6 - t), third("b2", 2))
            mm(third("b2", 1), ahead("PI", 1 + (t - 1) % 3), third("WIN", 6 - t))
            mm(third("b2", 0), ahead("PI", N - s), B("NU"))
            mov("BACK", B("WIN", 128 * (5 - t), 128 * (7 - t)), B("b2", 0, 256))
        for m in ms:
            turn(t, "index%d" % m)
            index(str(m), si, third("b0", m), (t + 1 + m) & 3, HALVES[m])
            look(t, str(m), PIECES[m] if t else EARLY[m], window(s if m == 2 else 0))
        turn(t, "scanS")
        mm(third("b3", 0), ahead("BO", N - s) if t else BO, place("S", 15))
        mov("VR", third("VR", 5 - t), third("b3", 0))
        firsts(t, ms)
        turn(t, "pool")
        for c in () if t else (1, 2):
            values(c, third("b7", 1 + c))
        if t:
            tt(eight("ZT", 0), verdict(t, 0, third("VR", 7 - t), [B("NONE")]), verdict(t, 1, third("VR", 6 - t), []), OP.max)
        if ZF:
            for h in () if t else (0, 1):
                copy(B("ZT", h, 8, 2), B("LZ", 2 * rank + h, 96, 24))
            tt(B("ZF"), verdict(t, 2, third("VR", 5 - t), []), eight("ZT", 0), OP.max)
        else:
            verdict(t, 2, third("VR", 5 - t), [eight("ZT", 0)] if t else [B("LZ", 2 * rank + h, 96, 24) for h in range(2)])
        turn(t, "decide")
        zq, zx, zm = B("ZF") if ZF else seg("ZS", 2), B("ZX"), B("ZM")
        seen.clear()
        seen["cycle"] = t
        gat("s", zx, zq, B("EXL"))
        op("v", [zm], [zq, B("EXL"), B("MSK")], lambda e, zq=zq: V.tensor_tensor(T.ZM[:], zq[0].indirect(T.EXL[:]), T.MSK[:], OP.mult),
           0.06 + 128 * CYC * GAT)
        mark("ZM", 15.5 * t)
        behind.append(len(ops) - 1)
        closing(t)
        behind.pop()
        mm(B("b3", 440, 448), zm, B("GU"))
        z = third("b2", 3)
        mm(z, zx, B("IDU"))
        copy(eight("ZI", 0), B("b3", 440, 448))
        ts(eight("ZI", 1), eight("ZI", 0), 12, OP.arith_shift_right, 511, OP.bitwise_and)
        copy(B("LST"), eight("ZI", 1))
        nu, ls = B("NU"), B("LST")
        w, wv = (B(n, 128 * (4 - t), 128 * (8 - t)) for n in ("WIN", "VR"))
        copy(B("NI"), z)
        ts(B("KEEP1"), z, col(9), OP.subtract, EMPTY - LOW, OP.min)
        act(B("KEEP"), z, AF.Sign, -1.0, col(9))
        ts(B("NJ"), B("NI"), 4095, OP.bitwise_and)
        gat(eng("NU"), nu, w, ls)
        xs, a = third("XI", 3), third("AS", t & 3)
        op("v", [xs], [w, ls, a], lambda e, w=w, a=a: V.tensor_tensor(xs[0], ind(w, ls), a[0], OP.mult), 0.06 + 128 * CYC * GAT)
        sca(wv, ls, B("NJ"))
        turn(t, "change")
        scamax(w, ls, B("S1"), B("KEEP1"))
        turn(t, "pass")
        tt(B("PP"), dif, B("KEEP"), OP.mult)
        mm(third("b1", 3), B("PSEL"), B("PP"), False, last)
        turn(t + 1, "indexS")
        index("S", None, None, t & 3, HALVES[3])
        look(t + 1, "S", LAST if last else PIECES[3], window(0))
    turn(RO, "names")

    s3 = 1 + (RO - 1) % 3

    def piece(n, s, lo=0, hi=288):
        return B(n, 288 * s + lo, 288 * s + hi)

    def tile(s, lo, hi, step=1):
        return B(("b6", "b7", "b3", "b4")[s], lo, hi, step)

    def plain(o, x, k):
        act(third("WA", k), x, AF.Abs, 1.0, col(10))
        mov("WH%d" % k, o, third("WA", k), -1.0, MID + LOW - 2047.0)

    mm(third("b2", 0), ahead("PI", s3), third("WIN", 1))
    for c in range(1, 4):
        mov("WV", B("WV", c, 512, 4) if c < 3 else third("WV", 4), third("VR", 4 - c), 1.0, -2047.0)
    plain(third("WH", 4), third("b1", 3), 4)
    for c in range(4):
        plain(B("WH", c, 512, 4), (B("NU"), third("WIN", 3), third("WIN", 2), third("b2", 0))[c], c)
    for k in range(4):
        for q in range(4):
            x = (third("WV", q), B("WV", 512 + 32 * q, 544 + 32 * q), B("WH", 512 + 32 * q, 544 + 32 * q), place("S", 15, 32 * q, 32 * q + 32))[k]
            o = (B("b5", 32, 160), B("b5", 35, 160, 4), B("b5", 0, 32), B("b5", 32, 160, 4))[k]
            lo = 3 - q + (32 - 8 * s3) * (k == 1)
            mm(o, B("HV" if k == 3 else "HP", lo, lo + 128), x, k + q == 0, k + q == 6)
    for s in (1, 2, 3, 0):
        turn(RO, "names" if s else "end")
        for q in range(4):
            lo = 132 * peer(s) + 3 - q
            mm(tile(s, 0, 128), B("HOME", lo, lo + 128), third("WH", q), q == 0, q == 3)
        mov("OU%d" % s, piece("OU" if s else "OUT", s, 0, 128), tile(s, 0, 128), 1.0, 0.0 if s else 2047.0)
        mov("OV%d" % s, piece("OU" if s else "OUT", s, 128), B("b5", 0, 160), 1.0, 0.0 if s else 2047.0)
    turn(RO, "names")
    for to in CALLS:
        tr = []
        for i, s in enumerate(to):
            en = topo.engines(core, T.cores[peer(s)])
            en = en[i * len(en) // len(to):(i + 1) * len(en) // len(to)]
            rid, pid = topo.addr(T.cores[peer(s)])[:2]
            tr.append(RemoteDMATransfer(dst_ids=[DstId(rid=rid, pnc=pid)], dma_engine_mask=sum(1 << e for e in en),
                                        remote_sem=T.sem["w%d" % s], srcs=[piece("OU", s)[0]], dsts=[piece("LO", s)[0]]))
            sent[0] += len(en)
        k = op("g", [], [piece("OU", s) for s in to], lambda tr=tr: g.remote_dma_fused(tr, local_sem=T.sem["snd"]), 2.0 + len(to), "rem")
        for s in to:
            sends["w%d" % s] = k
            arrive(piece("LO", s), "w%d" % s, len(topo.engines(T.cores[peer(-s)], core)) // len(to))
    mark("end")
    turn(RO, "end")
    for s in range(N):
        r = peer(-s)
        if s:
            mov("OUT%d" % s, piece("OUT", s, 0, 128), piece("LO", s, 0, 128), 1.0, 2047.0)
            mov("OUV%d" % s, piece("OUT", s, 128), piece("LO", s, 128), 1.0, 2047.0)
        dma("y", [], [piece("OUT", s, 0, 128)], T.yb[rows(r), :], piece("OUT", s, 0, 128)[0])
        dma("s", [], [piece("OUT", s, 128)], T.yv[2 * r:2 * r + 2, :], T.OUT[8 * rank:8 * rank + 8, 288 * s + 160:288 * s + 288])
        dma("s", [], [piece("OUT", s, 128)], T.yp[2 * r:2 * r + 2, :], T.OUT[8 * rank:8 * rank + 8, 288 * s + 128:288 * s + 160])
    flush()
    for k in dmas:
        if known["y"].get(k, 0) < 16:
            g.sync.wait_ge(T.sem[k], 16)
    for k in ("cv", "cs", "ct", "cg"):
        if cnt.get(k):
            g.wait_ge(T.sem[k], cnt[k])
    g.wait_ge(T.sem["snd"], sent[0])
